import numpy as np
import ml_dtypes


def mxq(x, axis, fmt="e4m3"):
    dtype, down = {"e4m3": (ml_dtypes.float8_e4m3fn, 7), "e5m2": (ml_dtypes.float8_e5m2, 14)}[fmt]
    v = np.moveaxis(np.asarray(x, np.float32).astype(ml_dtypes.bfloat16).astype(np.float64), axis, -1)
    blocks = v.reshape(v.shape[:-1] + (-1, 32))
    amax = np.abs(blocks).max(-1, keepdims=True)
    byte = np.maximum(np.where(amax > 0, np.frexp(amax)[1] - 1 + 127, 0) - down, 1)
    scale = np.exp2(byte - 127.0)
    codes = (blocks / scale).astype(np.float32).astype(dtype).astype(np.float64)
    return np.moveaxis((codes * scale).reshape(v.shape), -1, axis)


WIDE = False


def mx_kscale(k):
    if not WIDE:
        return np.ones(k)
    levels = np.array([10, -10, 5, -5, 0])
    if k % 512:
        return np.exp2(np.random.permutation(np.resize(levels, k // 32))).repeat(32)
    a = np.empty((k // 512, 16))
    for p in range(k // 512):
        a[p, :8] = np.random.permutation(np.resize(levels, 8))
        for g in range(8):
            far = levels[np.abs(levels - a[p, g]) >= 10]
            a[p, g + 8] = far[np.random.randint(len(far))]
    return np.exp2(a.ravel()).repeat(32)


def f64(x):
    return np.asarray(x).astype(np.float64)


def striped(idx):
    return np.tile(idx.reshape(-1, 16).T, (8, 1)).astype(np.uint16)


def unstriped(offs):
    return offs[:16].T.reshape(-1).astype(np.int64)


def striped8(idx):
    return np.concatenate([x.reshape(-1, 16).T for x in idx]).astype(np.uint16)


def runs(offs, k):
    lists = np.stack([offs[16 * r : 16 * r + 16].T.reshape(-1) for r in range(8)]).astype(np.int64)
    return lists[np.arange(k) % 512 // 64]


def pack_weight(w):
    k, n = w.shape
    w = f64(np.asarray(w, np.float32).astype(ml_dtypes.bfloat16)).reshape(k // 32, 32, n)
    amax = np.abs(w).max(1)
    byte = np.clip(np.where(amax > 0, np.frexp(amax)[1] - 1 + 127 - 7, 1), 1, 254)
    scaled = (w * np.exp2(127.0 - byte)[:, None, :]).reshape(k, n).astype(np.float32)
    words = np.ascontiguousarray(scaled.reshape(k // 512, 128, 4, n).transpose(0, 1, 3, 2)).astype(ml_dtypes.float8_e4m3fn).view(np.uint8)
    return words, np.ascontiguousarray(byte.astype(np.uint8).reshape(k // 512, 16, n))


def unpack_weight(words, scales):
    g, p, n, _ = words.shape
    vals = np.ascontiguousarray(words).view(ml_dtypes.float8_e4m3fn).astype(np.float64) * np.repeat(np.exp2(scales.astype(np.float64) - 127.0), 8, axis=1)[..., None]
    return vals.transpose(0, 1, 3, 2).reshape(g * 512, n)


K, T, S, N, H = 512, 2048, 512, 512, 512
P = 2 ** 7


def setup_inputs():
    n = np.random.standard_normal
    s = mx_kscale(K)[:, None]
    u = mx_kscale(H)
    packed_xT = pack_weight(n((K, T)) * s)
    return {
        "x_words": packed_xT[0],
        "x_scales": packed_xT[1],
        "w1": (n((K, H)) / np.sqrt(K) / s * u).astype(np.float32),
        "k11": np.tile(np.random.uniform(0.2, 1.0, S), (P, 1)).astype(np.float32),
        "k12": np.tile(np.random.uniform(0.2, 1.0, S), (P, 1)).astype(np.float32),
        "k21": np.tile(np.random.uniform(0.2, 1.0, S), (P, 1)).astype(np.float32),
        "k22": np.tile(np.random.uniform(0.2, 1.0, S), (P, 1)).astype(np.float32),
        "w2": (n((H, N)) / np.sqrt(2 * H) / u[:, None]).astype(np.float32),
        "w3": (n((H, N)) / np.sqrt(2 * H) / u[:, None]).astype(np.float32),
        "offs": striped(np.random.permutation(T)[:S]),
        "p1": striped8(np.stack([np.random.permutation(S) for _ in range(8)])),
        "p2": striped8(np.stack([np.random.permutation(S) for _ in range(8)])),
    }


def reference(x_words, x_scales, w1, k11, k12, k21, k22, w2, w3, offs, p1, p2):
    xq = unpack_weight(x_words, x_scales)[:, unstriped(offs)]
    y = mxq(f64(w1), 0, "e4m3").T @ xq
    z = f64(k11)[:1] * (y[np.arange(H)[:, None], runs(p1, H)]) + f64(k12)[:1] * (y[np.arange(H)[:, None], runs(p2, H)])
    z2 = f64(k21)[:1] * (y[np.arange(H)[:, None], runs(p1, H)]) + f64(k22)[:1] * (y[np.arange(H)[:, None], runs(p2, H)])
    return mxq(f64(w2), 0, "e4m3").T @ mxq(z, 0, "e4m3") + mxq(f64(w3), 0, "e4m3").T @ mxq(z2, 0, "e4m3")

@@ -1,0 +1,235 @@
+from contextlib import ExitStack
+
+import concourse.mybir as mybir
+from concourse.masks import make_identity
+
+K, T, S, N, H = 512, 2048, 512, 512, 512
+P = 128
+PACK = 4
+BLOCKS = S // P
+FLOPS = 2 * K * H * S + 2 * 2 * H * N * S
+BYTES = K * T + 16 * T + 3 * 4 * K * H + 4 * 4 * S + 3 * 2 * P * (S // 16) + 4 * N * S
+
+F32 = mybir.dt.float32
+BF16 = mybir.dt.bfloat16
+I32 = mybir.dt.int32
+U32 = mybir.dt.uint32
+U16 = mybir.dt.uint16
+U8 = mybir.dt.uint8
+FP8X4 = mybir.dt.float8_e4m3fn_x4
+COPY = mybir.ActivationFunctionType.Copy
+MULT = mybir.AluOpType.mult
+ADD = mybir.AluOpType.add
+
+HALF = H // 2
+M_HALF = HALF // PACK
+M_VECTOR = 40
+
+
+def tile_picked_kpconv2_none_p_kernel(
+    tc, x_words, x_scales, w1, k11, k12, k21, k22, w2, w3, offs, p1, p2, out
+):
+    nc = tc.nc
+    with ExitStack() as ctx:
+        keep = ctx.enter_context(tc.tile_pool(name="keep", bufs=1))
+        psum = ctx.enter_context(tc.psum_pool(name="psum", bufs=1))
+        banks = [psum.tile([P, 512], F32, name="bank%d" % i) for i in range(8)]
+
+        def sb(name, shape, dtype):
+            return keep.tile(shape, dtype, name=name, align_bytes=64)
+
+        offs_t = sb("offs_t", [P, S // 16], U16)
+        p1_t = sb("p1_t", [P, S // 16], U16)
+        p2_t = sb("p2_t", [P, S // 16], U16)
+        xw = sb("xw", [P, T], U32)
+        xs = sb("xs", [P, T], U8)
+        w1_raw = [sb("w1_raw%d" % c, [P, PACK, HALF], F32) for c in range(2)]
+        w_raw = [sb("w_raw%d" % i, [P, PACK, N], F32) for i in range(2)]
+        ident = sb("ident", [P, P], F32)
+        k_rows = sb("k_rows", [P, P], F32)
+        k_cols = sb("k_cols", [P, 4 * BLOCKS], F32)
+
+        nc.gpsimd.memset(xs[:].bitcast(I32), 0)
+        nc.vector.memset(k_rows[:64, :], 0.0)
+        nc.sync.dma_start(offs_t[:], offs)
+        nc.sync.dma_start(xw[:].bitcast(I32), x_words[0].rearrange("p n t -> p (n t)").bitcast(I32))
+        for q in range(4):
+            nc.scalar.dma_start(xs[32 * q : 32 * q + 4, :].bitcast(I32), x_scales[0, 4 * q : 4 * q + 4, :].bitcast(I32))
+        w1_rows = w1.rearrange("(p j) c -> p j c", j=PACK)
+        for c in range(2):
+            nc.sync.dma_start(w1_raw[c][:], w1_rows[:, :, c * HALF : (c + 1) * HALF])
+        nc.sync.dma_start(p1_t[:], p1)
+        nc.sync.dma_start(p2_t[:], p2)
+        make_identity(nc, ident[:])
+        nc.scalar.mul(k_rows[64:, :], ident[64:, :], 0.0)
+        for i, k in enumerate((k11, k12, k21, k22)):
+            nc.sync.dma_start(k_rows[4 * i : 4 * i + 4, :], k[0:1, :].rearrange("o (b q) -> (o b) q", b=BLOCKS))
+        for i, w in enumerate((w2, w3)):
+            nc.sync.dma_start(w_raw[i][:], w.rearrange("(p j) c -> p j c", j=PACK))
+
+
+        xs_g = sb("xs_g", [P, S], U8)
+        xw_g = sb("xw_g", [P, S], U32)
+        nc.vector.tensor_copy(xs_g[:], xs[:].indirect(offs_t[:]))
+        nc.vector.tensor_copy(xw_g[:], xw[:].indirect(offs_t[:]))
+
+        w1_codes = [sb("w1_codes%d" % t, [P, P], U32) for t in range(PACK)]
+        w1_scales = [sb("w1_scales%d" % t, [P, P], U8) for t in range(PACK)]
+        for c in range(2):
+            grouped = sb("w1_grouped%d" % c, [P, PACK, M_HALF * PACK], BF16)
+            dst = grouped[:].rearrange("p t (m j) -> p m j t", j=PACK)
+            src = w1_raw[c][:].rearrange("p j (m t) -> p m j t", t=PACK)
+            if c == 0:
+                nc.vector.tensor_copy(dst, src)
+            else:
+                nc.vector.tensor_copy(dst[:, :M_VECTOR], src[:, :M_VECTOR])
+                nc.scalar.copy(dst[:, M_VECTOR:], src[:, M_VECTOR:])
+            cols = slice(c * M_HALF, (c + 1) * M_HALF)
+            for t in range(PACK):
+                nc.vector.quantize_mx(out=w1_codes[t][:, cols].bitcast(FP8X4), scales=w1_scales[t][:, cols], in_=grouped[:, t, :])
+
+        y = [sb("y%d" % t, [P, S], F32) for t in range(PACK)]
+        for t in range(PACK):
+            nc.tensor.matmul_mx(
+                out=banks[t][:],
+                lhsT=w1_codes[t][:].bitcast(FP8X4),
+                lhsT_scale=w1_scales[t][:],
+                rhs=xw_g[:].bitcast(FP8X4),
+                rhs_scale=xs_g[:],
+                start=True,
+                stop=True,
+            )
+            nc.scalar.copy(y[t][:], banks[t][:])
+
+        nc.tensor.transpose(banks[7][:, :P], k_rows[:], ident[:])
+        nc.scalar.copy(k_cols[:], banks[7][:, : 4 * BLOCKS])
+
+        w_codes = [[sb("w_codes%d_%d" % (i, mt), [P, P], U32) for mt in range(4)] for i in range(2)]
+        w_scales = [[sb("w_scales%d_%d" % (i, mt), [P, P], U8) for mt in range(4)] for i in range(2)]
+
+        w_grouped = [[sb("w_grouped%d_%d" % (i, mt), [P, 2 * P], F32) for mt in range(4)] for i in range(2)]
+        z_in = {(b, i): sb("z_in%d_%d" % (b, i), [P, 2 * P], F32) for b in range(BLOCKS) for i in range(2)}
+
+        def prepare_weight(i, mt):
+            grouped = w_grouped[i][mt][:].bitcast(BF16)
+            nc.scalar.copy(
+                grouped.rearrange("p (c i j) -> p c j i", i=4, j=PACK),
+                w_raw[i][:, :, mt * P : (mt + 1) * P].rearrange("p j (c i) -> p c j i", i=4),
+            )
+            nc.vector.quantize_mx(out=w_codes[i][mt][:].bitcast(FP8X4), scales=w_scales[i][mt][:], in_=grouped)
+
+        work = [[sb("work%d_%d" % (s, i), [P, 512], F32)[:] for i in range(2)] for s in range(4)]
+        first_terms = [work[2], [w_raw[0][:, i, :] for i in range(2)], [w_raw[1][:, i, :] for i in range(2)], work[3]]
+
+        def quarters(row):
+            return [row[:, t * P : (t + 1) * P] for t in range(PACK)]
+
+        gathered = [[quarters(work[b][l]) for l in range(2)] for b in range(3)]
+        gathered.append(
+            [
+                [w_grouped[1][3][:, :P], w_grouped[1][3][:, P:], z_in[0, 1][:, :P], z_in[1, 1][:, :P]],
+                [first_terms[2][1][:, :P], first_terms[2][1][:, P : 2 * P], first_terms[2][1][:, 2 * P : 3 * P], first_terms[2][1][:, 3 * P :]],
+            ]
+        )
+        lists = (p1_t, p2_t)
+
+        def gather(b, which=(0, 1)):
+            pairs = [(l, t) for l in which for t in range(PACK)]
+            if b == 0:
+                pairs = [(l, t) for t in range(PACK) for l in range(2)]
+            for l, t in pairs:
+                piece = gathered[b][l][t]
+                nc.vector.tensor_copy(piece, y[t][:].indirect(lists[l][:, 8 * b : 8 * b + 8]))
+                place = t // 2 + 2 * (t % 2)
+                nc.tensor.transpose(banks[2 * (b % 2) + l][:, place * P : (place + 1) * P], piece, ident[:])
+
+        z_codes = {}
+        z_scales = {}
+
+        def combine(b):
+            turned = [banks[2 * (b % 2) + l][:].rearrange("q (e x) -> q x e", e=2) for l in range(2)]
+            for i in range(2):
+                first = first_terms[b][i].rearrange("q (x e) -> q x e", e=2)
+                nc.scalar.activation(first, turned[0], COPY, scale=k_cols[:, 8 * i + b : 8 * i + b + 1])
+            for i in range(2):
+                first = first_terms[b][i].rearrange("q (x e) -> q x e", e=2)
+                zt = sb("zt%d_%d" % (b, i), [P, H], BF16)
+                nc.vector.scalar_tensor_tensor(
+                    out=zt[:].rearrange("q (x e) -> q x e", e=2),
+                    in0=turned[1],
+                    scalar=k_cols[:, 8 * i + 4 + b : 8 * i + 4 + b + 1],
+                    in1=first,
+                    op0=MULT,
+                    op1=ADD,
+                )
+                words = zt[:].bitcast(F32)
+                for u in range(2):
+                    nc.tensor.transpose(banks[4 + i][:, u * P : (u + 1) * P], words[:, u * P : (u + 1) * P], ident[:])
+                nc.scalar.copy(
+                    z_in[b, i][:].rearrange("p (j u) -> p j u", u=2),
+                    banks[4 + i][:, : 2 * P].rearrange("p (u j) -> p j u", u=2),
+                )
+                z_codes[b, i] = sb("z_codes%d_%d" % (b, i), [P, P], U32)
+                z_scales[b, i] = sb("z_scales%d_%d" % (b, i), [P, P], U8)
+
+        def quantise(b):
+            for i in range(2):
+                nc.vector.quantize_mx(out=z_codes[b, i][:].bitcast(FP8X4), scales=z_scales[b, i][:], in_=z_in[b, i][:].bitcast(BF16))
+
+        out_rows = out.rearrange("(mt p) j -> p mt j", p=P)
+
+        def product(b, i, mt, target):
+            nc.tensor.matmul_mx(
+                out=target,
+                lhsT=w_codes[i][mt][:].bitcast(FP8X4),
+                lhsT_scale=w_scales[i][mt][:],
+                rhs=z_codes[b, i][:].bitcast(FP8X4),
+                rhs_scale=z_scales[b, i][:],
+                start=(i == 0),
+                stop=(i == 1),
+            )
+
+        def finish(b):
+            result = sb("result%d" % b, [P, 4, P], F32)
+            bank = banks[6 + b % 2]
+            for mt in range(4):
+                for i in range(2):
+                    product(b, i, mt, bank[:, mt * P : (mt + 1) * P])
+            nc.scalar.copy(result[:].rearrange("p mt j -> p (mt j)"), bank[:])
+            nc.sync.dma_start(out_rows[:, :, b * P : (b + 1) * P], result[:])
+
+        def finish_last(b):
+            targets = [banks[n][:, :P] for n in (6, 0, 1, 7)]
+            for i in range(2):
+                for mt in range(4):
+                    product(b, i, mt, targets[mt])
+            for mt in range(4):
+                result = sb("last%d" % mt, [P, P], F32)
+                if mt % 2 == 0:
+                    nc.vector.tensor_copy(result[:], targets[mt])
+                    nc.sync.dma_start(out_rows[:, mt, b * P : (b + 1) * P], result[:])
+                else:
+                    nc.scalar.copy(result[:], targets[mt])
+                    nc.scalar.dma_start(out_rows[:, mt, b * P : (b + 1) * P], result[:])
+
+        gather(0)
+        gather(1)
+        combine(0)
+        for mt in range(4):
+            prepare_weight(0, mt)
+        gather(2)
+        combine(1)
+        for mt in range(4):
+            prepare_weight(1, mt)
+        quantise(0)
+        finish(0)
+        quantise(1)
+        finish(1)
+        gather(3, (0,))
+        combine(2)
+        gather(3, (1,))
+        quantise(2)
+        finish(2)
+        combine(3)
+        quantise(3)
+        finish_last(3)

@@ -21,9 +21,8 @@ COPY = mybir.ActivationFunctionType.Copy
 MULT = mybir.AluOpType.mult
 ADD = mybir.AluOpType.add
 
-HALF = H // 2
-M_HALF = HALF // PACK
-M_VECTOR = 40
+HALF = S // 2
+M_VECTOR = 64
 
 
 def tile_picked_kpconv2_none_p_kernel(
@@ -43,193 +42,206 @@ def tile_picked_kpconv2_none_p_kernel(
         p2_t = sb("p2_t", [P, S // 16], U16)
         xw = sb("xw", [P, T], U32)
         xs = sb("xs", [P, T], U8)
-        w1_raw = [sb("w1_raw%d" % c, [P, PACK, HALF], F32) for c in range(2)]
-        w_raw = [sb("w_raw%d" % i, [P, PACK, N], F32) for i in range(2)]
+        w1_raw = sb("w1_raw", [P, PACK, H], F32)
+        w_flat = [sb("w_flat%d" % i, [P, PACK * N], F32) for i in range(2)]
+        w_raw = [flat[:].rearrange("p (j c) -> p j c", j=PACK) for flat in w_flat]
         ident = sb("ident", [P, P], F32)
         k_rows = sb("k_rows", [P, P], F32)
         k_cols = sb("k_cols", [P, 4 * BLOCKS], F32)
 
         nc.gpsimd.memset(xs[:].bitcast(I32), 0)
-        nc.vector.memset(k_rows[:64, :], 0.0)
         nc.sync.dma_start(offs_t[:], offs)
-        nc.sync.dma_start(xw[:].bitcast(I32), x_words[0].rearrange("p n t -> p (n t)").bitcast(I32))
-        for q in range(4):
-            nc.scalar.dma_start(xs[32 * q : 32 * q + 4, :].bitcast(I32), x_scales[0, 4 * q : 4 * q + 4, :].bitcast(I32))
-        w1_rows = w1.rearrange("(p j) c -> p j c", j=PACK)
-        for c in range(2):
-            nc.sync.dma_start(w1_raw[c][:], w1_rows[:, :, c * HALF : (c + 1) * HALF])
         nc.sync.dma_start(p1_t[:], p1)
         nc.sync.dma_start(p2_t[:], p2)
-        make_identity(nc, ident[:])
-        nc.scalar.mul(k_rows[64:, :], ident[64:, :], 0.0)
         for i, k in enumerate((k11, k12, k21, k22)):
-            nc.sync.dma_start(k_rows[4 * i : 4 * i + 4, :], k[0:1, :].rearrange("o (b q) -> (o b) q", b=BLOCKS))
+            nc.scalar.dma_start(k_rows[32 * i : 32 * i + 32, :], k[0:8, :].rearrange("r (b q) -> (r b) q", b=BLOCKS))
+        nc.sync.dma_start(w1_raw[:], w1.rearrange("(p j) c -> p j c", j=PACK))
+        for q in range(4):
+            nc.sync.dma_start(xs[32 * q : 32 * q + 4, :].bitcast(I32), x_scales[0, 4 * q : 4 * q + 4, :].bitcast(I32))
+        nc.sync.dma_start(xw[:].bitcast(I32), x_words[0].rearrange("p n t -> p (n t)").bitcast(I32))
+        make_identity(nc, ident[:])
         for i, w in enumerate((w2, w3)):
-            nc.sync.dma_start(w_raw[i][:], w.rearrange("(p j) c -> p j c", j=PACK))
-
+            nc.sync.dma_start(w_flat[i][:], w.rearrange("(p j) c -> p (j c)", j=PACK))
 
         xs_g = sb("xs_g", [P, S], U8)
         xw_g = sb("xw_g", [P, S], U32)
         nc.vector.tensor_copy(xs_g[:], xs[:].indirect(offs_t[:]))
-        nc.vector.tensor_copy(xw_g[:], xw[:].indirect(offs_t[:]))
 
-        w1_codes = [sb("w1_codes%d" % t, [P, P], U32) for t in range(PACK)]
-        w1_scales = [sb("w1_scales%d" % t, [P, P], U8) for t in range(PACK)]
-        for c in range(2):
-            grouped = sb("w1_grouped%d" % c, [P, PACK, M_HALF * PACK], BF16)
-            dst = grouped[:].rearrange("p t (m j) -> p m j t", j=PACK)
-            src = w1_raw[c][:].rearrange("p j (m t) -> p m j t", t=PACK)
-            if c == 0:
-                nc.vector.tensor_copy(dst, src)
-            else:
-                nc.vector.tensor_copy(dst[:, :M_VECTOR], src[:, :M_VECTOR])
-                nc.scalar.copy(dst[:, M_VECTOR:], src[:, M_VECTOR:])
-            cols = slice(c * M_HALF, (c + 1) * M_HALF)
-            for t in range(PACK):
-                nc.vector.quantize_mx(out=w1_codes[t][:, cols].bitcast(FP8X4), scales=w1_scales[t][:, cols], in_=grouped[:, t, :])
+        w1_codes = sb("w1_codes", [P, H], U32)
+        w1_scales = sb("w1_scales", [P, H], U8)
+        w1_grouped = sb("w1_grouped", [P, H * PACK], BF16)
+        dst = w1_grouped[:].rearrange("p (t m j) -> p m j t", t=PACK, j=PACK)
+        src = w1_raw[:].rearrange("p j (m t) -> p m j t", t=PACK)
+        nc.vector.tensor_copy(dst[:, :M_VECTOR], src[:, :M_VECTOR])
+        nc.scalar.copy(dst[:, M_VECTOR:], src[:, M_VECTOR:])
+        nc.vector.quantize_mx(out=w1_codes[:].bitcast(FP8X4), scales=w1_scales[:], in_=w1_grouped[:])
+
+        for h in range(2):
+            nc.vector.tensor_copy(xw_g[:, h * HALF : (h + 1) * HALF], xw[:].indirect(offs_t[:, 16 * h : 16 * h + 16]))
+
+        nc.tensor.transpose(banks[5][:, :P], k_rows[:], ident[:])
+        nc.scalar.copy(
+            k_cols[:].rearrange("q (i b) -> q i b", b=BLOCKS),
+            banks[5][:, :P].rearrange("q (i r) -> q i r", i=4)[:, :, :BLOCKS],
+        )
 
         y = [sb("y%d" % t, [P, S], F32) for t in range(PACK)]
-        for t in range(PACK):
+        whole = slice(0, S)
+        steps = [(0, slice(0, HALF), 4), (0, slice(HALF, S), 5), (1, whole, 6), (2, whole, 7), (3, whole, 4)]
+        for t, cols, bank in steps:
+            width = cols.stop - cols.start
             nc.tensor.matmul_mx(
-                out=banks[t][:],
-                lhsT=w1_codes[t][:].bitcast(FP8X4),
-                lhsT_scale=w1_scales[t][:],
-                rhs=xw_g[:].bitcast(FP8X4),
-                rhs_scale=xs_g[:],
+                out=banks[bank][:, :width],
+                lhsT=w1_codes[:, t * P : (t + 1) * P].bitcast(FP8X4),
+                lhsT_scale=w1_scales[:, t * P : (t + 1) * P],
+                rhs=xw_g[:, cols].bitcast(FP8X4),
+                rhs_scale=xs_g[:, cols],
                 start=True,
                 stop=True,
             )
-            nc.scalar.copy(y[t][:], banks[t][:])
+            nc.scalar.copy(y[t][:, cols], banks[bank][:, :width])
 
-        nc.tensor.transpose(banks[7][:, :P], k_rows[:], ident[:])
-        nc.scalar.copy(k_cols[:], banks[7][:, : 4 * BLOCKS])
+        w_codes = [sb("w_codes%d" % i, [P, N], U32) for i in range(2)]
+        w_scales = [sb("w_scales%d" % i, [P, N], U8) for i in range(2)]
+        w_grouped = [sb("w_grouped%d" % i, [P, 2 * N], F32) for i in range(2)]
+        z_pair = sb("z_pair", [P, 2, 2, 2 * P], F32)
+        z_third = sb("z_third", [P, 2, 2 * P], F32)
+        z_last = [sb("z_last%d" % i, [P, 2 * P], F32) for i in range(2)]
 
-        w_codes = [[sb("w_codes%d_%d" % (i, mt), [P, P], U32) for mt in range(4)] for i in range(2)]
-        w_scales = [[sb("w_scales%d_%d" % (i, mt), [P, P], U8) for mt in range(4)] for i in range(2)]
+        def cast_weight(i, c0, c1):
+            dst = w_grouped[i][:].bitcast(BF16)[:, c0 * PACK : c1 * PACK].rearrange("p (c i j) -> p c j i", i=4, j=PACK)
+            src = w_raw[i][:, :, c0:c1].rearrange("p j (c i) -> p c j i", i=4)
+            nc.scalar.copy(dst, src)
 
-        w_grouped = [[sb("w_grouped%d_%d" % (i, mt), [P, 2 * P], F32) for mt in range(4)] for i in range(2)]
-        z_in = {(b, i): sb("z_in%d_%d" % (b, i), [P, 2 * P], F32) for b in range(BLOCKS) for i in range(2)}
+        def quantise_weight(i):
+            nc.vector.quantize_mx(out=w_codes[i][:].bitcast(FP8X4), scales=w_scales[i][:], in_=w_grouped[i][:].bitcast(BF16))
 
-        def prepare_weight(i, mt):
-            grouped = w_grouped[i][mt][:].bitcast(BF16)
-            nc.scalar.copy(
-                grouped.rearrange("p (c i j) -> p c j i", i=4, j=PACK),
-                w_raw[i][:, :, mt * P : (mt + 1) * P].rearrange("p j (c i) -> p c j i", i=4),
-            )
-            nc.vector.quantize_mx(out=w_codes[i][mt][:].bitcast(FP8X4), scales=w_scales[i][mt][:], in_=grouped)
-
-        work = [[sb("work%d_%d" % (s, i), [P, 512], F32)[:] for i in range(2)] for s in range(4)]
-        first_terms = [work[2], [w_raw[0][:, i, :] for i in range(2)], [w_raw[1][:, i, :] for i in range(2)], work[3]]
-
-        def quarters(row):
-            return [row[:, t * P : (t + 1) * P] for t in range(PACK)]
-
-        gathered = [[quarters(work[b][l]) for l in range(2)] for b in range(3)]
-        gathered.append(
-            [
-                [w_grouped[1][3][:, :P], w_grouped[1][3][:, P:], z_in[0, 1][:, :P], z_in[1, 1][:, :P]],
-                [first_terms[2][1][:, :P], first_terms[2][1][:, P : 2 * P], first_terms[2][1][:, 2 * P : 3 * P], first_terms[2][1][:, 3 * P :]],
-            ]
-        )
         lists = (p1_t, p2_t)
+        first_terms = [
+            [w_flat[0][:, :H], w_flat[0][:, H : 2 * H]],
+            [w_flat[0][:, 2 * H : 3 * H], w_flat[0][:, 3 * H :]],
+            [sb("first2_%d" % i, [P, H], F32)[:] for i in range(2)],
+            [sb("first3_%d" % i, [P, H], F32)[:] for i in range(2)],
+        ]
 
-        def gather(b, which=(0, 1)):
-            pairs = [(l, t) for l in which for t in range(PACK)]
-            if b == 0:
-                pairs = [(l, t) for t in range(PACK) for l in range(2)]
-            for l, t in pairs:
-                piece = gathered[b][l][t]
-                nc.vector.tensor_copy(piece, y[t][:].indirect(lists[l][:, 8 * b : 8 * b + 8]))
-                place = t // 2 + 2 * (t % 2)
-                nc.tensor.transpose(banks[2 * (b % 2) + l][:, place * P : (place + 1) * P], piece, ident[:])
+        def gather(l, t, b0, nb, target):
+            nc.vector.tensor_copy(target, y[t][:].indirect(lists[l][:, 8 * b0 : 8 * (b0 + nb)]))
 
-        z_codes = {}
-        z_scales = {}
+        def turn(l, t, b, piece):
+            place = t // 2 + 2 * (t % 2)
+            nc.tensor.transpose(banks[2 * (b % 2) + l][:, place * P : (place + 1) * P], piece, ident[:])
 
-        def combine(b):
-            turned = [banks[2 * (b % 2) + l][:].rearrange("q (e x) -> q x e", e=2) for l in range(2)]
+        def scale_first(b):
+            turned = banks[2 * (b % 2)][:].rearrange("q (e x) -> q x e", e=2)
             for i in range(2):
                 first = first_terms[b][i].rearrange("q (x e) -> q x e", e=2)
-                nc.scalar.activation(first, turned[0], COPY, scale=k_cols[:, 8 * i + b : 8 * i + b + 1])
-            for i in range(2):
-                first = first_terms[b][i].rearrange("q (x e) -> q x e", e=2)
-                zt = sb("zt%d_%d" % (b, i), [P, H], BF16)
-                nc.vector.scalar_tensor_tensor(
-                    out=zt[:].rearrange("q (x e) -> q x e", e=2),
-                    in0=turned[1],
-                    scalar=k_cols[:, 8 * i + 4 + b : 8 * i + 4 + b + 1],
-                    in1=first,
-                    op0=MULT,
-                    op1=ADD,
-                )
-                words = zt[:].bitcast(F32)
-                for u in range(2):
-                    nc.tensor.transpose(banks[4 + i][:, u * P : (u + 1) * P], words[:, u * P : (u + 1) * P], ident[:])
-                nc.scalar.copy(
-                    z_in[b, i][:].rearrange("p (j u) -> p j u", u=2),
-                    banks[4 + i][:, : 2 * P].rearrange("p (u j) -> p j u", u=2),
-                )
-                z_codes[b, i] = sb("z_codes%d_%d" % (b, i), [P, P], U32)
-                z_scales[b, i] = sb("z_scales%d_%d" % (b, i), [P, P], U8)
+                nc.scalar.activation(first, turned, COPY, scale=k_cols[:, 8 * i + b : 8 * i + b + 1])
 
-        def quantise(b):
+        def combine(b, i, target):
+            zt = sb("zt%d_%d" % (b, i), [P, H], BF16)
+            nc.vector.scalar_tensor_tensor(
+                out=zt[:].rearrange("q (x e) -> q x e", e=2),
+                in0=banks[2 * (b % 2) + 1][:].rearrange("q (e x) -> q x e", e=2),
+                scalar=k_cols[:, 8 * i + 4 + b : 8 * i + 4 + b + 1],
+                in1=first_terms[b][i].rearrange("q (x e) -> q x e", e=2),
+                op0=MULT,
+                op1=ADD,
+            )
+            words = zt[:].bitcast(F32)
+            for u in range(2):
+                nc.tensor.transpose(target[:, u * P : (u + 1) * P], words[:, u * P : (u + 1) * P], ident[:])
+
+        def combine_both(b, bank, target):
             for i in range(2):
-                nc.vector.quantize_mx(out=z_codes[b, i][:].bitcast(FP8X4), scales=z_scales[b, i][:], in_=z_in[b, i][:].bitcast(BF16))
+                combine(b, i, bank[:, 2 * i * P : 2 * (i + 1) * P])
+            nc.scalar.copy(target.rearrange("p i (j u) -> p i j u", u=2), bank[:].rearrange("p (i u j) -> p i j u", i=2, u=2))
+
+        def quantise(name, words, width):
+            codes = sb(name + "_codes", [P, width], U32)
+            scales = sb(name + "_scales", [P, width], U8)
+            nc.vector.quantize_mx(out=codes[:].bitcast(FP8X4), scales=scales[:], in_=words.bitcast(BF16))
+            return codes, scales
 
         out_rows = out.rearrange("(mt p) j -> p mt j", p=P)
 
-        def product(b, i, mt, target):
+        def product(i, mt, codes, scales, target):
             nc.tensor.matmul_mx(
                 out=target,
-                lhsT=w_codes[i][mt][:].bitcast(FP8X4),
-                lhsT_scale=w_scales[i][mt][:],
-                rhs=z_codes[b, i][:].bitcast(FP8X4),
-                rhs_scale=z_scales[b, i][:],
+                lhsT=w_codes[i][:, mt * P : (mt + 1) * P].bitcast(FP8X4),
+                lhsT_scale=w_scales[i][:, mt * P : (mt + 1) * P],
+                rhs=codes.bitcast(FP8X4),
+                rhs_scale=scales,
                 start=(i == 0),
                 stop=(i == 1),
             )
 
-        def finish(b):
-            result = sb("result%d" % b, [P, 4, P], F32)
-            bank = banks[6 + b % 2]
-            for mt in range(4):
-                for i in range(2):
-                    product(b, i, mt, bank[:, mt * P : (mt + 1) * P])
-            nc.scalar.copy(result[:].rearrange("p mt j -> p (mt j)"), bank[:])
-            nc.sync.dma_start(out_rows[:, :, b * P : (b + 1) * P], result[:])
+        early = [[sb("early%d_%d" % (l, t), [P, HALF], F32) for t in range(PACK)] for l in range(2)]
+        late = [sb("late%d" % t, [P, HALF], F32) for t in range(PACK)]
+        for t in range(PACK):
+            for l in range(2):
+                gather(l, t, 0, 2, early[l][t][:])
+                for b in range(2):
+                    turn(l, t, b, early[l][t][:, b * P : (b + 1) * P])
+            gather(0, t, 2, 2, late[t][:])
+        for c0 in range(0, N, 256):
+            cast_weight(0, c0, c0 + 256)
+        quantise_weight(0)
+        cast_weight(1, 0, 256)
 
-        def finish_last(b):
-            targets = [banks[n][:, :P] for n in (6, 0, 1, 7)]
+        for b in range(2):
+            scale_first(b)
+        cast_weight(1, 256, 512)
+        for b in range(2):
+            combine_both(b, banks[4 + b], z_pair[:, :, b, :])
+        for b in range(2, 4):
+            for t in range(PACK):
+                turn(0, t, b, late[t][:, (b - 2) * P : (b - 1) * P])
+        for t in range(PACK):
+            piece = first_terms[1][1][:, t * P : (t + 1) * P]
+            gather(1, t, 2, 1, piece)
+            turn(1, t, 2, piece)
+        quantise_weight(1)
+        codes, scales = quantise("pair", z_pair[:].rearrange("p i b w -> p (i b w)"), 4 * P)
+        scale_first(2)
+        result = sb("result_pair", [P, 4, HALF], F32)
+        for mt in range(4):
             for i in range(2):
-                for mt in range(4):
-                    product(b, i, mt, targets[mt])
+                cols = slice(i * HALF, (i + 1) * HALF)
+                product(i, mt, codes[:, cols], scales[:, cols], banks[6 + mt // 2][:, (mt % 2) * HALF : (mt % 2 + 1) * HALF])
+        combine_both(2, banks[5], z_third[:])
+        scale_first(3)
+        for t in range(PACK):
+            piece = first_terms[2][1][:, t * P : (t + 1) * P]
+            gather(1, t, 3, 1, piece)
+            turn(1, t, 3, piece)
+        for half in range(2):
+            rows = result[:, 2 * half : 2 * half + 2, :]
+            nc.scalar.copy(rows.rearrange("p mt j -> p (mt j)"), banks[6 + half][:])
+            nc.sync.dma_start(out_rows[:, 2 * half : 2 * half + 2, :HALF], rows)
+        codes, scales = quantise("third", z_third[:].rearrange("p i w -> p (i w)"), 2 * P)
+        for mt in range(4):
+            for i in range(2):
+                cols = slice(i * P, (i + 1) * P)
+                product(i, mt, codes[:, cols], scales[:, cols], banks[0][:, mt * P : (mt + 1) * P])
+        last = []
+        for i in range(2):
+            bank = banks[4 + i]
+            combine(3, i, bank[:, : 2 * P])
+            nc.scalar.copy(z_last[i][:].rearrange("p (j u) -> p j u", u=2), bank[:, : 2 * P].rearrange("p (u j) -> p j u", u=2))
+        for i in range(2):
+            last.append(quantise("last%d" % i, z_last[i][:], P))
+        result = sb("result_third", [P, 4, P], F32)
+        nc.scalar.copy(result[:].rearrange("p mt j -> p (mt j)"), banks[0][:])
+        nc.sync.dma_start(out_rows[:, :, 2 * P : 3 * P], result[:])
+        targets = [banks[n][:, :P] for n in (1, 2, 6, 7)]
+        for i in range(2):
             for mt in range(4):
-                result = sb("last%d" % mt, [P, P], F32)
-                if mt % 2 == 0:
-                    nc.vector.tensor_copy(result[:], targets[mt])
-                    nc.sync.dma_start(out_rows[:, mt, b * P : (b + 1) * P], result[:])
-                else:
-                    nc.scalar.copy(result[:], targets[mt])
-                    nc.scalar.dma_start(out_rows[:, mt, b * P : (b + 1) * P], result[:])
-
-        gather(0)
-        gather(1)
-        combine(0)
+                product(i, mt, last[i][0][:], last[i][1][:], targets[mt])
         for mt in range(4):
-            prepare_weight(0, mt)
-        gather(2)
-        combine(1)
-        for mt in range(4):
-            prepare_weight(1, mt)
-        quantise(0)
-        finish(0)
-        quantise(1)
-        finish(1)
-        gather(3, (0,))
-        combine(2)
-        gather(3, (1,))
-        quantise(2)
-        finish(2)
-        combine(3)
-        quantise(3)
-        finish_last(3)
+            result = sb("result_last%d" % mt, [P, P], F32)
+            if mt % 2 == 0:
+                nc.vector.tensor_copy(result[:], targets[mt])
+                nc.sync.dma_start(out_rows[:, mt, 3 * P :], result[:])
+            else:
+                nc.scalar.copy(result[:], targets[mt])
+                nc.scalar.dma_start(out_rows[:, mt, 3 * P :], result[:])

@@ -22,7 +22,7 @@ MULT = mybir.AluOpType.mult
 ADD = mybir.AluOpType.add
 
 HALF = S // 2
-M_VECTOR = 64
+M_VECTOR = 40
 
 
 def tile_picked_kpconv2_none_p_kernel(
@@ -65,7 +65,6 @@ def tile_picked_kpconv2_none_p_kernel(
 
         xs_g = sb("xs_g", [P, S], U8)
         xw_g = sb("xw_g", [P, S], U32)
-        nc.vector.tensor_copy(xs_g[:], xs[:].indirect(offs_t[:]))
 
         w1_codes = sb("w1_codes", [P, H], U32)
         w1_scales = sb("w1_scales", [P, H], U8)
@@ -74,6 +73,7 @@ def tile_picked_kpconv2_none_p_kernel(
         src = w1_raw[:].rearrange("p j (m t) -> p m j t", t=PACK)
         nc.vector.tensor_copy(dst[:, :M_VECTOR], src[:, :M_VECTOR])
         nc.scalar.copy(dst[:, M_VECTOR:], src[:, M_VECTOR:])
+        nc.vector.tensor_copy(xs_g[:], xs[:].indirect(offs_t[:]))
         nc.vector.quantize_mx(out=w1_codes[:].bitcast(FP8X4), scales=w1_scales[:], in_=w1_grouped[:])
 
         for h in range(2):
@@ -101,27 +101,18 @@ def tile_picked_kpconv2_none_p_kernel(
             )
             nc.scalar.copy(y[t][:, cols], banks[bank][:, :width])
 
-        w_codes = [sb("w_codes%d" % i, [P, N], U32) for i in range(2)]
-        w_scales = [sb("w_scales%d" % i, [P, N], U8) for i in range(2)]
-        w_grouped = [sb("w_grouped%d" % i, [P, 2 * N], F32) for i in range(2)]
-        z_pair = sb("z_pair", [P, 2, 2, 2 * P], F32)
-        z_third = sb("z_third", [P, 2, 2 * P], F32)
+        w_codes = sb("w_codes", [P, 2 * N], U32)
+        w_scales = sb("w_scales", [P, 2 * N], U8)
+        w_grouped = sb("w_grouped", [P, 2 * N * PACK], BF16)
+        z_both = [sb("z_both%d" % b, [P, 4 * P], F32) for b in range(3)]
         z_last = [sb("z_last%d" % i, [P, 2 * P], F32) for i in range(2)]
-
-        def cast_weight(i, c0, c1):
-            dst = w_grouped[i][:].bitcast(BF16)[:, c0 * PACK : c1 * PACK].rearrange("p (c i j) -> p c j i", i=4, j=PACK)
-            src = w_raw[i][:, :, c0:c1].rearrange("p j (c i) -> p c j i", i=4)
-            nc.scalar.copy(dst, src)
-
-        def quantise_weight(i):
-            nc.vector.quantize_mx(out=w_codes[i][:].bitcast(FP8X4), scales=w_scales[i][:], in_=w_grouped[i][:].bitcast(BF16))
 
         lists = (p1_t, p2_t)
         first_terms = [
-            [w_flat[0][:, :H], w_flat[0][:, H : 2 * H]],
-            [w_flat[0][:, 2 * H : 3 * H], w_flat[0][:, 3 * H :]],
+            [w_flat[1][:, :H], w_flat[1][:, H : 2 * H]],
+            [w_flat[1][:, 2 * H : 3 * H], w_flat[1][:, 3 * H :]],
             [sb("first2_%d" % i, [P, H], F32)[:] for i in range(2)],
-            [sb("first3_%d" % i, [P, H], F32)[:] for i in range(2)],
+            [z_both[0][:], sb("first3_1", [P, H], F32)[:]],
         ]
 
         def gather(l, t, b0, nb, target):
@@ -138,23 +129,26 @@ def tile_picked_kpconv2_none_p_kernel(
                 nc.scalar.activation(first, turned, COPY, scale=k_cols[:, 8 * i + b : 8 * i + b + 1])
 
         def combine(b, i, target):
-            zt = sb("zt%d_%d" % (b, i), [P, H], BF16)
+            if b >= 2 and i == 0:
+                zt = z_both[b - 1][:, : 2 * P].bitcast(BF16)
+            else:
+                zt = sb("zt%d_%d" % (b, i), [P, H], BF16)[:]
             nc.vector.scalar_tensor_tensor(
-                out=zt[:].rearrange("q (x e) -> q x e", e=2),
+                out=zt.rearrange("q (x e) -> q x e", e=2),
                 in0=banks[2 * (b % 2) + 1][:].rearrange("q (e x) -> q x e", e=2),
                 scalar=k_cols[:, 8 * i + 4 + b : 8 * i + 4 + b + 1],
                 in1=first_terms[b][i].rearrange("q (x e) -> q x e", e=2),
                 op0=MULT,
                 op1=ADD,
             )
-            words = zt[:].bitcast(F32)
+            words = zt.bitcast(F32)
             for u in range(2):
                 nc.tensor.transpose(target[:, u * P : (u + 1) * P], words[:, u * P : (u + 1) * P], ident[:])
 
         def combine_both(b, bank, target):
             for i in range(2):
                 combine(b, i, bank[:, 2 * i * P : 2 * (i + 1) * P])
-            nc.scalar.copy(target.rearrange("p i (j u) -> p i j u", u=2), bank[:].rearrange("p (i u j) -> p i j u", i=2, u=2))
+            nc.scalar.copy(target.rearrange("p (i j u) -> p i j u", i=2, u=2), bank[:].rearrange("p (i u j) -> p i j u", i=2, u=2))
 
         def quantise(name, words, width):
             codes = sb(name + "_codes", [P, width], U32)
@@ -167,8 +161,8 @@ def tile_picked_kpconv2_none_p_kernel(
         def product(i, mt, codes, scales, target):
             nc.tensor.matmul_mx(
                 out=target,
-                lhsT=w_codes[i][:, mt * P : (mt + 1) * P].bitcast(FP8X4),
-                lhsT_scale=w_scales[i][:, mt * P : (mt + 1) * P],
+                lhsT=w_codes[:, i * N + mt * P : i * N + (mt + 1) * P].bitcast(FP8X4),
+                lhsT_scale=w_scales[:, i * N + mt * P : i * N + (mt + 1) * P],
                 rhs=codes.bitcast(FP8X4),
                 rhs_scale=scales,
                 start=(i == 0),
@@ -183,56 +177,54 @@ def tile_picked_kpconv2_none_p_kernel(
                 for b in range(2):
                     turn(l, t, b, early[l][t][:, b * P : (b + 1) * P])
             gather(0, t, 2, 2, late[t][:])
-        for c0 in range(0, N, 256):
-            cast_weight(0, c0, c0 + 256)
-        quantise_weight(0)
-        cast_weight(1, 0, 256)
-
+        for i in range(2):
+            nc.scalar.copy(
+                w_grouped[:, i * N * PACK : (i + 1) * N * PACK].rearrange("p (c i j) -> p c j i", i=4, j=PACK),
+                w_raw[i].rearrange("p j (c i) -> p c j i", i=4),
+            )
+        nc.vector.quantize_mx(out=w_codes[:].bitcast(FP8X4), scales=w_scales[:], in_=w_grouped[:])
         for b in range(2):
             scale_first(b)
-        cast_weight(1, 256, 512)
+
+        def multiply(b, bank):
+            codes, scales = quantise("z%d" % b, z_both[b][:], 2 * P)
+            for mt in range(4):
+                for i in range(2):
+                    cols = slice(i * P, (i + 1) * P)
+                    product(i, mt, codes[:, cols], scales[:, cols], bank[:, mt * P : (mt + 1) * P])
+
+        def store(b, bank, copy):
+            result = sb("result%d" % b, [P, 4, P], F32)
+            copy(result[:].rearrange("p mt j -> p (mt j)"), bank[:])
+            nc.sync.dma_start(out_rows[:, :, b * P : (b + 1) * P], result[:])
+
+        def second_list(b):
+            for t in range(PACK):
+                piece = first_terms[b - 1][1][:, t * P : (t + 1) * P]
+                gather(1, t, b, 1, piece)
+                turn(1, t, b, piece)
+
         for b in range(2):
-            combine_both(b, banks[4 + b], z_pair[:, :, b, :])
+            combine_both(b, banks[4 + b], z_both[b][:])
         for b in range(2, 4):
             for t in range(PACK):
                 turn(0, t, b, late[t][:, (b - 2) * P : (b - 1) * P])
-        for t in range(PACK):
-            piece = first_terms[1][1][:, t * P : (t + 1) * P]
-            gather(1, t, 2, 1, piece)
-            turn(1, t, 2, piece)
-        quantise_weight(1)
-        codes, scales = quantise("pair", z_pair[:].rearrange("p i b w -> p (i b w)"), 4 * P)
+        multiply(0, banks[6])
+        second_list(2)
         scale_first(2)
-        result = sb("result_pair", [P, 4, HALF], F32)
-        for mt in range(4):
-            for i in range(2):
-                cols = slice(i * HALF, (i + 1) * HALF)
-                product(i, mt, codes[:, cols], scales[:, cols], banks[6 + mt // 2][:, (mt % 2) * HALF : (mt % 2 + 1) * HALF])
-        combine_both(2, banks[5], z_third[:])
+        multiply(1, banks[7])
+        combine_both(2, banks[4], z_both[2][:])
         scale_first(3)
-        for t in range(PACK):
-            piece = first_terms[2][1][:, t * P : (t + 1) * P]
-            gather(1, t, 3, 1, piece)
-            turn(1, t, 3, piece)
-        for half in range(2):
-            rows = result[:, 2 * half : 2 * half + 2, :]
-            nc.scalar.copy(rows.rearrange("p mt j -> p (mt j)"), banks[6 + half][:])
-            nc.sync.dma_start(out_rows[:, 2 * half : 2 * half + 2, :HALF], rows)
-        codes, scales = quantise("third", z_third[:].rearrange("p i w -> p (i w)"), 2 * P)
-        for mt in range(4):
-            for i in range(2):
-                cols = slice(i * P, (i + 1) * P)
-                product(i, mt, codes[:, cols], scales[:, cols], banks[0][:, mt * P : (mt + 1) * P])
-        last = []
+        store(0, banks[6], nc.scalar.copy)
+        second_list(3)
+        store(1, banks[7], nc.scalar.copy)
+        multiply(2, banks[0])
         for i in range(2):
-            bank = banks[4 + i]
+            bank = banks[5 - i]
             combine(3, i, bank[:, : 2 * P])
             nc.scalar.copy(z_last[i][:].rearrange("p (j u) -> p j u", u=2), bank[:, : 2 * P].rearrange("p (u j) -> p j u", u=2))
-        for i in range(2):
-            last.append(quantise("last%d" % i, z_last[i][:], P))
-        result = sb("result_third", [P, 4, P], F32)
-        nc.scalar.copy(result[:].rearrange("p mt j -> p (mt j)"), banks[0][:])
-        nc.sync.dma_start(out_rows[:, :, 2 * P : 3 * P], result[:])
+        store(2, banks[0], nc.vector.tensor_copy)
+        last = [quantise("last%d" % i, z_last[i][:], P) for i in range(2)]
         targets = [banks[n][:, :P] for n in (1, 2, 6, 7)]
         for i in range(2):
             for mt in range(4):

@@ -109,24 +109,27 @@ def tile_picked_kpconv2_none_p_kernel(
 
         lists = (p1_t, p2_t)
         first_terms = [
-            [w_flat[1][:, :H], w_flat[1][:, H : 2 * H]],
-            [w_flat[1][:, 2 * H : 3 * H], w_flat[1][:, 3 * H :]],
+            [w_flat[0][:, :H], w_flat[0][:, H : 2 * H]],
+            [sb("first1_%d" % i, [P, H], F32)[:] for i in range(2)],
             [sb("first2_%d" % i, [P, H], F32)[:] for i in range(2)],
             [z_both[0][:], sb("first3_1", [P, H], F32)[:]],
         ]
+        turned_banks = [[banks[0], banks[2], banks[4], banks[5]], [banks[1], banks[3], banks[0], banks[2]]]
 
         def gather(l, t, b0, nb, target):
             nc.vector.tensor_copy(target, y[t][:].indirect(lists[l][:, 8 * b0 : 8 * (b0 + nb)]))
 
         def turn(l, t, b, piece):
             place = t // 2 + 2 * (t % 2)
-            nc.tensor.transpose(banks[2 * (b % 2) + l][:, place * P : (place + 1) * P], piece, ident[:])
+            nc.tensor.transpose(turned_banks[l][b][:, place * P : (place + 1) * P], piece, ident[:])
 
-        def scale_first(b):
-            turned = banks[2 * (b % 2)][:].rearrange("q (e x) -> q x e", e=2)
-            for i in range(2):
-                first = first_terms[b][i].rearrange("q (x e) -> q x e", e=2)
-                nc.scalar.activation(first, turned, COPY, scale=k_cols[:, 8 * i + b : 8 * i + b + 1])
+        def k_col(i, l, b):
+            n = (2 * i + l) * BLOCKS + b
+            return k_cols[:, n : n + 1]
+
+        def scale_paired(b, i):
+            turned = turned_banks[0][b][:].rearrange("q (e x) -> q x e", e=2)
+            nc.scalar.activation(first_terms[b][i].rearrange("q (x e) -> q x e", e=2), turned, COPY, scale=k_col(i, 0, b))
 
         def combine(b, i, target):
             if b >= 2 and i == 0:
@@ -135,8 +138,8 @@ def tile_picked_kpconv2_none_p_kernel(
                 zt = sb("zt%d_%d" % (b, i), [P, H], BF16)[:]
             nc.vector.scalar_tensor_tensor(
                 out=zt.rearrange("q (x e) -> q x e", e=2),
-                in0=banks[2 * (b % 2) + 1][:].rearrange("q (e x) -> q x e", e=2),
-                scalar=k_cols[:, 8 * i + 4 + b : 8 * i + 4 + b + 1],
+                in0=turned_banks[1][b][:].rearrange("q (e x) -> q x e", e=2),
+                scalar=k_col(i, 1, b),
                 in1=first_terms[b][i].rearrange("q (x e) -> q x e", e=2),
                 op0=MULT,
                 op1=ADD,
@@ -145,10 +148,16 @@ def tile_picked_kpconv2_none_p_kernel(
             for u in range(2):
                 nc.tensor.transpose(target[:, u * P : (u + 1) * P], words[:, u * P : (u + 1) * P], ident[:])
 
-        def combine_both(b, bank, target):
-            for i in range(2):
-                combine(b, i, bank[:, 2 * i * P : 2 * (i + 1) * P])
-            nc.scalar.copy(target.rearrange("p (i j u) -> p i j u", i=2, u=2), bank[:].rearrange("p (i u j) -> p i j u", i=2, u=2))
+        def weave(target, source):
+            nc.scalar.copy(target.rearrange("p (j u) -> p j u", u=2), source.rearrange("p (u j) -> p j u", u=2))
+
+        def sum_on_tensor(b, bank):
+            second = sb("second%d" % b, [P, H], F32)
+            nc.scalar.activation(second[:], turned_banks[1][b][:], COPY, scale=k_col(1, 1, b))
+            for place in range(PACK):
+                cols = slice(place * P, (place + 1) * P)
+                for n, term in enumerate((first_terms[b][1], second)):
+                    nc.tensor.matmul(bank[:, cols], term[:, cols], ident[:], start=(n == 0), stop=(n == 1), is_transpose=True)
 
         def quantise(name, words, width):
             codes = sb(name + "_codes", [P, width], U32)
@@ -169,23 +178,6 @@ def tile_picked_kpconv2_none_p_kernel(
                 stop=(i == 1),
             )
 
-        early = [[sb("early%d_%d" % (l, t), [P, HALF], F32) for t in range(PACK)] for l in range(2)]
-        late = [sb("late%d" % t, [P, HALF], F32) for t in range(PACK)]
-        for t in range(PACK):
-            for l in range(2):
-                gather(l, t, 0, 2, early[l][t][:])
-                for b in range(2):
-                    turn(l, t, b, early[l][t][:, b * P : (b + 1) * P])
-            gather(0, t, 2, 2, late[t][:])
-        for i in range(2):
-            nc.scalar.copy(
-                w_grouped[:, i * N * PACK : (i + 1) * N * PACK].rearrange("p (c i j) -> p c j i", i=4, j=PACK),
-                w_raw[i].rearrange("p j (c i) -> p c j i", i=4),
-            )
-        nc.vector.quantize_mx(out=w_codes[:].bitcast(FP8X4), scales=w_scales[:], in_=w_grouped[:])
-        for b in range(2):
-            scale_first(b)
-
         def multiply(b, bank):
             codes, scales = quantise("z%d" % b, z_both[b][:], 2 * P)
             for mt in range(4):
@@ -198,34 +190,72 @@ def tile_picked_kpconv2_none_p_kernel(
             copy(result[:].rearrange("p mt j -> p (mt j)"), bank[:])
             nc.sync.dma_start(out_rows[:, :, b * P : (b + 1) * P], result[:])
 
-        def second_list(b):
+        def second_list(b, row):
             for t in range(PACK):
-                piece = first_terms[b - 1][1][:, t * P : (t + 1) * P]
+                piece = row[:, t * P : (t + 1) * P]
                 gather(1, t, b, 1, piece)
                 turn(1, t, b, piece)
 
+        early = [[sb("early%d_%d" % (l, t), [P, HALF], F32) for t in range(PACK)] for l in range(2)]
+        for t in range(PACK):
+            for l in range(2):
+                gather(l, t, 0, 2, early[l][t][:])
+                for b in range(2):
+                    turn(l, t, b, early[l][t][:, b * P : (b + 1) * P])
+        nc.scalar.copy(
+            w_grouped[:, : N * PACK].rearrange("p (c i j) -> p c j i", i=4, j=PACK),
+            w_raw[0].rearrange("p j (c i) -> p c j i", i=4),
+        )
+        nc.gpsimd.tensor_scalar(
+            w_grouped[:, N * PACK :].rearrange("p (c j) -> p c j", j=PACK),
+            w_raw[1].rearrange("p j c -> p c j"),
+            1.0,
+            0.0,
+            MULT,
+            ADD,
+        )
+        for t in range(PACK):
+            late = w_flat[0][:, 2 * H + t * HALF : 2 * H + (t + 1) * HALF]
+            gather(0, t, 2, 2, late)
+            for b in range(2, 4):
+                turn(0, t, b, late[:, (b - 2) * P : (b - 1) * P])
+        nc.vector.quantize_mx(out=w_codes[:].bitcast(FP8X4), scales=w_scales[:], in_=w_grouped[:])
         for b in range(2):
-            combine_both(b, banks[4 + b], z_both[b][:])
-        for b in range(2, 4):
-            for t in range(PACK):
-                turn(0, t, b, late[t][:, (b - 2) * P : (b - 1) * P])
-        multiply(0, banks[6])
-        second_list(2)
-        scale_first(2)
-        multiply(1, banks[7])
-        combine_both(2, banks[4], z_both[2][:])
-        scale_first(3)
-        store(0, banks[6], nc.scalar.copy)
-        second_list(3)
-        store(1, banks[7], nc.scalar.copy)
-        multiply(2, banks[0])
+            scale_paired(b, 0)
+            nc.scalar.activation(first_terms[b][1], turned_banks[0][b][:], COPY, scale=k_col(1, 0, b))
+        for b in range(2):
+            sum_on_tensor(b, banks[6 + b])
         for i in range(2):
-            bank = banks[5 - i]
+            scale_paired(2, i)
+        for b in range(2):
+            combine(b, 0, banks[4][:, 2 * b * P : 2 * (b + 1) * P])
+        for b in range(2):
+            nc.scalar.copy(
+                z_both[b][:, 2 * P :].bitcast(BF16).rearrange("p (j u e) -> p j u e", u=2, e=2),
+                banks[6 + b][:].rearrange("p (e u j) -> p j u e", e=2, u=2),
+            )
+            weave(z_both[b][:, : 2 * P], banks[4][:, 2 * b * P : 2 * (b + 1) * P])
+        second_list(2, first_terms[1][0])
+        multiply(0, banks[6])
+        multiply(1, banks[7])
+        for i in range(2):
+            combine(2, i, banks[1][:, 2 * i * P : 2 * (i + 1) * P])
+        for i in range(2):
+            scale_paired(3, i)
+        nc.scalar.copy(
+            z_both[2][:].rearrange("p (i j u) -> p i j u", i=2, u=2), banks[1][:].rearrange("p (i u j) -> p i j u", i=2, u=2)
+        )
+        store(0, banks[6], nc.scalar.copy)
+        second_list(3, first_terms[2][1])
+        store(1, banks[7], nc.scalar.copy)
+        multiply(2, banks[5])
+        for i in range(2):
+            bank = banks[3 + i]
             combine(3, i, bank[:, : 2 * P])
-            nc.scalar.copy(z_last[i][:].rearrange("p (j u) -> p j u", u=2), bank[:, : 2 * P].rearrange("p (u j) -> p j u", u=2))
-        store(2, banks[0], nc.vector.tensor_copy)
+            weave(z_last[i][:], bank[:, : 2 * P])
+        store(2, banks[5], nc.vector.tensor_copy)
         last = [quantise("last%d" % i, z_last[i][:], P) for i in range(2)]
-        targets = [banks[n][:, :P] for n in (1, 2, 6, 7)]
+        targets = [banks[n][:, :P] for n in (0, 1, 6, 7)]
         for i in range(2):
             for mt in range(4):
                 product(i, mt, last[i][0][:], last[i][1][:], targets[mt])

@@ -7,6 +7,7 @@ K, T, S, N, H = 512, 2048, 512, 512, 512
 P = 128
 PACK = 4
 BLOCKS = S // P
+HALF = S // 2
 FLOPS = 2 * K * H * S + 2 * 2 * H * N * S
 BYTES = K * T + 16 * T + 3 * 4 * K * H + 4 * 4 * S + 3 * 2 * P * (S // 16) + 4 * N * S
 
@@ -21,8 +22,7 @@ COPY = mybir.ActivationFunctionType.Copy
 MULT = mybir.AluOpType.mult
 ADD = mybir.AluOpType.add
 
-HALF = S // 2
-M_VECTOR = 40
+M_VECTOR = 48
 
 
 def tile_picked_kpconv2_none_p_kernel(
@@ -32,7 +32,7 @@ def tile_picked_kpconv2_none_p_kernel(
     with ExitStack() as ctx:
         keep = ctx.enter_context(tc.tile_pool(name="keep", bufs=1))
         psum = ctx.enter_context(tc.psum_pool(name="psum", bufs=1))
-        banks = [psum.tile([P, 512], F32, name="bank%d" % i) for i in range(8)]
+        banks = [psum.tile([P, 512], F32, name="bank%d" % n) for n in range(8)]
 
         def sb(name, shape, dtype):
             return keep.tile(shape, dtype, name=name, align_bytes=64)
@@ -43,29 +43,30 @@ def tile_picked_kpconv2_none_p_kernel(
         xw = sb("xw", [P, T], U32)
         xs = sb("xs", [P, T], U8)
         w1_raw = sb("w1_raw", [P, PACK, H], F32)
-        w_flat = [sb("w_flat%d" % i, [P, PACK * N], F32) for i in range(2)]
-        w_raw = [flat[:].rearrange("p (j c) -> p j c", j=PACK) for flat in w_flat]
+        w_raw = [sb("w_raw%d" % i, [P, PACK, N], F32) for i in range(2)]
         ident = sb("ident", [P, P], F32)
         k_rows = sb("k_rows", [P, P], F32)
         k_cols = sb("k_cols", [P, 4 * BLOCKS], F32)
 
-        nc.gpsimd.memset(xs[:].bitcast(I32), 0)
+        for n, k in enumerate((k11, k12, k21, k22)):
+            nc.gpsimd.dma_start(k_rows[8 * n : 8 * n + 8, :], k[0:2, :].rearrange("r (b q) -> (r b) q", b=BLOCKS))
+        nc.vector.memset(xs[:].bitcast(I32), 0)
+        nc.gpsimd.memset(k_rows[32:64, :], 0.0)
+        nc.gpsimd.memset(k_rows[64:128, :], 0.0)
+        make_identity(nc, ident[:])
+        by_rows = "(p j) c -> p j c"
         nc.sync.dma_start(offs_t[:], offs)
-        nc.sync.dma_start(p1_t[:], p1)
-        nc.sync.dma_start(p2_t[:], p2)
-        for i, k in enumerate((k11, k12, k21, k22)):
-            nc.scalar.dma_start(k_rows[32 * i : 32 * i + 32, :], k[0:8, :].rearrange("r (b q) -> (r b) q", b=BLOCKS))
-        nc.sync.dma_start(w1_raw[:], w1.rearrange("(p j) c -> p j c", j=PACK))
+        nc.sync.dma_start(w1_raw[:], w1.rearrange(by_rows, j=PACK))
         for q in range(4):
             nc.sync.dma_start(xs[32 * q : 32 * q + 4, :].bitcast(I32), x_scales[0, 4 * q : 4 * q + 4, :].bitcast(I32))
         nc.sync.dma_start(xw[:].bitcast(I32), x_words[0].rearrange("p n t -> p (n t)").bitcast(I32))
-        make_identity(nc, ident[:])
-        for i, w in enumerate((w2, w3)):
-            nc.sync.dma_start(w_flat[i][:], w.rearrange("(p j) c -> p (j c)", j=PACK))
+        nc.sync.dma_start(p1_t[:], p1)
+        nc.sync.dma_start(w_raw[0][:], w2.rearrange(by_rows, j=PACK))
+        nc.sync.dma_start(p2_t[:], p2)
+        nc.sync.dma_start(w_raw[1][:], w3.rearrange(by_rows, j=PACK))
 
         xs_g = sb("xs_g", [P, S], U8)
-        xw_g = sb("xw_g", [P, S], U32)
-
+        xw_g = [sb("xw_g%d" % h, [P, HALF], U32) for h in range(2)]
         w1_codes = sb("w1_codes", [P, H], U32)
         w1_scales = sb("w1_scales", [P, H], U8)
         w1_grouped = sb("w1_grouped", [P, H * PACK], BF16)
@@ -75,195 +76,167 @@ def tile_picked_kpconv2_none_p_kernel(
         nc.scalar.copy(dst[:, M_VECTOR:], src[:, M_VECTOR:])
         nc.vector.tensor_copy(xs_g[:], xs[:].indirect(offs_t[:]))
         nc.vector.quantize_mx(out=w1_codes[:].bitcast(FP8X4), scales=w1_scales[:], in_=w1_grouped[:])
-
         for h in range(2):
-            nc.vector.tensor_copy(xw_g[:, h * HALF : (h + 1) * HALF], xw[:].indirect(offs_t[:, 16 * h : 16 * h + 16]))
-
-        nc.tensor.transpose(banks[5][:, :P], k_rows[:], ident[:])
-        nc.scalar.copy(
-            k_cols[:].rearrange("q (i b) -> q i b", b=BLOCKS),
-            banks[5][:, :P].rearrange("q (i r) -> q i r", i=4)[:, :, :BLOCKS],
-        )
+            nc.vector.tensor_copy(xw_g[h][:], xw[:].indirect(offs_t[:, 16 * h : 16 * h + 16]))
 
         y = [sb("y%d" % t, [P, S], F32) for t in range(PACK)]
-        whole = slice(0, S)
-        steps = [(0, slice(0, HALF), 4), (0, slice(HALF, S), 5), (1, whole, 6), (2, whole, 7), (3, whole, 4)]
-        for t, cols, bank in steps:
-            width = cols.stop - cols.start
+
+        def first_product(t, h, bank, copy):
+            cols = slice(h * HALF, (h + 1) * HALF)
             nc.tensor.matmul_mx(
-                out=banks[bank][:, :width],
+                out=bank,
                 lhsT=w1_codes[:, t * P : (t + 1) * P].bitcast(FP8X4),
                 lhsT_scale=w1_scales[:, t * P : (t + 1) * P],
-                rhs=xw_g[:, cols].bitcast(FP8X4),
+                rhs=xw_g[h][:].bitcast(FP8X4),
                 rhs_scale=xs_g[:, cols],
                 start=True,
                 stop=True,
             )
-            nc.scalar.copy(y[t][:, cols], banks[bank][:, :width])
+            if copy is not None:
+                copy(y[t][:, cols], bank)
+
+        first_product(0, 0, banks[4][:, :HALF], nc.scalar.copy)
+        first_product(1, 0, banks[6][:, :HALF], nc.scalar.copy)
+        first_product(0, 1, banks[5][:, :HALF], nc.vector.tensor_copy)
+        first_product(1, 1, banks[7][:, :HALF], nc.scalar.copy)
+        for t in range(2, PACK):
+            for h in range(2):
+                first_product(t, h, banks[t][:, h * HALF : (h + 1) * HALF], None)
+            nc.scalar.copy(y[t][:], banks[t][:])
+
+        nc.tensor.transpose(banks[6][:, :P], k_rows[:], ident[:])
+        nc.scalar.copy(
+            k_cols[:].rearrange("q (n b) -> q n b", b=BLOCKS),
+            banks[6][:, :32].rearrange("q (n r) -> q n r", n=4)[:, :, :BLOCKS],
+        )
 
         w_codes = sb("w_codes", [P, 2 * N], U32)
         w_scales = sb("w_scales", [P, 2 * N], U8)
         w_grouped = sb("w_grouped", [P, 2 * N * PACK], BF16)
-        z_both = [sb("z_both%d" % b, [P, 4 * P], F32) for b in range(3)]
-        z_last = [sb("z_last%d" % i, [P, 2 * P], F32) for i in range(2)]
+
+        def round_weights(i, c0, c1):
+            nc.scalar.copy(
+                w_grouped[:, (i * N + c0) * PACK : (i * N + c1) * PACK].rearrange("p (c n j) -> p c j n", n=4, j=PACK),
+                w_raw[i][:, :, c0:c1].rearrange("p j (c n) -> p c j n", n=4),
+            )
 
         lists = (p1_t, p2_t)
-        first_terms = [
-            [w_flat[0][:, :H], w_flat[0][:, H : 2 * H]],
-            [sb("first1_%d" % i, [P, H], F32)[:] for i in range(2)],
-            [sb("first2_%d" % i, [P, H], F32)[:] for i in range(2)],
-            [z_both[0][:], sb("first3_1", [P, H], F32)[:]],
-        ]
-        turned_banks = [[banks[0], banks[2], banks[4], banks[5]], [banks[1], banks[3], banks[0], banks[2]]]
-
-        def gather(l, t, b0, nb, target):
-            nc.vector.tensor_copy(target, y[t][:].indirect(lists[l][:, 8 * b0 : 8 * (b0 + nb)]))
-
-        def turn(l, t, b, piece):
-            place = t // 2 + 2 * (t % 2)
-            nc.tensor.transpose(turned_banks[l][b][:, place * P : (place + 1) * P], piece, ident[:])
+        turned = [[banks[0], banks[1], banks[4], banks[5]], [banks[2], banks[3], banks[6], banks[7]]]
 
         def k_col(i, l, b):
             n = (2 * i + l) * BLOCKS + b
             return k_cols[:, n : n + 1]
 
-        def scale_paired(b, i):
-            turned = turned_banks[0][b][:].rearrange("q (e x) -> q x e", e=2)
-            nc.scalar.activation(first_terms[b][i].rearrange("q (x e) -> q x e", e=2), turned, COPY, scale=k_col(i, 0, b))
+        def look_up(l, b0, blocks, targets):
+            for t in range(PACK):
+                nc.vector.tensor_copy(targets[t], y[t][:].indirect(lists[l][:, 8 * b0 : 8 * (b0 + blocks)]))
+                place = t // 2 + 2 * (t % 2)
+                for c in range(blocks):
+                    nc.tensor.transpose(
+                        turned[l][b0 + c][:, place * P : (place + 1) * P], targets[t][:, c * P : (c + 1) * P], ident[:]
+                    )
 
-        def combine(b, i, target):
-            if b >= 2 and i == 0:
-                zt = z_both[b - 1][:, : 2 * P].bitcast(BF16)
-            else:
-                zt = sb("zt%d_%d" % (b, i), [P, H], BF16)[:]
-            nc.vector.scalar_tensor_tensor(
-                out=zt.rearrange("q (x e) -> q x e", e=2),
-                in0=turned_banks[1][b][:].rearrange("q (e x) -> q x e", e=2),
-                scalar=k_col(i, 1, b),
-                in1=first_terms[b][i].rearrange("q (x e) -> q x e", e=2),
-                op0=MULT,
-                op1=ADD,
-            )
-            words = zt.bitcast(F32)
-            for u in range(2):
-                nc.tensor.transpose(target[:, u * P : (u + 1) * P], words[:, u * P : (u + 1) * P], ident[:])
+        def fresh(name, count):
+            return [sb("%s_%d" % (name, t), [P, HALF], F32)[:] for t in range(count)]
 
-        def weave(target, source):
-            nc.scalar.copy(target.rearrange("p (j u) -> p j u", u=2), source.rearrange("p (u j) -> p j u", u=2))
+        def pairs(ap, order):
+            return ap.rearrange("q (%s) -> q x e" % order, e=2)
 
-        def sum_on_tensor(b, bank):
-            second = sb("second%d" % b, [P, H], F32)
-            nc.scalar.activation(second[:], turned_banks[1][b][:], COPY, scale=k_col(1, 1, b))
-            for place in range(PACK):
-                cols = slice(place * P, (place + 1) * P)
-                for n, term in enumerate((first_terms[b][1], second)):
-                    nc.tensor.matmul(bank[:, cols], term[:, cols], ident[:], start=(n == 0), stop=(n == 1), is_transpose=True)
-
-        def quantise(name, words, width):
+        def quantise(name, values, width):
             codes = sb(name + "_codes", [P, width], U32)
             scales = sb(name + "_scales", [P, width], U8)
-            nc.vector.quantize_mx(out=codes[:].bitcast(FP8X4), scales=scales[:], in_=words.bitcast(BF16))
+            nc.vector.quantize_mx(out=codes[:].bitcast(FP8X4), scales=scales[:], in_=values)
             return codes, scales
 
-        out_rows = out.rearrange("(mt p) j -> p mt j", p=P)
-
-        def product(i, mt, codes, scales, target):
+        def product(i, mt, codes, scales, target, start, stop):
             nc.tensor.matmul_mx(
                 out=target,
                 lhsT=w_codes[:, i * N + mt * P : i * N + (mt + 1) * P].bitcast(FP8X4),
                 lhsT_scale=w_scales[:, i * N + mt * P : i * N + (mt + 1) * P],
                 rhs=codes.bitcast(FP8X4),
                 rhs_scale=scales,
-                start=(i == 0),
-                stop=(i == 1),
+                start=start,
+                stop=stop,
             )
 
-        def multiply(b, bank):
-            codes, scales = quantise("z%d" % b, z_both[b][:], 2 * P)
-            for mt in range(4):
-                for i in range(2):
-                    cols = slice(i * P, (i + 1) * P)
-                    product(i, mt, codes[:, cols], scales[:, cols], bank[:, mt * P : (mt + 1) * P])
+        out_rows = out.rearrange("(mt p) j -> p mt j", p=P)
 
-        def store(b, bank, copy):
-            result = sb("result%d" % b, [P, 4, P], F32)
-            copy(result[:].rearrange("p mt j -> p (mt j)"), bank[:])
-            nc.sync.dma_start(out_rows[:, :, b * P : (b + 1) * P], result[:])
+        def store(name, bank, mt0, tiles, col0, width, copy, queue):
+            result = sb(name, [P, tiles, width], F32)
+            copy(result[:].rearrange("p mt j -> p (mt j)"), bank[:, : tiles * width])
+            queue.dma_start(out_rows[:, mt0 : mt0 + tiles, col0 : col0 + width], result[:])
 
-        def second_list(b, row):
-            for t in range(PACK):
-                piece = row[:, t * P : (t + 1) * P]
-                gather(1, t, b, 1, piece)
-                turn(1, t, b, piece)
+        firsts = {}
 
-        early = [[sb("early%d_%d" % (l, t), [P, HALF], F32) for t in range(PACK)] for l in range(2)]
-        for t in range(PACK):
-            for l in range(2):
-                gather(l, t, 0, 2, early[l][t][:])
-                for b in range(2):
-                    turn(l, t, b, early[l][t][:, b * P : (b + 1) * P])
-        nc.scalar.copy(
-            w_grouped[:, : N * PACK].rearrange("p (c i j) -> p c j i", i=4, j=PACK),
-            w_raw[0].rearrange("p j (c i) -> p c j i", i=4),
-        )
-        nc.gpsimd.tensor_scalar(
-            w_grouped[:, N * PACK :].rearrange("p (c j) -> p c j", j=PACK),
-            w_raw[1].rearrange("p j c -> p c j"),
-            1.0,
-            0.0,
-            MULT,
-            ADD,
-        )
-        for t in range(PACK):
-            late = w_flat[0][:, 2 * H + t * HALF : 2 * H + (t + 1) * HALF]
-            gather(0, t, 2, 2, late)
-            for b in range(2, 4):
-                turn(0, t, b, late[:, (b - 2) * P : (b - 1) * P])
-        nc.vector.quantize_mx(out=w_codes[:].bitcast(FP8X4), scales=w_scales[:], in_=w_grouped[:])
+        def first_terms(b, room):
+            for i in range(2):
+                firsts[b, i] = room[:, i * H : (i + 1) * H]
+                nc.scalar.activation(pairs(firsts[b, i], "x e"), pairs(turned[0][b][:], "e x"), COPY, scale=k_col(i, 0, b))
+
+        def combine(b, i, target):
+            zt = sb("zt%d_%d" % (b, i), [P, H], BF16)
+            nc.vector.scalar_tensor_tensor(
+                out=pairs(zt[:], "x e"),
+                in0=pairs(turned[1][b][:], "e x"),
+                scalar=k_col(i, 1, b),
+                in1=pairs(firsts[b, i], "x e"),
+                op0=MULT,
+                op1=ADD,
+            )
+            words = zt[:].bitcast(F32)
+            for u in range(2):
+                nc.tensor.transpose(target[:, u * P : (u + 1) * P], words[:, u * P : (u + 1) * P], ident[:])
+
+        g00 = fresh("g00", PACK)
+        look_up(0, 0, 2, g00)
+        round_weights(0, 0, N)
+        look_up(1, 0, 2, fresh("g10", PACK))
+        look_up(0, 2, 2, [w_raw[0][:, t, :HALF] for t in range(PACK)])
         for b in range(2):
-            scale_paired(b, 0)
-            nc.scalar.activation(first_terms[b][1], turned_banks[0][b][:], COPY, scale=k_col(1, 0, b))
+            first_terms(b, sb("firsts%d" % b, [P, 2 * H], F32)[:])
+        round_weights(1, 0, N)
+        z_early = sb("z_early", [P, 2 * HALF * 2], F32)
         for b in range(2):
-            sum_on_tensor(b, banks[6 + b])
-        for i in range(2):
-            scale_paired(2, i)
-        for b in range(2):
-            combine(b, 0, banks[4][:, 2 * b * P : 2 * (b + 1) * P])
-        for b in range(2):
+            for i in range(2):
+                combine(b, i, banks[6 + b][:, 2 * i * P : 2 * (i + 1) * P])
             nc.scalar.copy(
-                z_both[b][:, 2 * P :].bitcast(BF16).rearrange("p (j u e) -> p j u e", u=2, e=2),
-                banks[6 + b][:].rearrange("p (e u j) -> p j u e", e=2, u=2),
+                z_early[:].rearrange("p (i b j u) -> p b i j u", i=2, b=2, u=2)[:, b],
+                banks[6 + b][:].rearrange("p (i u j) -> p i j u", i=2, u=2),
             )
-            weave(z_both[b][:, : 2 * P], banks[4][:, 2 * b * P : 2 * (b + 1) * P])
-        second_list(2, first_terms[1][0])
-        multiply(0, banks[6])
-        multiply(1, banks[7])
-        for i in range(2):
-            combine(2, i, banks[1][:, 2 * i * P : 2 * (i + 1) * P])
-        for i in range(2):
-            scale_paired(3, i)
-        nc.scalar.copy(
-            z_both[2][:].rearrange("p (i j u) -> p i j u", i=2, u=2), banks[1][:].rearrange("p (i u j) -> p i j u", i=2, u=2)
-        )
-        store(0, banks[6], nc.scalar.copy)
-        second_list(3, first_terms[2][1])
-        store(1, banks[7], nc.scalar.copy)
-        multiply(2, banks[5])
-        for i in range(2):
-            bank = banks[3 + i]
-            combine(3, i, bank[:, : 2 * P])
-            weave(z_last[i][:], bank[:, : 2 * P])
-        store(2, banks[5], nc.vector.tensor_copy)
-        last = [quantise("last%d" % i, z_last[i][:], P) for i in range(2)]
-        targets = [banks[n][:, :P] for n in (0, 1, 6, 7)]
-        for i in range(2):
-            for mt in range(4):
-                product(i, mt, last[i][0][:], last[i][1][:], targets[mt])
+        nc.vector.quantize_mx(out=w_codes[:].bitcast(FP8X4), scales=w_scales[:], in_=w_grouped[:])
+        for b in range(2, 4):
+            first_terms(b, w_grouped[:].bitcast(F32)[:, (b - 2) * 2 * H : (b - 1) * 2 * H])
+        codes, scales = quantise("early", z_early[:].bitcast(BF16), 2 * HALF)
         for mt in range(4):
-            result = sb("result_last%d" % mt, [P, P], F32)
-            if mt % 2 == 0:
-                nc.vector.tensor_copy(result[:], targets[mt])
-                nc.sync.dma_start(out_rows[:, mt, 3 * P :], result[:])
-            else:
-                nc.scalar.copy(result[:], targets[mt])
-                nc.scalar.dma_start(out_rows[:, mt, 3 * P :], result[:])
+            for i in range(2):
+                cols = slice(i * HALF, (i + 1) * HALF)
+                target = banks[mt // 2][:, (mt % 2) * HALF : (mt % 2 + 1) * HALF]
+                product(i, mt, codes[:, cols], scales[:, cols], target, i == 0, i == 1)
+        for b, spent in ((2, w_raw[1][:, 0, :]), (3, z_early[:])):
+            look_up(1, b, 1, [spent[:, t * P : (t + 1) * P] for t in range(PACK)])
+
+        for half in range(2):
+            store("result_early%d" % half, banks[half], 2 * half, 2, 0, HALF, nc.scalar.copy, nc.sync)
+        for i in range(2):
+            combine(2, i, banks[2][:, 2 * i * P : 2 * (i + 1) * P])
+        z_third = sb("z_third", [P, 4 * P], F32)
+        nc.scalar.copy(
+            z_third[:].rearrange("p (i j u) -> p i j u", i=2, u=2), banks[2][:].rearrange("p (i u j) -> p i j u", i=2, u=2)
+        )
+        z_last = [sb("z_last%d" % i, [P, 2 * P], F32) for i in range(2)]
+        for i, bank in enumerate((banks[3], banks[4])):
+            combine(3, i, bank[:, : 2 * P])
+            nc.scalar.copy(z_last[i][:].rearrange("p (j u) -> p j u", u=2), bank[:, : 2 * P].rearrange("p (u j) -> p j u", u=2))
+        codes, scales = quantise("third", z_third[:].bitcast(BF16), 2 * P)
+        for mt in range(4):
+            for i in range(2):
+                cols = slice(i * P, (i + 1) * P)
+                product(i, mt, codes[:, cols], scales[:, cols], banks[5][:, mt * P : (mt + 1) * P], i == 0, i == 1)
+        store("result_third", banks[5], 0, 4, 2 * P, P, nc.scalar.copy, nc.sync)
+        for i in range(2):
+            codes, scales = quantise("last%d" % i, z_last[i][:].bitcast(BF16), P)
+            for mt in range(4):
+                target = banks[mt // 2][:, (mt % 2) * P : (mt % 2 + 1) * P]
+                product(i, mt, codes[:], scales[:], target, i == 0 and mt % 2 == 0, i == 1 and mt % 2 == 1)
+        store("result_last0", banks[0], 0, 2, 3 * P, P, nc.vector.tensor_copy, nc.sync)
+        store("result_last1", banks[1], 2, 2, 3 * P, P, nc.scalar.copy, nc.scalar)

@@ -112,13 +112,16 @@ def tile_picked_kpconv2_none_p_kernel(
 
         w_codes = sb("w_codes", [P, 2 * N], U32)
         w_scales = sb("w_scales", [P, 2 * N], U8)
-        w_grouped = sb("w_grouped", [P, 2 * N * PACK], BF16)
+        w_grouped = [sb("w_grouped%d" % i, [P, N * PACK], BF16) for i in range(2)]
 
-        def round_weights(i, c0, c1):
-            nc.scalar.copy(
-                w_grouped[:, (i * N + c0) * PACK : (i * N + c1) * PACK].rearrange("p (c n j) -> p c j n", n=4, j=PACK),
-                w_raw[i][:, :, c0:c1].rearrange("p j (c n) -> p c j n", n=4),
+        def round_weights(i):
+            nc.gpsimd.tensor_scalar(
+                w_grouped[i][:].rearrange("p (c j) -> p c j", j=PACK), w_raw[i][:].rearrange("p j c -> p c j"), 1.0, 0.0, MULT, ADD
             )
+
+        def quantise_weights(i):
+            cols = slice(i * N, (i + 1) * N)
+            nc.vector.quantize_mx(out=w_codes[:, cols].bitcast(FP8X4), scales=w_scales[:, cols], in_=w_grouped[i][:])
 
         lists = (p1_t, p2_t)
         turned = [[banks[0], banks[1], banks[4], banks[5]], [banks[2], banks[3], banks[6], banks[7]]]
@@ -189,12 +192,14 @@ def tile_picked_kpconv2_none_p_kernel(
 
         g00 = fresh("g00", PACK)
         look_up(0, 0, 2, g00)
-        round_weights(0, 0, N)
-        look_up(1, 0, 2, fresh("g10", PACK))
-        look_up(0, 2, 2, [w_raw[0][:, t, :HALF] for t in range(PACK)])
+        round_weights(0)
+        g10 = fresh("g10", PACK)
+        look_up(1, 0, 2, g10)
+        look_up(0, 2, 2, g10)
         for b in range(2):
             first_terms(b, sb("firsts%d" % b, [P, 2 * H], F32)[:])
-        round_weights(1, 0, N)
+        round_weights(1)
+        quantise_weights(0)
         z_early = sb("z_early", [P, 2 * HALF * 2], F32)
         for b in range(2):
             for i in range(2):
@@ -203,17 +208,17 @@ def tile_picked_kpconv2_none_p_kernel(
                 z_early[:].rearrange("p (i b j u) -> p b i j u", i=2, b=2, u=2)[:, b],
                 banks[6 + b][:].rearrange("p (i u j) -> p i j u", i=2, u=2),
             )
-        nc.vector.quantize_mx(out=w_codes[:].bitcast(FP8X4), scales=w_scales[:], in_=w_grouped[:])
-        for b in range(2, 4):
-            first_terms(b, w_grouped[:].bitcast(F32)[:, (b - 2) * 2 * H : (b - 1) * 2 * H])
+        first_terms(2, sb("firsts2", [P, 2 * H], F32)[:])
+        look_up(1, 2, 1, [firsts[1, 0][:, t * P : (t + 1) * P] for t in range(PACK)])
+        quantise_weights(1)
+        first_terms(3, w_grouped[1][:].bitcast(F32))
         codes, scales = quantise("early", z_early[:].bitcast(BF16), 2 * HALF)
         for mt in range(4):
             for i in range(2):
                 cols = slice(i * HALF, (i + 1) * HALF)
                 target = banks[mt // 2][:, (mt % 2) * HALF : (mt % 2 + 1) * HALF]
                 product(i, mt, codes[:, cols], scales[:, cols], target, i == 0, i == 1)
-        for b, spent in ((2, w_raw[1][:, 0, :]), (3, z_early[:])):
-            look_up(1, b, 1, [spent[:, t * P : (t + 1) * P] for t in range(PACK)])
+        look_up(1, 3, 1, [z_early[:, t * P : (t + 1) * P] for t in range(PACK)])
 
         for half in range(2):
             store("result_early%d" % half, banks[half], 2 * half, 2, 0, HALF, nc.scalar.copy, nc.sync)

@@ -34,8 +34,8 @@ def tile_picked_kpconv2_none_p_kernel(
         psum = ctx.enter_context(tc.psum_pool(name="psum", bufs=1))
         banks = [psum.tile([P, 512], F32, name="bank%d" % n) for n in range(8)]
 
-        def sb(name, shape, dtype):
-            return keep.tile(shape, dtype, name=name, align_bytes=64)
+        def sb(name, shape, dtype, tag=None):
+            return keep.tile(shape, dtype, name=name, tag=tag or name, align_bytes=64)
 
         offs_t = sb("offs_t", [P, S // 16], U16)
         p1_t = sb("p1_t", [P, S // 16], U16)
@@ -57,12 +57,12 @@ def tile_picked_kpconv2_none_p_kernel(
         by_rows = "(p j) c -> p j c"
         nc.sync.dma_start(offs_t[:], offs)
         nc.sync.dma_start(w1_raw[:], w1.rearrange(by_rows, j=PACK))
+        nc.sync.dma_start(p2_t[:], p2)
         for q in range(4):
             nc.sync.dma_start(xs[32 * q : 32 * q + 4, :].bitcast(I32), x_scales[0, 4 * q : 4 * q + 4, :].bitcast(I32))
         nc.sync.dma_start(xw[:].bitcast(I32), x_words[0].rearrange("p n t -> p (n t)").bitcast(I32))
         nc.sync.dma_start(p1_t[:], p1)
         nc.sync.dma_start(w_raw[0][:], w2.rearrange(by_rows, j=PACK))
-        nc.sync.dma_start(p2_t[:], p2)
         nc.sync.dma_start(w_raw[1][:], w3.rearrange(by_rows, j=PACK))
 
         xs_g = sb("xs_g", [P, S], U8)
@@ -104,24 +104,25 @@ def tile_picked_kpconv2_none_p_kernel(
                 first_product(t, h, banks[t][:, h * HALF : (h + 1) * HALF], None)
             nc.scalar.copy(y[t][:], banks[t][:])
 
-        nc.tensor.transpose(banks[6][:, :P], k_rows[:], ident[:])
+        nc.tensor.transpose(banks[3][:, :P], k_rows[:], ident[:])
         nc.scalar.copy(
             k_cols[:].rearrange("q (n b) -> q n b", b=BLOCKS),
-            banks[6][:, :32].rearrange("q (n r) -> q n r", n=4)[:, :, :BLOCKS],
+            banks[3][:, :32].rearrange("q (n r) -> q n r", n=4)[:, :, :BLOCKS],
         )
 
         w_codes = sb("w_codes", [P, 2 * N], U32)
         w_scales = sb("w_scales", [P, 2 * N], U8)
-        w_grouped = [sb("w_grouped%d" % i, [P, N * PACK], BF16) for i in range(2)]
+        w_grouped = sb("w_grouped", [P, 2 * N * PACK], BF16)
 
         def round_weights(i):
             nc.gpsimd.tensor_scalar(
-                w_grouped[i][:].rearrange("p (c j) -> p c j", j=PACK), w_raw[i][:].rearrange("p j c -> p c j"), 1.0, 0.0, MULT, ADD
+                w_grouped[:, i * N * PACK : (i + 1) * N * PACK].rearrange("p (c j) -> p c j", j=PACK),
+                w_raw[i][:].rearrange("p j c -> p c j"),
+                1.0,
+                0.0,
+                MULT,
+                ADD,
             )
-
-        def quantise_weights(i):
-            cols = slice(i * N, (i + 1) * N)
-            nc.vector.quantize_mx(out=w_codes[:, cols].bitcast(FP8X4), scales=w_scales[:, cols], in_=w_grouped[i][:])
 
         lists = (p1_t, p2_t)
         turned = [[banks[0], banks[1], banks[4], banks[5]], [banks[2], banks[3], banks[6], banks[7]]]
@@ -138,9 +139,6 @@ def tile_picked_kpconv2_none_p_kernel(
                     nc.tensor.transpose(
                         turned[l][b0 + c][:, place * P : (place + 1) * P], targets[t][:, c * P : (c + 1) * P], ident[:]
                     )
-
-        def fresh(name, count):
-            return [sb("%s_%d" % (name, t), [P, HALF], F32)[:] for t in range(count)]
 
         def pairs(ap, order):
             return ap.rearrange("q (%s) -> q x e" % order, e=2)
@@ -169,79 +167,96 @@ def tile_picked_kpconv2_none_p_kernel(
             copy(result[:].rearrange("p mt j -> p (mt j)"), bank[:, : tiles * width])
             queue.dma_start(out_rows[:, mt0 : mt0 + tiles, col0 : col0 + width], result[:])
 
-        firsts = {}
+        terms = {}
 
-        def first_terms(b, room):
-            for i in range(2):
-                firsts[b, i] = room[:, i * H : (i + 1) * H]
-                nc.scalar.activation(pairs(firsts[b, i], "x e"), pairs(turned[0][b][:], "e x"), COPY, scale=k_col(i, 0, b))
+        def scale(l, b, i, target):
+            terms[l, b, i] = target
+            nc.scalar.activation(pairs(target, "x e"), pairs(turned[l][b][:], "e x"), COPY, scale=k_col(i, l, b))
 
-        def combine(b, i, target):
-            zt = sb("zt%d_%d" % (b, i), [P, H], BF16)
-            nc.vector.scalar_tensor_tensor(
-                out=pairs(zt[:], "x e"),
-                in0=pairs(turned[1][b][:], "e x"),
-                scalar=k_col(i, 1, b),
-                in1=pairs(firsts[b, i], "x e"),
-                op0=MULT,
-                op1=ADD,
-            )
-            words = zt[:].bitcast(F32)
+        def turn_back(zt, target):
+            words = zt.bitcast(F32)
             for u in range(2):
                 nc.tensor.transpose(target[:, u * P : (u + 1) * P], words[:, u * P : (u + 1) * P], ident[:])
 
-        g00 = fresh("g00", PACK)
-        look_up(0, 0, 2, g00)
-        round_weights(0)
-        g10 = fresh("g10", PACK)
-        look_up(1, 0, 2, g10)
-        look_up(0, 2, 2, g10)
-        for b in range(2):
-            first_terms(b, sb("firsts%d" % b, [P, 2 * H], F32)[:])
-        round_weights(1)
-        quantise_weights(0)
-        z_early = sb("z_early", [P, 2 * HALF * 2], F32)
-        for b in range(2):
-            for i in range(2):
-                combine(b, i, banks[6 + b][:, 2 * i * P : 2 * (i + 1) * P])
-            nc.scalar.copy(
-                z_early[:].rearrange("p (i b j u) -> p b i j u", i=2, b=2, u=2)[:, b],
-                banks[6 + b][:].rearrange("p (i u j) -> p i j u", i=2, u=2),
-            )
-        first_terms(2, sb("firsts2", [P, 2 * H], F32)[:])
-        look_up(1, 2, 1, [firsts[1, 0][:, t * P : (t + 1) * P] for t in range(PACK)])
-        quantise_weights(1)
-        first_terms(3, w_grouped[1][:].bitcast(F32))
-        codes, scales = quantise("early", z_early[:].bitcast(BF16), 2 * HALF)
-        for mt in range(4):
-            for i in range(2):
-                cols = slice(i * HALF, (i + 1) * HALF)
-                target = banks[mt // 2][:, (mt % 2) * HALF : (mt % 2 + 1) * HALF]
-                product(i, mt, codes[:, cols], scales[:, cols], target, i == 0, i == 1)
-        look_up(1, 3, 1, [z_early[:, t * P : (t + 1) * P] for t in range(PACK)])
+        def add_terms(b, i, zt):
+            nc.gpsimd.tensor_tensor(zt, terms[0, b, i], terms[1, b, i], ADD)
+            turn_back(zt, banks[b][:, 2 * i * P : 2 * (i + 1) * P])
 
-        for half in range(2):
-            store("result_early%d" % half, banks[half], 2 * half, 2, 0, HALF, nc.scalar.copy, nc.sync)
-        for i in range(2):
-            combine(2, i, banks[2][:, 2 * i * P : 2 * (i + 1) * P])
-        z_third = sb("z_third", [P, 4 * P], F32)
-        nc.scalar.copy(
-            z_third[:].rearrange("p (i j u) -> p i j u", i=2, u=2), banks[2][:].rearrange("p (i u j) -> p i j u", i=2, u=2)
-        )
-        z_last = [sb("z_last%d" % i, [P, 2 * P], F32) for i in range(2)]
-        for i, bank in enumerate((banks[3], banks[4])):
-            combine(3, i, bank[:, : 2 * P])
-            nc.scalar.copy(z_last[i][:].rearrange("p (j u) -> p j u", u=2), bank[:, : 2 * P].rearrange("p (u j) -> p j u", u=2))
-        codes, scales = quantise("third", z_third[:].bitcast(BF16), 2 * P)
-        for mt in range(4):
-            for i in range(2):
-                cols = slice(i * P, (i + 1) * P)
-                product(i, mt, codes[:, cols], scales[:, cols], banks[5][:, mt * P : (mt + 1) * P], i == 0, i == 1)
-        store("result_third", banks[5], 0, 4, 2 * P, P, nc.scalar.copy, nc.sync)
-        for i in range(2):
-            codes, scales = quantise("last%d" % i, z_last[i][:].bitcast(BF16), P)
+        def combine(b, i, target):
+            zt = sb("zt%d_%d" % (b, i), [P, H], BF16)[:]
+            nc.vector.scalar_tensor_tensor(
+                out=pairs(zt, "x e"),
+                in0=pairs(turned[1][b][:], "e x"),
+                scalar=k_col(i, 1, b),
+                in1=pairs(terms[0, b, i], "x e"),
+                op0=MULT,
+                op1=ADD,
+            )
+            turn_back(zt, target)
+
+        def weave(name, bank, points):
+            z = sb(name, [P, points * 2 * P], F32)
+            nc.scalar.copy(
+                z[:].rearrange("p (i j u) -> p i j u", i=points, u=2),
+                bank[:, : points * 2 * P].rearrange("p (i u j) -> p i j u", i=points, u=2),
+            )
+            return z[:].bitcast(BF16)
+
+        def multiply(b, z, bank):
+            codes, scales = quantise("z%d" % b, z, 2 * P)
             for mt in range(4):
-                target = banks[mt // 2][:, (mt % 2) * P : (mt % 2 + 1) * P]
+                for i in range(2):
+                    cols = slice(i * P, (i + 1) * P)
+                    product(i, mt, codes[:, cols], scales[:, cols], bank[:, mt * P : (mt + 1) * P], i == 0, i == 1)
+
+        def look_up_both(b, room):
+            for t in range(PACK):
+                for l in range(2):
+                    piece = room[:, (2 * t + l) * P : (2 * t + l + 1) * P]
+                    nc.vector.tensor_copy(piece, y[t][:].indirect(lists[l][:, 8 * b : 8 * (b + 1)]))
+                    place = t // 2 + 2 * (t % 2)
+                    nc.tensor.transpose(turned[l][b][:, place * P : (place + 1) * P], piece, ident[:])
+
+        look_up_both(0, sb("g_block0", [P, 2 * H], F32))
+        g_block1 = sb("g_block1", [P, 2 * H], F32, tag="k_rows")
+        look_up_both(1, g_block1)
+        look_up(0, 2, 2, [g_block1[:, t * HALF : (t + 1) * HALF] for t in range(PACK)])
+        for i in range(2):
+            round_weights(i)
+        for b in range(2):
+            for i in range(2):
+                for l in range(2):
+                    scale(l, b, i, sb("term%d_%d_%d" % (l, b, i), [P, H], F32)[:])
+        nc.vector.quantize_mx(out=w_codes[:].bitcast(FP8X4), scales=w_scales[:], in_=w_grouped[:])
+
+        for b in range(2):
+            for i in range(2):
+                add_terms(b, i, w_raw[1][:, 2 * b + i, : H // 2].bitcast(BF16))
+        spent = w_grouped[:].bitcast(F32)
+        for b in range(2, 4):
+            look_up(1, b, 1, [spent[:, (b * PACK + t) * P : (b * PACK + t + 1) * P] for t in range(PACK)])
+        for b in range(2, 4):
+            for i in range(2):
+                scale(0, b, i, sb("term0_%d_%d" % (b, i), [P, H], F32)[:])
+        multiply(0, weave("z0", banks[0], 2), banks[2])
+        for i in range(2):
+            combine(2, i, banks[0][:, 2 * i * P : 2 * (i + 1) * P])
+        store("result0", banks[2], 0, 4, 0, P, nc.scalar.copy, nc.sync)
+        multiply(1, weave("z1", banks[1], 2), banks[3])
+        z2 = weave("z2", banks[0], 2)
+        z3 = []
+        for i in range(2):
+            combine(3, i, banks[4 + i][:, : 2 * P])
+            if i == 0:
+                multiply(2, z2, banks[6])
+                store("result1", banks[3], 0, 4, P, P, nc.scalar.copy, nc.sync)
+            z3.append(weave("z3_%d" % i, banks[4 + i], 1))
+        store("result2", banks[6], 0, 4, 2 * P, P, nc.vector.tensor_copy, nc.sync)
+        last_banks = (banks[1], banks[2])
+        for i in range(2):
+            codes, scales = quantise("last%d" % i, z3[i], P)
+            for mt in range(4):
+                target = last_banks[mt // 2][:, (mt % 2) * P : (mt % 2 + 1) * P]
                 product(i, mt, codes[:], scales[:], target, i == 0 and mt % 2 == 0, i == 1 and mt % 2 == 1)
-        store("result_last0", banks[0], 0, 2, 3 * P, P, nc.vector.tensor_copy, nc.sync)
-        store("result_last1", banks[1], 2, 2, 3 * P, P, nc.scalar.copy, nc.scalar)
+        store("result_last0", last_banks[0], 0, 2, 3 * P, P, nc.vector.tensor_copy, nc.sync)
+        store("result_last1", last_banks[1], 2, 2, 3 * P, P, nc.scalar.copy, nc.scalar)

@@ -23,6 +23,7 @@ MULT = mybir.AluOpType.mult
 ADD = mybir.AluOpType.add
 
 M_VECTOR = 48
+W2_GPSIMD = 320
 
 
 def tile_picked_kpconv2_none_p_kernel(
@@ -43,7 +44,8 @@ def tile_picked_kpconv2_none_p_kernel(
         xw = sb("xw", [P, T], U32)
         xs = sb("xs", [P, T], U8)
         w1_raw = sb("w1_raw", [P, PACK, H], F32)
-        w_raw = [sb("w_raw%d" % i, [P, PACK, N], F32) for i in range(2)]
+        w2_raw = sb("w2_raw", [P, PACK, N], F32)
+        w3_raw = [sb("w3_raw%d" % h, [P, PACK, N // 2], F32) for h in range(2)]
         ident = sb("ident", [P, P], F32)
         k_rows = sb("k_rows", [P, P], F32)
         k_cols = sb("k_cols", [P, 4 * BLOCKS], F32)
@@ -62,8 +64,9 @@ def tile_picked_kpconv2_none_p_kernel(
             nc.sync.dma_start(xs[32 * q : 32 * q + 4, :].bitcast(I32), x_scales[0, 4 * q : 4 * q + 4, :].bitcast(I32))
         nc.sync.dma_start(xw[:].bitcast(I32), x_words[0].rearrange("p n t -> p (n t)").bitcast(I32))
         nc.sync.dma_start(p1_t[:], p1)
-        nc.sync.dma_start(w_raw[0][:], w2.rearrange(by_rows, j=PACK))
-        nc.sync.dma_start(w_raw[1][:], w3.rearrange(by_rows, j=PACK))
+        nc.sync.dma_start(w2_raw[:], w2.rearrange(by_rows, j=PACK))
+        for h in range(2):
+            nc.sync.dma_start(w3_raw[h][:], w3.rearrange(by_rows, j=PACK)[:, :, h * N // 2 : (h + 1) * N // 2])
 
         xs_g = sb("xs_g", [P, S], U8)
         xw_g = [sb("xw_g%d" % h, [P, HALF], U32) for h in range(2)]
@@ -114,10 +117,10 @@ def tile_picked_kpconv2_none_p_kernel(
         w_scales = sb("w_scales", [P, 2 * N], U8)
         w_grouped = sb("w_grouped", [P, 2 * N * PACK], BF16)
 
-        def round_weights(i):
+        def round_on_gpsimd(first, raw):
             nc.gpsimd.tensor_scalar(
-                w_grouped[:, i * N * PACK : (i + 1) * N * PACK].rearrange("p (c j) -> p c j", j=PACK),
-                w_raw[i][:].rearrange("p j c -> p c j"),
+                w_grouped[:, first * PACK : (first + raw.shape[2]) * PACK].rearrange("p (c j) -> p c j", j=PACK),
+                raw.rearrange("p j c -> p c j"),
                 1.0,
                 0.0,
                 MULT,
@@ -125,7 +128,7 @@ def tile_picked_kpconv2_none_p_kernel(
             )
 
         lists = (p1_t, p2_t)
-        turned = [[banks[0], banks[1], banks[4], banks[5]], [banks[2], banks[3], banks[6], banks[7]]]
+        turned = [[banks[0], banks[1], banks[4], banks[5]], [banks[2], banks[3], banks[0], banks[1]]]
 
         def k_col(i, l, b):
             n = (2 * i + l) * BLOCKS + b
@@ -178,12 +181,13 @@ def tile_picked_kpconv2_none_p_kernel(
             for u in range(2):
                 nc.tensor.transpose(target[:, u * P : (u + 1) * P], words[:, u * P : (u + 1) * P], ident[:])
 
-        def add_terms(b, i, zt):
+        def add_terms(b, i, room):
+            zt = room[:, : H // 2].bitcast(BF16)
             nc.gpsimd.tensor_tensor(zt, terms[0, b, i], terms[1, b, i], ADD)
             turn_back(zt, banks[b][:, 2 * i * P : 2 * (i + 1) * P])
 
-        def combine(b, i, target):
-            zt = sb("zt%d_%d" % (b, i), [P, H], BF16)[:]
+        def combine(b, i, room, target):
+            zt = room[:, : H // 2].bitcast(BF16)
             nc.vector.scalar_tensor_tensor(
                 out=pairs(zt, "x e"),
                 in0=pairs(turned[1][b][:], "e x"),
@@ -194,13 +198,12 @@ def tile_picked_kpconv2_none_p_kernel(
             )
             turn_back(zt, target)
 
-        def weave(name, bank, points):
-            z = sb(name, [P, points * 2 * P], F32)
+        def weave(z, bank, sums):
             nc.scalar.copy(
-                z[:].rearrange("p (i j u) -> p i j u", i=points, u=2),
-                bank[:, : points * 2 * P].rearrange("p (i u j) -> p i j u", i=points, u=2),
+                z.rearrange("p (i j u) -> p i j u", i=sums, u=2),
+                bank[:, : sums * 2 * P].rearrange("p (i u j) -> p i j u", i=sums, u=2),
             )
-            return z[:].bitcast(BF16)
+            return z.bitcast(BF16)
 
         def multiply(b, z, bank):
             codes, scales = quantise("z%d" % b, z, 2 * P)
@@ -217,42 +220,51 @@ def tile_picked_kpconv2_none_p_kernel(
                     place = t // 2 + 2 * (t % 2)
                     nc.tensor.transpose(turned[l][b][:, place * P : (place + 1) * P], piece, ident[:])
 
-        look_up_both(0, sb("g_block0", [P, 2 * H], F32))
+        g_block0 = sb("g_block0", [P, 2 * H], F32)
         g_block1 = sb("g_block1", [P, 2 * H], F32, tag="k_rows")
+        look_up_both(0, g_block0)
         look_up_both(1, g_block1)
         look_up(0, 2, 2, [g_block1[:, t * HALF : (t + 1) * HALF] for t in range(PACK)])
-        for i in range(2):
-            round_weights(i)
+        round_on_gpsimd(0, w2_raw[:, :, :W2_GPSIMD])
+        nc.scalar.copy(
+            w_grouped[:, W2_GPSIMD * PACK : N * PACK].rearrange("p (c n j) -> p c j n", n=4, j=PACK),
+            w2_raw[:, :, W2_GPSIMD:].rearrange("p j (c n) -> p c j n", n=4),
+        )
+        for h in range(2):
+            round_on_gpsimd(N + h * N // 2, w3_raw[h][:])
         for b in range(2):
             for i in range(2):
                 for l in range(2):
                     scale(l, b, i, sb("term%d_%d_%d" % (l, b, i), [P, H], F32)[:])
         nc.vector.quantize_mx(out=w_codes[:].bitcast(FP8X4), scales=w_scales[:], in_=w_grouped[:])
 
-        for b in range(2):
-            for i in range(2):
-                add_terms(b, i, w_raw[1][:, 2 * b + i, : H // 2].bitcast(BF16))
-        spent = w_grouped[:].bitcast(F32)
-        for b in range(2, 4):
-            look_up(1, b, 1, [spent[:, (b * PACK + t) * P : (b * PACK + t + 1) * P] for t in range(PACK)])
-        for b in range(2, 4):
-            for i in range(2):
-                scale(0, b, i, sb("term0_%d_%d" % (b, i), [P, H], F32)[:])
-        multiply(0, weave("z0", banks[0], 2), banks[2])
         for i in range(2):
-            combine(2, i, banks[0][:, 2 * i * P : 2 * (i + 1) * P])
+            add_terms(0, i, w3_raw[1][:, i, :])
+        for i in range(2):
+            add_terms(1, i, terms[0, 0, i])
+        z0 = weave(sb("z0", [P, H], F32)[:], banks[0], 2)
+        look_up(1, 2, 1, [g_block1[:, 2 * t * P : (2 * t + 1) * P] for t in range(PACK)])
+        early = sb("early", [P, 2 * H], F32, tag="w3_raw1")
+        for i in range(2):
+            scale(0, 2, i, early[:, i * H : (i + 1) * H])
+        z1 = weave(sb("z1", [P, H], F32)[:], banks[1], 2)
+        look_up(1, 3, 1, [g_block1[:, (2 * t + 1) * P : (2 * t + 2) * P] for t in range(PACK)])
+        late = sb("late", [P, 2 * H], F32, tag="term0_0_1")
+        for i in range(2):
+            scale(0, 3, i, late[:, i * H : (i + 1) * H])
+        multiply(0, z0, banks[2])
+        multiply(1, z1, banks[3])
+        for i in range(2):
+            combine(2, i, z1.bitcast(F32)[:, i * HALF :], banks[6][:, 2 * i * P : 2 * (i + 1) * P])
+        for i in range(2):
+            combine(3, i, sb("zt3_%d" % i, [P, HALF], F32)[:], banks[(7, 4)[i]][:, : 2 * P])
         store("result0", banks[2], 0, 4, 0, P, nc.scalar.copy, nc.sync)
-        multiply(1, weave("z1", banks[1], 2), banks[3])
-        z2 = weave("z2", banks[0], 2)
-        z3 = []
-        for i in range(2):
-            combine(3, i, banks[4 + i][:, : 2 * P])
-            if i == 0:
-                multiply(2, z2, banks[6])
-                store("result1", banks[3], 0, 4, P, P, nc.scalar.copy, nc.sync)
-            z3.append(weave("z3_%d" % i, banks[4 + i], 1))
-        store("result2", banks[6], 0, 4, 2 * P, P, nc.vector.tensor_copy, nc.sync)
-        last_banks = (banks[1], banks[2])
+        store("result1", banks[3], 0, 4, P, P, nc.vector.tensor_copy, nc.sync)
+        z2 = weave(sb("z2", [P, H], F32)[:], banks[6], 2)
+        z3 = [weave(sb("z3_%d" % i, [P, HALF], F32)[:], banks[(7, 4)[i]], 1) for i in range(2)]
+        multiply(2, z2, banks[5])
+        store("result2", banks[5], 0, 4, 2 * P, P, nc.scalar.copy, nc.sync)
+        last_banks = (banks[0], banks[1])
         for i in range(2):
             codes, scales = quantise("last%d" % i, z3[i], P)
             for mt in range(4):

@@ -113,7 +113,6 @@ def tile_picked_kpconv2_none_p_kernel(
             banks[3][:, :32].rearrange("q (n r) -> q n r", n=4)[:, :, :BLOCKS],
         )
 
-        w_codes = sb("w_codes", [P, 2 * N], U32)
         w_scales = sb("w_scales", [P, 2 * N], U8)
         w_grouped = sb("w_grouped", [P, 2 * N * PACK], BF16)
 
@@ -146,8 +145,8 @@ def tile_picked_kpconv2_none_p_kernel(
         def pairs(ap, order):
             return ap.rearrange("q (%s) -> q x e" % order, e=2)
 
-        def quantise(name, values, width):
-            codes = sb(name + "_codes", [P, width], U32)
+        def quantise(name, values, width, tag=None):
+            codes = sb(name + "_codes", [P, width], U32, tag=tag)
             scales = sb(name + "_scales", [P, width], U8)
             nc.vector.quantize_mx(out=codes[:].bitcast(FP8X4), scales=scales[:], in_=values)
             return codes, scales
@@ -205,8 +204,8 @@ def tile_picked_kpconv2_none_p_kernel(
             )
             return z.bitcast(BF16)
 
-        def multiply(b, z, bank):
-            codes, scales = quantise("z%d" % b, z, 2 * P)
+        def multiply(b, z, bank, tag=None):
+            codes, scales = quantise("z%d" % b, z, 2 * P, tag)
             for mt in range(4):
                 for i in range(2):
                     cols = slice(i * P, (i + 1) * P)
@@ -236,12 +235,12 @@ def tile_picked_kpconv2_none_p_kernel(
             for i in range(2):
                 for l in range(2):
                     scale(l, b, i, sb("term%d_%d_%d" % (l, b, i), [P, H], F32)[:])
-        nc.vector.quantize_mx(out=w_codes[:].bitcast(FP8X4), scales=w_scales[:], in_=w_grouped[:])
-
         for i in range(2):
             add_terms(0, i, w3_raw[1][:, i, :])
         for i in range(2):
             add_terms(1, i, terms[0, 0, i])
+        w_codes = sb("w_codes", [P, 2 * N], U32, tag="term1_1_1")
+        nc.vector.quantize_mx(out=w_codes[:].bitcast(FP8X4), scales=w_scales[:], in_=w_grouped[:])
         z0 = weave(sb("z0", [P, H], F32)[:], banks[0], 2)
         look_up(1, 2, 1, [g_block1[:, 2 * t * P : (2 * t + 1) * P] for t in range(PACK)])
         early = sb("early", [P, 2 * H], F32, tag="w3_raw1")
@@ -249,13 +248,13 @@ def tile_picked_kpconv2_none_p_kernel(
             scale(0, 2, i, early[:, i * H : (i + 1) * H])
         z1 = weave(sb("z1", [P, H], F32)[:], banks[1], 2)
         look_up(1, 3, 1, [g_block1[:, (2 * t + 1) * P : (2 * t + 2) * P] for t in range(PACK)])
-        late = sb("late", [P, 2 * H], F32, tag="term0_0_1")
+        late = sb("late", [P, 3 * H], F32, tag="term0_0_1")
         for i in range(2):
             scale(0, 3, i, late[:, i * H : (i + 1) * H])
-        multiply(0, z0, banks[2])
-        multiply(1, z1, banks[3])
+        multiply(0, z0, banks[2], tag="term0_1_1")
         for i in range(2):
-            combine(2, i, z1.bitcast(F32)[:, i * HALF :], banks[6][:, 2 * i * P : 2 * (i + 1) * P])
+            combine(2, i, late[:, 2 * H + i * HALF :], banks[6][:, 2 * i * P : 2 * (i + 1) * P])
+        multiply(1, z1, banks[3])
         for i in range(2):
             combine(3, i, sb("zt3_%d" % i, [P, HALF], F32)[:], banks[(7, 4)[i]][:, : 2 * P])
         store("result0", banks[2], 0, 4, 0, P, nc.scalar.copy, nc.sync)

@@ -23,7 +23,7 @@ MULT = mybir.AluOpType.mult
 ADD = mybir.AluOpType.add
 
 M_VECTOR = 48
-W2_GPSIMD = 320
+W2_GPSIMD = 384
 
 
 def tile_picked_kpconv2_none_p_kernel(
@@ -60,8 +60,8 @@ def tile_picked_kpconv2_none_p_kernel(
         nc.sync.dma_start(offs_t[:], offs)
         nc.sync.dma_start(w1_raw[:], w1.rearrange(by_rows, j=PACK))
         nc.sync.dma_start(p2_t[:], p2)
-        for q in range(4):
-            nc.sync.dma_start(xs[32 * q : 32 * q + 4, :].bitcast(I32), x_scales[0, 4 * q : 4 * q + 4, :].bitcast(I32))
+        for r in range(4):
+            nc.sync.dma_start(xs[r:P:32, :].bitcast(I32), x_scales[0, r:16:4, :].bitcast(I32))
         nc.sync.dma_start(xw[:].bitcast(I32), x_words[0].rearrange("p n t -> p (n t)").bitcast(I32))
         nc.sync.dma_start(p1_t[:], p1)
         nc.sync.dma_start(w2_raw[:], w2.rearrange(by_rows, j=PACK))
@@ -142,6 +142,15 @@ def tile_picked_kpconv2_none_p_kernel(
                         turned[l][b0 + c][:, place * P : (place + 1) * P], targets[t][:, c * P : (c + 1) * P], ident[:]
                     )
 
+        def gather(l, b0, blocks, targets):
+            for t in range(PACK):
+                nc.vector.tensor_copy(targets[t], y[t][:].indirect(lists[l][:, 8 * b0 : 8 * (b0 + blocks)]))
+
+        def turn(l, b, pieces):
+            for t in range(PACK):
+                place = t // 2 + 2 * (t % 2)
+                nc.tensor.transpose(turned[l][b][:, place * P : (place + 1) * P], pieces[t], ident[:])
+
         def pairs(ap, order):
             return ap.rearrange("q (%s) -> q x e" % order, e=2)
 
@@ -197,19 +206,22 @@ def tile_picked_kpconv2_none_p_kernel(
             )
             turn_back(zt, target)
 
-        def weave(z, bank, sums):
-            nc.scalar.copy(
+        def weave(z, bank, sums, copy=nc.scalar.copy):
+            copy(
                 z.rearrange("p (i j u) -> p i j u", i=sums, u=2),
                 bank[:, : sums * 2 * P].rearrange("p (i u j) -> p i j u", i=sums, u=2),
             )
             return z.bitcast(BF16)
 
-        def multiply(b, z, bank, tag=None):
-            codes, scales = quantise("z%d" % b, z, 2 * P, tag)
-            for mt in range(4):
-                for i in range(2):
-                    cols = slice(i * P, (i + 1) * P)
-                    product(i, mt, codes[:, cols], scales[:, cols], bank[:, mt * P : (mt + 1) * P], i == 0, i == 1)
+        def multiply(planes, targets):
+            codes, scales = planes
+            per_bank = 4 // len(targets)
+            for i in range(2):
+                cols = slice(i * P, (i + 1) * P)
+                for mt in range(4):
+                    place = mt % per_bank
+                    target = targets[mt // per_bank][:, place * P : (place + 1) * P]
+                    product(i, mt, codes[:, cols], scales[:, cols], target, i == 0 and place == 0, i == 1 and place == per_bank - 1)
 
         def look_up_both(b, room):
             for t in range(PACK):
@@ -239,35 +251,42 @@ def tile_picked_kpconv2_none_p_kernel(
             add_terms(0, i, w3_raw[1][:, i, :])
         for i in range(2):
             add_terms(1, i, terms[0, 0, i])
-        w_codes = sb("w_codes", [P, 2 * N], U32, tag="term1_1_1")
-        nc.vector.quantize_mx(out=w_codes[:].bitcast(FP8X4), scales=w_scales[:], in_=w_grouped[:])
         z0 = weave(sb("z0", [P, H], F32)[:], banks[0], 2)
-        look_up(1, 2, 1, [g_block1[:, 2 * t * P : (2 * t + 1) * P] for t in range(PACK)])
+        second = [g_block1[:, t * HALF : (t + 1) * HALF] for t in range(PACK)]
+        gather(1, 2, 2, second)
+        turn(1, 2, [piece[:, :P] for piece in second])
         early = sb("early", [P, 2 * H], F32, tag="w3_raw1")
         for i in range(2):
             scale(0, 2, i, early[:, i * H : (i + 1) * H])
         z1 = weave(sb("z1", [P, H], F32)[:], banks[1], 2)
-        look_up(1, 3, 1, [g_block1[:, (2 * t + 1) * P : (2 * t + 2) * P] for t in range(PACK)])
+        turn(1, 3, [piece[:, P:] for piece in second])
         late = sb("late", [P, 3 * H], F32, tag="term0_0_1")
         for i in range(2):
             scale(0, 3, i, late[:, i * H : (i + 1) * H])
-        multiply(0, z0, banks[2], tag="term0_1_1")
+        z0_planes = quantise("z0", z0, 2 * P, tag="term0_1_1")
+        w_codes = sb("w_codes", [P, 2 * N], U32, tag="term1_1_1")
+        for i in range(2):
+            cols = slice(i * N, (i + 1) * N)
+            nc.vector.quantize_mx(
+                out=w_codes[:, cols].bitcast(FP8X4), scales=w_scales[:, cols], in_=w_grouped[:, i * N * PACK : (i + 1) * N * PACK]
+            )
+        multiply(z0_planes, banks[2:3])
         for i in range(2):
             combine(2, i, late[:, 2 * H + i * HALF :], banks[6][:, 2 * i * P : 2 * (i + 1) * P])
-        multiply(1, z1, banks[3])
+        multiply(quantise("z1", z1, 2 * P), banks[3:4])
         for i in range(2):
             combine(3, i, sb("zt3_%d" % i, [P, HALF], F32)[:], banks[(7, 4)[i]][:, : 2 * P])
         store("result0", banks[2], 0, 4, 0, P, nc.scalar.copy, nc.sync)
-        store("result1", banks[3], 0, 4, P, P, nc.vector.tensor_copy, nc.sync)
         z2 = weave(sb("z2", [P, H], F32)[:], banks[6], 2)
-        z3 = [weave(sb("z3_%d" % i, [P, HALF], F32)[:], banks[(7, 4)[i]], 1) for i in range(2)]
-        multiply(2, z2, banks[5])
-        store("result2", banks[5], 0, 4, 2 * P, P, nc.scalar.copy, nc.sync)
-        last_banks = (banks[0], banks[1])
+        z3 = [weave(sb("z3_%d" % i, [P, HALF], F32)[:], banks[(7, 4)[i]], 1, (nc.scalar.copy, nc.vector.tensor_copy)[i]) for i in range(2)]
+        store("result1", banks[3], 0, 4, P, P, nc.scalar.copy, nc.sync)
+        multiply(quantise("z2", z2, 2 * P), banks[5:7])
+        for half in range(2):
+            store("result2_%d" % half, banks[5 + half], 2 * half, 2, 2 * P, P, nc.scalar.copy, nc.sync)
         for i in range(2):
             codes, scales = quantise("last%d" % i, z3[i], P)
             for mt in range(4):
-                target = last_banks[mt // 2][:, (mt % 2) * P : (mt % 2 + 1) * P]
-                product(i, mt, codes[:], scales[:], target, i == 0 and mt % 2 == 0, i == 1 and mt % 2 == 1)
-        store("result_last0", last_banks[0], 0, 2, 3 * P, P, nc.vector.tensor_copy, nc.sync)
-        store("result_last1", last_banks[1], 2, 2, 3 * P, P, nc.scalar.copy, nc.scalar)
+                product(i, mt, codes[:], scales[:], banks[mt][:, :P], i == 0, i == 1)
+        for mt in range(4):
+            copy, queue = ((nc.vector.tensor_copy, nc.sync), (nc.scalar.copy, nc.scalar))[mt % 2]
+            store("result_last%d" % mt, banks[mt], mt, 1, 3 * P, P, copy, queue)

@@ -23,7 +23,7 @@ MULT = mybir.AluOpType.mult
 ADD = mybir.AluOpType.add
 
 M_VECTOR = 48
-W2_GPSIMD = 384
+AT_W3, AT_GATHER, AT_LAST, AT_W2 = 0, 4096, 20480, 24576
 
 
 def tile_picked_kpconv2_none_p_kernel(
@@ -32,6 +32,7 @@ def tile_picked_kpconv2_none_p_kernel(
     nc = tc.nc
     with ExitStack() as ctx:
         keep = ctx.enter_context(tc.tile_pool(name="keep", bufs=1))
+        shared = ctx.enter_context(tc.tile_pool(name="shared", bufs=1))
         psum = ctx.enter_context(tc.psum_pool(name="psum", bufs=1))
         banks = [psum.tile([P, 512], F32, name="bank%d" % n) for n in range(8)]
 
@@ -45,16 +46,19 @@ def tile_picked_kpconv2_none_p_kernel(
         xs = sb("xs", [P, T], U8)
         w1_raw = sb("w1_raw", [P, PACK, H], F32)
         w2_raw = sb("w2_raw", [P, PACK, N], F32)
-        w3_raw = [sb("w3_raw%d" % h, [P, PACK, N // 2], F32) for h in range(2)]
+
+        def placed(name, shape, dtype, offset):
+            return shared.tile(shape, dtype, name=name, offset=offset, align_bytes=64)
+
+        w3_raw = [sb("w3_raw0", [P, PACK, N // 2], F32), placed("w3_raw1", [P, PACK, N // 2], F32, AT_W3)]
         ident = sb("ident", [P, P], F32)
         k_rows = sb("k_rows", [P, P], F32)
         k_cols = sb("k_cols", [P, 4 * BLOCKS], F32)
 
+        nc.gpsimd.memset(k_rows[:], 0.0)
         for n, k in enumerate((k11, k12, k21, k22)):
-            nc.gpsimd.dma_start(k_rows[8 * n : 8 * n + 8, :], k[0:2, :].rearrange("r (b q) -> (r b) q", b=BLOCKS))
+            nc.gpsimd.dma_start(k_rows[BLOCKS * n : BLOCKS * (n + 1), :], k[0:1, :].rearrange("r (b q) -> (r b) q", b=BLOCKS))
         nc.vector.memset(xs[:].bitcast(I32), 0)
-        nc.gpsimd.memset(k_rows[32:64, :], 0.0)
-        nc.gpsimd.memset(k_rows[64:128, :], 0.0)
         make_identity(nc, ident[:])
         by_rows = "(p j) c -> p j c"
         nc.sync.dma_start(offs_t[:], offs)
@@ -84,13 +88,13 @@ def tile_picked_kpconv2_none_p_kernel(
 
         y = [sb("y%d" % t, [P, S], F32) for t in range(PACK)]
 
-        def first_product(t, h, bank, copy):
-            cols = slice(h * HALF, (h + 1) * HALF)
+        def first_product(t, col0, width, bank, copy):
+            h, cols = col0 // HALF, slice(col0, col0 + width)
             nc.tensor.matmul_mx(
                 out=bank,
                 lhsT=w1_codes[:, t * P : (t + 1) * P].bitcast(FP8X4),
                 lhsT_scale=w1_scales[:, t * P : (t + 1) * P],
-                rhs=xw_g[h][:].bitcast(FP8X4),
+                rhs=xw_g[h][:, col0 % HALF : col0 % HALF + width].bitcast(FP8X4),
                 rhs_scale=xs_g[:, cols],
                 start=True,
                 stop=True,
@@ -98,27 +102,25 @@ def tile_picked_kpconv2_none_p_kernel(
             if copy is not None:
                 copy(y[t][:, cols], bank)
 
-        first_product(0, 0, banks[4][:, :HALF], nc.scalar.copy)
-        first_product(1, 0, banks[6][:, :HALF], nc.scalar.copy)
-        first_product(0, 1, banks[5][:, :HALF], nc.vector.tensor_copy)
-        first_product(1, 1, banks[7][:, :HALF], nc.scalar.copy)
+        first_product(0, 0, HALF, banks[4][:, :HALF], nc.scalar.copy)
+        first_product(1, 0, HALF, banks[0][:, :HALF], None)
+        first_product(0, HALF, P, banks[5][:, :P], nc.vector.tensor_copy)
+        first_product(0, HALF + P, P, banks[7][:, :P], nc.scalar.copy)
+        first_product(1, HALF, HALF, banks[0][:, HALF:], None)
+        nc.scalar.copy(y[1][:], banks[0][:])
         for t in range(2, PACK):
             for h in range(2):
-                first_product(t, h, banks[t][:, h * HALF : (h + 1) * HALF], None)
+                first_product(t, h * HALF, HALF, banks[t][:, h * HALF : (h + 1) * HALF], None)
             nc.scalar.copy(y[t][:], banks[t][:])
 
-        nc.tensor.transpose(banks[3][:, :P], k_rows[:], ident[:])
-        nc.scalar.copy(
-            k_cols[:].rearrange("q (n b) -> q n b", b=BLOCKS),
-            banks[3][:, :32].rearrange("q (n r) -> q n r", n=4)[:, :, :BLOCKS],
-        )
+        nc.tensor.transpose(banks[0][:, :P], k_rows[:], ident[:])
+        nc.vector.tensor_copy(k_cols[:], banks[0][:, : 4 * BLOCKS])
 
-        w_scales = sb("w_scales", [P, 2 * N], U8)
-        w_grouped = sb("w_grouped", [P, 2 * N * PACK], BF16)
+        w_grouped = [placed("w_grouped0", [P, N * PACK], BF16, AT_W2), sb("w_grouped1", [P, N * PACK], BF16)]
 
-        def round_on_gpsimd(first, raw):
+        def round_on_gpsimd(i, first, raw):
             nc.gpsimd.tensor_scalar(
-                w_grouped[:, first * PACK : (first + raw.shape[2]) * PACK].rearrange("p (c j) -> p c j", j=PACK),
+                w_grouped[i][:, first * PACK : (first + raw.shape[2]) * PACK].rearrange("p (c j) -> p c j", j=PACK),
                 raw.rearrange("p j c -> p c j"),
                 1.0,
                 0.0,
@@ -127,84 +129,63 @@ def tile_picked_kpconv2_none_p_kernel(
             )
 
         lists = (p1_t, p2_t)
-        turned = [[banks[0], banks[1], banks[4], banks[5]], [banks[2], banks[3], banks[0], banks[1]]]
+        by_pair = [[banks[0], banks[3]], [banks[1], banks[2]]]
+        by_list = {2: [banks[3], banks[1]], 3: [banks[2], banks[0]]}
 
         def k_col(i, l, b):
             n = (2 * i + l) * BLOCKS + b
             return k_cols[:, n : n + 1]
 
-        def look_up(l, b0, blocks, targets):
-            for t in range(PACK):
-                nc.vector.tensor_copy(targets[t], y[t][:].indirect(lists[l][:, 8 * b0 : 8 * (b0 + blocks)]))
-                place = t // 2 + 2 * (t % 2)
-                for c in range(blocks):
-                    nc.tensor.transpose(
-                        turned[l][b0 + c][:, place * P : (place + 1) * P], targets[t][:, c * P : (c + 1) * P], ident[:]
-                    )
-
-        def gather(l, b0, blocks, targets):
-            for t in range(PACK):
-                nc.vector.tensor_copy(targets[t], y[t][:].indirect(lists[l][:, 8 * b0 : 8 * (b0 + blocks)]))
-
-        def turn(l, b, pieces):
-            for t in range(PACK):
-                place = t // 2 + 2 * (t % 2)
-                nc.tensor.transpose(turned[l][b][:, place * P : (place + 1) * P], pieces[t], ident[:])
+        def look_up(l, b, t, piece):
+            nc.vector.tensor_copy(piece, y[t][:].indirect(lists[l][:, 8 * b : 8 * (b + 1)]))
+            if b < 2:
+                bank, place = by_pair[b][t // 2], 2 * l + t % 2
+            else:
+                bank, place = by_list[b][l], t // 2 + 2 * (t % 2)
+            nc.tensor.transpose(bank[:, place * P : (place + 1) * P], piece, ident[:])
 
         def pairs(ap, order):
             return ap.rearrange("q (%s) -> q x e" % order, e=2)
 
-        def quantise(name, values, width, tag=None):
-            codes = sb(name + "_codes", [P, width], U32, tag=tag)
-            scales = sb(name + "_scales", [P, width], U8)
-            nc.vector.quantize_mx(out=codes[:].bitcast(FP8X4), scales=scales[:], in_=values)
-            return codes, scales
-
-        def product(i, mt, codes, scales, target, start, stop):
-            nc.tensor.matmul_mx(
-                out=target,
-                lhsT=w_codes[:, i * N + mt * P : i * N + (mt + 1) * P].bitcast(FP8X4),
-                lhsT_scale=w_scales[:, i * N + mt * P : i * N + (mt + 1) * P],
-                rhs=codes.bitcast(FP8X4),
-                rhs_scale=scales,
-                start=start,
-                stop=stop,
-            )
-
-        out_rows = out.rearrange("(mt p) j -> p mt j", p=P)
-
-        def store(name, bank, mt0, tiles, col0, width, copy, queue):
-            result = sb(name, [P, tiles, width], F32)
-            copy(result[:].rearrange("p mt j -> p (mt j)"), bank[:, : tiles * width])
-            queue.dma_start(out_rows[:, mt0 : mt0 + tiles, col0 : col0 + width], result[:])
-
         terms = {}
+
+        def scale_half(l, b, i, u):
+            source = by_pair[b][u][:, l * HALF : (l + 1) * HALF]
+            target = terms[l, b, i][:, u * HALF : (u + 1) * HALF]
+            if (b, i) != (0, 0):
+                source, target = pairs(source, "e x"), pairs(target, "x e")
+            nc.scalar.activation(target, source, COPY, scale=k_col(i, l, b))
 
         def scale(l, b, i, target):
             terms[l, b, i] = target
-            nc.scalar.activation(pairs(target, "x e"), pairs(turned[l][b][:], "e x"), COPY, scale=k_col(i, l, b))
+            nc.scalar.activation(pairs(target, "x e"), pairs(by_list[b][l][:], "e x"), COPY, scale=k_col(i, l, b))
 
-        def turn_back(zt, target):
-            words = zt.bitcast(F32)
+        def turn_back(words, target):
             for u in range(2):
                 nc.tensor.transpose(target[:, u * P : (u + 1) * P], words[:, u * P : (u + 1) * P], ident[:])
 
-        def add_terms(b, i, room):
-            zt = room[:, : H // 2].bitcast(BF16)
-            nc.gpsimd.tensor_tensor(zt, terms[0, b, i], terms[1, b, i], ADD)
-            turn_back(zt, banks[b][:, 2 * i * P : 2 * (i + 1) * P])
+        def add_terms(b, i, room, target):
+            nc.gpsimd.tensor_tensor(room.bitcast(BF16), terms[0, b, i], terms[1, b, i], ADD)
+            turn_back(room, target)
+
+        def add_by_turning(b, i, bank):
+            for n in range(2 * PACK):
+                u, l, e = n // 4, n // 2 % 2, n % 2
+                cols = slice((2 * u + e) * P, (2 * u + e + 1) * P)
+                nc.tensor.matmul(
+                    bank[:, cols], terms[l, b, i][:, cols], ident[:], start=n == 0, stop=n == 2 * PACK - 1, is_transpose=True
+                )
 
         def combine(b, i, room, target):
-            zt = room[:, : H // 2].bitcast(BF16)
             nc.vector.scalar_tensor_tensor(
-                out=pairs(zt, "x e"),
-                in0=pairs(turned[1][b][:], "e x"),
+                out=pairs(room.bitcast(BF16), "x e"),
+                in0=pairs(by_list[b][1][:], "e x"),
                 scalar=k_col(i, 1, b),
                 in1=pairs(terms[0, b, i], "x e"),
                 op0=MULT,
                 op1=ADD,
             )
-            turn_back(zt, target)
+            turn_back(room, target)
 
         def weave(z, bank, sums, copy=nc.scalar.copy):
             copy(
@@ -212,6 +193,26 @@ def tile_picked_kpconv2_none_p_kernel(
                 bank[:, : sums * 2 * P].rearrange("p (i u j) -> p i j u", i=sums, u=2),
             )
             return z.bitcast(BF16)
+
+        def quantise(name, values, width, scales=None):
+            codes = sb(name + "_codes", [P, width], U32)
+            if scales is None:
+                scales = sb(name + "_scales", [P, width], U8)
+            nc.vector.quantize_mx(out=codes[:].bitcast(FP8X4), scales=scales[:], in_=values)
+            return codes, scales
+
+        weights = []
+
+        def product(i, mt, codes, scales, target, start, stop):
+            nc.tensor.matmul_mx(
+                out=target,
+                lhsT=weights[i][0][:, mt * P : (mt + 1) * P].bitcast(FP8X4),
+                lhsT_scale=weights[i][1][:, mt * P : (mt + 1) * P],
+                rhs=codes.bitcast(FP8X4),
+                rhs_scale=scales,
+                start=start,
+                stop=stop,
+            )
 
         def multiply(planes, targets):
             codes, scales = planes
@@ -223,70 +224,80 @@ def tile_picked_kpconv2_none_p_kernel(
                     target = targets[mt // per_bank][:, place * P : (place + 1) * P]
                     product(i, mt, codes[:, cols], scales[:, cols], target, i == 0 and place == 0, i == 1 and place == per_bank - 1)
 
-        def look_up_both(b, room):
-            for t in range(PACK):
-                for l in range(2):
-                    piece = room[:, (2 * t + l) * P : (2 * t + l + 1) * P]
-                    nc.vector.tensor_copy(piece, y[t][:].indirect(lists[l][:, 8 * b : 8 * (b + 1)]))
-                    place = t // 2 + 2 * (t % 2)
-                    nc.tensor.transpose(turned[l][b][:, place * P : (place + 1) * P], piece, ident[:])
+        out_rows = out.rearrange("(mt p) j -> p mt j", p=P)
 
-        g_block0 = sb("g_block0", [P, 2 * H], F32)
-        g_block1 = sb("g_block1", [P, 2 * H], F32, tag="k_rows")
-        look_up_both(0, g_block0)
-        look_up_both(1, g_block1)
-        look_up(0, 2, 2, [g_block1[:, t * HALF : (t + 1) * HALF] for t in range(PACK)])
-        round_on_gpsimd(0, w2_raw[:, :, :W2_GPSIMD])
-        nc.scalar.copy(
-            w_grouped[:, W2_GPSIMD * PACK : N * PACK].rearrange("p (c n j) -> p c j n", n=4, j=PACK),
-            w2_raw[:, :, W2_GPSIMD:].rearrange("p j (c n) -> p c j n", n=4),
-        )
+        def store(name, bank, mt0, tiles, col0, copy, queue):
+            result = sb(name, [P, tiles, P], F32)
+            copy(result[:].rearrange("p mt j -> p (mt j)"), bank[:, : tiles * P])
+            queue.dma_start(out_rows[:, mt0 : mt0 + tiles, col0 : col0 + P], result[:])
+
+        for t in range(PACK):
+            for l in range(2):
+                if (t, l) == (2, 1):
+                    look_up(l, 0, t, placed("g0_anchor", [P, P], F32, AT_GATHER)[:])
+                else:
+                    look_up(l, 0, t, sb("g0_%d_%d" % (t, l), [P, P], F32)[:])
+        round_on_gpsimd(0, 0, w2_raw[:])
         for h in range(2):
-            round_on_gpsimd(N + h * N // 2, w3_raw[h][:])
+            round_on_gpsimd(1, h * N // 2, w3_raw[h][:])
+        gathered = placed("gathered", [P, 3, PACK, 2, P], F32, AT_GATHER)
+        z0 = sb("z0", [P, H], F32)
         for b in range(2):
+            if b == 1:
+                for t in range(PACK):
+                    for l in range(2):
+                        look_up(l, b, t, gathered[:, 0, t, l, :])
             for i in range(2):
                 for l in range(2):
-                    scale(l, b, i, sb("term%d_%d_%d" % (l, b, i), [P, H], F32)[:])
+                    terms[l, b, i] = sb("term%d_%d_%d" % (l, b, i), [P, H], F32)[:]
+            for u in range(2):
+                for i in range(2):
+                    for l in range(2):
+                        scale_half(l, b, i, u)
+            if b == 0:
+                add_by_turning(0, 0, banks[0])
+                add_terms(0, 1, placed("zt0_1", [P, HALF], F32, AT_W3)[:], banks[4])
         for i in range(2):
-            add_terms(0, i, w3_raw[1][:, i, :])
-        for i in range(2):
-            add_terms(1, i, terms[0, 0, i])
-        z0 = weave(sb("z0", [P, H], F32)[:], banks[0], 2)
-        second = [g_block1[:, t * HALF : (t + 1) * HALF] for t in range(PACK)]
-        gather(1, 2, 2, second)
-        turn(1, 2, [piece[:, :P] for piece in second])
-        early = sb("early", [P, 2 * H], F32, tag="w3_raw1")
-        for i in range(2):
-            scale(0, 2, i, early[:, i * H : (i + 1) * H])
-        z1 = weave(sb("z1", [P, H], F32)[:], banks[1], 2)
-        turn(1, 3, [piece[:, P:] for piece in second])
-        late = sb("late", [P, 3 * H], F32, tag="term0_0_1")
-        for i in range(2):
-            scale(0, 3, i, late[:, i * H : (i + 1) * H])
-        z0_planes = quantise("z0", z0, 2 * P, tag="term0_1_1")
-        w_codes = sb("w_codes", [P, 2 * N], U32, tag="term1_1_1")
-        for i in range(2):
-            cols = slice(i * N, (i + 1) * N)
-            nc.vector.quantize_mx(
-                out=w_codes[:, cols].bitcast(FP8X4), scales=w_scales[:, cols], in_=w_grouped[:, i * N * PACK : (i + 1) * N * PACK]
-            )
-        multiply(z0_planes, banks[2:3])
-        for i in range(2):
-            combine(2, i, late[:, 2 * H + i * HALF :], banks[6][:, 2 * i * P : 2 * (i + 1) * P])
-        multiply(quantise("z1", z1, 2 * P), banks[3:4])
-        for i in range(2):
-            combine(3, i, sb("zt3_%d" % i, [P, HALF], F32)[:], banks[(7, 4)[i]][:, : 2 * P])
-        store("result0", banks[2], 0, 4, 0, P, nc.scalar.copy, nc.sync)
+            add_terms(1, i, placed("zt1_%d" % i, [P, HALF], F32, AT_W3 + 1024 * (1 + i))[:], banks[5][:, i * HALF : (i + 1) * HALF])
+        nc.scalar.copy(
+            z0[:, :HALF].bitcast(BF16).rearrange("p (j u e) -> p j u e", u=2, e=2),
+            banks[0][:].rearrange("p (u e j) -> p j u e", u=2, e=2),
+        )
+        for t in range(PACK):
+            for l in range(2):
+                look_up(l, 2, t, gathered[:, 1, t, l, :])
+        for l in range(2):
+            scale(l, 2, 0, placed("term%d_2_0" % l, [P, H], F32, AT_LAST + 2048 * l)[:])
+        add_terms(2, 0, placed("zt2_0", [P, HALF], F32, AT_W3 + 3072)[:], banks[6][:, :HALF])
+        scale(0, 2, 1, sb("term0_2_1", [P, H], F32)[:])
+        for l in range(2):
+            for t in range(PACK):
+                look_up(l, 3, t, gathered[:, 2, t, l, :])
+        combine(2, 1, sb("zt2_1", [P, HALF], F32)[:], banks[6][:, HALF:])
+        weave(z0[:, HALF:], banks[4], 1)
+        z1 = weave(sb("z1", [P, H], F32)[:], banks[5], 2)
+        weights.append(quantise("w2", w_grouped[0][:], N, placed("w2_scales", [P, N], U8, AT_LAST)))
+        z0_planes = quantise("z0", z0[:].bitcast(BF16), 2 * P, placed("z0_scales", [P, 2 * P], U8, AT_LAST + 2048))
+        weights.append(quantise("w3", w_grouped[1][:], N, placed("w3_scales", [P, N], U8, AT_W2)))
+        multiply(z0_planes, banks[3:4])
+        multiply(quantise("z1", z1, 2 * P, placed("z1_scales", [P, 2 * P], U8, AT_W2 + 512)), banks[1:2])
+        scale(0, 3, 0, sb("term0_3_0", [P, H], F32)[:])
+        combine(3, 0, sb("zt3_0", [P, HALF], F32)[:], banks[7])
         z2 = weave(sb("z2", [P, H], F32)[:], banks[6], 2)
+        scale(0, 3, 1, sb("term0_3_1", [P, H], F32)[:])
+        z2_planes = quantise("z2", z2, 2 * P)
+        combine(3, 1, sb("zt3_1", [P, HALF], F32)[:], banks[4])
+        store("result0", banks[3], 0, 4, 0, nc.scalar.copy, nc.sync)
         z3 = [weave(sb("z3_%d" % i, [P, HALF], F32)[:], banks[(7, 4)[i]], 1, (nc.scalar.copy, nc.vector.tensor_copy)[i]) for i in range(2)]
-        store("result1", banks[3], 0, 4, P, P, nc.scalar.copy, nc.sync)
-        multiply(quantise("z2", z2, 2 * P), banks[5:7])
+        multiply(z2_planes, banks[5:7])
+        store("result1", banks[1], 0, 4, P, nc.scalar.copy, nc.sync)
         for half in range(2):
-            store("result2_%d" % half, banks[5 + half], 2 * half, 2, 2 * P, P, nc.scalar.copy, nc.sync)
+            store("result2_%d" % half, banks[5 + half], 2 * half, 2, 2 * P, nc.scalar.copy, nc.sync)
+        last = [banks[n] for n in (2, 7, 0, 3)]
+        last_planes = [quantise("last%d" % i, z3[i], P) for i in range(2)]
         for i in range(2):
-            codes, scales = quantise("last%d" % i, z3[i], P)
             for mt in range(4):
-                product(i, mt, codes[:], scales[:], banks[mt][:, :P], i == 0, i == 1)
+                product(i, mt, last_planes[i][0][:], last_planes[i][1][:], last[mt][:, :P], i == 0, i == 1)
         for mt in range(4):
             copy, queue = ((nc.vector.tensor_copy, nc.sync), (nc.scalar.copy, nc.scalar))[mt % 2]
-            store("result_last%d" % mt, banks[mt], mt, 1, 3 * P, P, copy, queue)
+            store("result_last%d" % mt, last[mt], mt, 1, 3 * P, copy, queue)

@@ -73,7 +73,7 @@ def tile_picked_kpconv2_none_p_kernel(
             nc.sync.dma_start(w3_raw[h][:], w3.rearrange(by_rows, j=PACK)[:, :, h * N // 2 : (h + 1) * N // 2])
 
         xs_g = sb("xs_g", [P, S], U8)
-        xw_g = [sb("xw_g%d" % h, [P, HALF], U32) for h in range(2)]
+        xw_g = sb("xw_g", [P, S], U32)
         w1_codes = sb("w1_codes", [P, H], U32)
         w1_scales = sb("w1_scales", [P, H], U8)
         w1_grouped = sb("w1_grouped", [P, H * PACK], BF16)
@@ -84,17 +84,17 @@ def tile_picked_kpconv2_none_p_kernel(
         nc.vector.tensor_copy(xs_g[:], xs[:].indirect(offs_t[:]))
         nc.vector.quantize_mx(out=w1_codes[:].bitcast(FP8X4), scales=w1_scales[:], in_=w1_grouped[:])
         for h in range(2):
-            nc.vector.tensor_copy(xw_g[h][:], xw[:].indirect(offs_t[:, 16 * h : 16 * h + 16]))
+            nc.vector.tensor_copy(xw_g[:, h * HALF : (h + 1) * HALF], xw[:].indirect(offs_t[:, 16 * h : 16 * h + 16]))
 
         y = [sb("y%d" % t, [P, S], F32) for t in range(PACK)]
 
         def first_product(t, col0, width, bank, copy):
-            h, cols = col0 // HALF, slice(col0, col0 + width)
+            cols = slice(col0, col0 + width)
             nc.tensor.matmul_mx(
                 out=bank,
                 lhsT=w1_codes[:, t * P : (t + 1) * P].bitcast(FP8X4),
                 lhsT_scale=w1_scales[:, t * P : (t + 1) * P],
-                rhs=xw_g[h][:, col0 % HALF : col0 % HALF + width].bitcast(FP8X4),
+                rhs=xw_g[:, cols].bitcast(FP8X4),
                 rhs_scale=xs_g[:, cols],
                 start=True,
                 stop=True,
@@ -273,6 +273,8 @@ def tile_picked_kpconv2_none_p_kernel(
         for l in range(2):
             for t in range(PACK):
                 look_up(l, 3, t, gathered[:, 2, t, l, :])
+        for t in range(2):
+            first_product(t, 0, S, banks[3][:], None)
         combine(2, 1, sb("zt2_1", [P, HALF], F32)[:], banks[6][:, HALF:])
         weave(z0[:, HALF:], banks[4], 1)
         z1 = weave(sb("z1", [P, H], F32)[:], banks[5], 2)

@@ -270,11 +270,11 @@ def tile_picked_kpconv2_none_p_kernel(
             scale(l, 2, 0, placed("term%d_2_0" % l, [P, H], F32, AT_LAST + 2048 * l)[:])
         add_terms(2, 0, placed("zt2_0", [P, HALF], F32, AT_W3 + 3072)[:], banks[6][:, :HALF])
         scale(0, 2, 1, sb("term0_2_1", [P, H], F32)[:])
+        for t in range(3):
+            first_product(t, 0, S, banks[2][:], None)
         for l in range(2):
             for t in range(PACK):
                 look_up(l, 3, t, gathered[:, 2, t, l, :])
-        for t in range(2):
-            first_product(t, 0, S, banks[3][:], None)
         combine(2, 1, sb("zt2_1", [P, HALF], F32)[:], banks[6][:, HALF:])
         weave(z0[:, HALF:], banks[4], 1)
         z1 = weave(sb("z1", [P, H], F32)[:], banks[5], 2)

@@ -23,7 +23,7 @@ MULT = mybir.AluOpType.mult
 ADD = mybir.AluOpType.add
 
 M_VECTOR = 48
-AT_W3, AT_GATHER, AT_LAST, AT_W2 = 0, 4096, 20480, 24576
+AT_W3, AT_GATHER, AT_LAST, AT_W2, AT_Z1 = 2048, 8192, 24576, 28672, 36864
 
 
 def tile_picked_kpconv2_none_p_kernel(
@@ -57,17 +57,17 @@ def tile_picked_kpconv2_none_p_kernel(
 
         nc.gpsimd.memset(k_rows[:], 0.0)
         for n, k in enumerate((k11, k12, k21, k22)):
-            nc.gpsimd.dma_start(k_rows[BLOCKS * n : BLOCKS * (n + 1), :], k[0:1, :].rearrange("r (b q) -> (r b) q", b=BLOCKS))
+            (nc.gpsimd, nc.scalar)[n % 2].dma_start(k_rows[BLOCKS * n : BLOCKS * (n + 1), :], k[0:1, :].rearrange("r (b q) -> (r b) q", b=BLOCKS))
         nc.vector.memset(xs[:].bitcast(I32), 0)
         make_identity(nc, ident[:])
         by_rows = "(p j) c -> p j c"
         nc.sync.dma_start(offs_t[:], offs)
         nc.sync.dma_start(w1_raw[:], w1.rearrange(by_rows, j=PACK))
-        nc.sync.dma_start(p2_t[:], p2)
         for r in range(4):
             nc.sync.dma_start(xs[r:P:32, :].bitcast(I32), x_scales[0, r:16:4, :].bitcast(I32))
         nc.sync.dma_start(xw[:].bitcast(I32), x_words[0].rearrange("p n t -> p (n t)").bitcast(I32))
         nc.sync.dma_start(p1_t[:], p1)
+        nc.sync.dma_start(p2_t[:], p2)
         nc.sync.dma_start(w2_raw[:], w2.rearrange(by_rows, j=PACK))
         for h in range(2):
             nc.sync.dma_start(w3_raw[h][:], w3.rearrange(by_rows, j=PACK)[:, :, h * N // 2 : (h + 1) * N // 2])
@@ -102,6 +102,8 @@ def tile_picked_kpconv2_none_p_kernel(
             if copy is not None:
                 copy(y[t][:, cols], bank)
 
+        nc.tensor.transpose(banks[4][:, :P], k_rows[:], ident[:])
+        nc.scalar.copy(k_cols[:], banks[4][:, : 4 * BLOCKS])
         first_product(0, 0, HALF, banks[4][:, :HALF], nc.scalar.copy)
         first_product(1, 0, HALF, banks[0][:, :HALF], None)
         first_product(0, HALF, P, banks[5][:, :P], nc.vector.tensor_copy)
@@ -113,10 +115,8 @@ def tile_picked_kpconv2_none_p_kernel(
                 first_product(t, h * HALF, HALF, banks[t][:, h * HALF : (h + 1) * HALF], None)
             nc.scalar.copy(y[t][:], banks[t][:])
 
-        nc.tensor.transpose(banks[0][:, :P], k_rows[:], ident[:])
-        nc.vector.tensor_copy(k_cols[:], banks[0][:, : 4 * BLOCKS])
 
-        w_grouped = [placed("w_grouped0", [P, N * PACK], BF16, AT_W2), sb("w_grouped1", [P, N * PACK], BF16)]
+        w_grouped = [placed("w_grouped%d" % i, [P, N * PACK], BF16, AT_W2 + 4096 * i) for i in range(2)]
 
         def round_on_gpsimd(i, first, raw):
             nc.gpsimd.tensor_scalar(
@@ -130,7 +130,7 @@ def tile_picked_kpconv2_none_p_kernel(
 
         lists = (p1_t, p2_t)
         by_pair = [[banks[0], banks[3]], [banks[1], banks[2]]]
-        by_list = {2: [banks[3], banks[1]], 3: [banks[2], banks[0]]}
+        by_list = {2: [banks[3], banks[1]], 3: [banks[2], banks[4]]}
 
         def k_col(i, l, b):
             n = (2 * i + l) * BLOCKS + b
@@ -256,9 +256,9 @@ def tile_picked_kpconv2_none_p_kernel(
                         scale_half(l, b, i, u)
             if b == 0:
                 add_by_turning(0, 0, banks[0])
-                add_terms(0, 1, placed("zt0_1", [P, HALF], F32, AT_W3)[:], banks[4])
+                add_terms(0, 1, placed("zt0_1", [P, HALF], F32, AT_W3 + 1024)[:], banks[4])
         for i in range(2):
-            add_terms(1, i, placed("zt1_%d" % i, [P, HALF], F32, AT_W3 + 1024 * (1 + i))[:], banks[5][:, i * HALF : (i + 1) * HALF])
+            add_terms(1, i, placed("zt1_%d" % i, [P, HALF], F32, AT_W3 + 2048 * (1 - i))[:], banks[5][:, i * HALF : (i + 1) * HALF])
         nc.scalar.copy(
             z0[:, :HALF].bitcast(BF16).rearrange("p (j u e) -> p j u e", u=2, e=2),
             banks[0][:].rearrange("p (u e j) -> p j u e", u=2, e=2),
@@ -272,30 +272,31 @@ def tile_picked_kpconv2_none_p_kernel(
         scale(0, 2, 1, sb("term0_2_1", [P, H], F32)[:])
         for t in range(3):
             first_product(t, 0, S, banks[2][:], None)
-        for l in range(2):
-            for t in range(PACK):
-                look_up(l, 3, t, gathered[:, 2, t, l, :])
-        combine(2, 1, sb("zt2_1", [P, HALF], F32)[:], banks[6][:, HALF:])
+        for t in range(PACK):
+            look_up(0, 3, t, gathered[:, 2, t, 0, :])
         weave(z0[:, HALF:], banks[4], 1)
-        z1 = weave(sb("z1", [P, H], F32)[:], banks[5], 2)
+        for t in range(PACK):
+            look_up(1, 3, t, gathered[:, 2, t, 1, :])
+        combine(2, 1, sb("zt2_1", [P, HALF], F32)[:], banks[6][:, HALF:])
+        z1 = weave(placed("z1", [P, H], F32, AT_Z1)[:], banks[5], 2)
         weights.append(quantise("w2", w_grouped[0][:], N, placed("w2_scales", [P, N], U8, AT_LAST)))
         z0_planes = quantise("z0", z0[:].bitcast(BF16), 2 * P, placed("z0_scales", [P, 2 * P], U8, AT_LAST + 2048))
         weights.append(quantise("w3", w_grouped[1][:], N, placed("w3_scales", [P, N], U8, AT_W2)))
         multiply(z0_planes, banks[3:4])
         multiply(quantise("z1", z1, 2 * P, placed("z1_scales", [P, 2 * P], U8, AT_W2 + 512)), banks[1:2])
-        scale(0, 3, 0, sb("term0_3_0", [P, H], F32)[:])
-        combine(3, 0, sb("zt3_0", [P, HALF], F32)[:], banks[7])
+        scale(0, 3, 0, placed("term0_3_0", [P, H], F32, AT_W3 - 1024)[:])
+        combine(3, 0, placed("zt3_0", [P, HALF], F32, AT_W2 + 4096)[:], banks[7])
         z2 = weave(sb("z2", [P, H], F32)[:], banks[6], 2)
-        scale(0, 3, 1, sb("term0_3_1", [P, H], F32)[:])
+        scale(0, 3, 1, placed("term0_3_1", [P, H], F32, AT_W3 + 3072)[:])
         z2_planes = quantise("z2", z2, 2 * P)
-        combine(3, 1, sb("zt3_1", [P, HALF], F32)[:], banks[4])
+        combine(3, 1, placed("zt3_1", [P, HALF], F32, AT_Z1)[:], banks[0])
         store("result0", banks[3], 0, 4, 0, nc.scalar.copy, nc.sync)
-        z3 = [weave(sb("z3_%d" % i, [P, HALF], F32)[:], banks[(7, 4)[i]], 1, (nc.scalar.copy, nc.vector.tensor_copy)[i]) for i in range(2)]
+        z3 = [weave(sb("z3_%d" % i, [P, HALF], F32)[:], banks[(7, 0)[i]], 1, (nc.scalar.copy, nc.vector.tensor_copy)[i]) for i in range(2)]
         multiply(z2_planes, banks[5:7])
         store("result1", banks[1], 0, 4, P, nc.scalar.copy, nc.sync)
         for half in range(2):
             store("result2_%d" % half, banks[5 + half], 2 * half, 2, 2 * P, nc.scalar.copy, nc.sync)
-        last = [banks[n] for n in (2, 7, 0, 3)]
+        last = [banks[n] for n in (2, 7, 4, 3)]
         last_planes = [quantise("last%d" % i, z3[i], P) for i in range(2)]
         for i in range(2):
             for mt in range(4):

@@ -57,17 +57,17 @@ def tile_picked_kpconv2_none_p_kernel(
 
         nc.gpsimd.memset(k_rows[:], 0.0)
         for n, k in enumerate((k11, k12, k21, k22)):
-            (nc.gpsimd, nc.scalar)[n % 2].dma_start(k_rows[BLOCKS * n : BLOCKS * (n + 1), :], k[0:1, :].rearrange("r (b q) -> (r b) q", b=BLOCKS))
+            nc.gpsimd.dma_start(k_rows[BLOCKS * n : BLOCKS * (n + 1), :], k[0:1, :].rearrange("r (b q) -> (r b) q", b=BLOCKS))
         nc.vector.memset(xs[:].bitcast(I32), 0)
         make_identity(nc, ident[:])
         by_rows = "(p j) c -> p j c"
         nc.sync.dma_start(offs_t[:], offs)
         nc.sync.dma_start(w1_raw[:], w1.rearrange(by_rows, j=PACK))
+        nc.sync.dma_start(p2_t[:], p2)
         for r in range(4):
             nc.sync.dma_start(xs[r:P:32, :].bitcast(I32), x_scales[0, r:16:4, :].bitcast(I32))
         nc.sync.dma_start(xw[:].bitcast(I32), x_words[0].rearrange("p n t -> p (n t)").bitcast(I32))
         nc.sync.dma_start(p1_t[:], p1)
-        nc.sync.dma_start(p2_t[:], p2)
         nc.sync.dma_start(w2_raw[:], w2.rearrange(by_rows, j=PACK))
         for h in range(2):
             nc.sync.dma_start(w3_raw[h][:], w3.rearrange(by_rows, j=PACK)[:, :, h * N // 2 : (h + 1) * N // 2])
@@ -102,8 +102,6 @@ def tile_picked_kpconv2_none_p_kernel(
             if copy is not None:
                 copy(y[t][:, cols], bank)
 
-        nc.tensor.transpose(banks[4][:, :P], k_rows[:], ident[:])
-        nc.scalar.copy(k_cols[:], banks[4][:, : 4 * BLOCKS])
         first_product(0, 0, HALF, banks[4][:, :HALF], nc.scalar.copy)
         first_product(1, 0, HALF, banks[0][:, :HALF], None)
         first_product(0, HALF, P, banks[5][:, :P], nc.vector.tensor_copy)
@@ -116,6 +114,8 @@ def tile_picked_kpconv2_none_p_kernel(
             nc.scalar.copy(y[t][:], banks[t][:])
 
 
+        nc.tensor.transpose(banks[2][:, :P], k_rows[:], ident[:])
+        nc.scalar.copy(k_cols[:], banks[2][:, : 4 * BLOCKS])
         w_grouped = [placed("w_grouped%d" % i, [P, N * PACK], BF16, AT_W2 + 4096 * i) for i in range(2)]
 
         def round_on_gpsimd(i, first, raw):
@@ -291,11 +291,11 @@ def tile_picked_kpconv2_none_p_kernel(
         z2_planes = quantise("z2", z2, 2 * P)
         combine(3, 1, placed("zt3_1", [P, HALF], F32, AT_Z1)[:], banks[0])
         store("result0", banks[3], 0, 4, 0, nc.scalar.copy, nc.sync)
-        z3 = [weave(sb("z3_%d" % i, [P, HALF], F32)[:], banks[(7, 0)[i]], 1, (nc.scalar.copy, nc.vector.tensor_copy)[i]) for i in range(2)]
+        z3 = [weave(sb("z3_%d" % i, [P, HALF], F32)[:], banks[(7, 0)[i]], 1, nc.scalar.copy) for i in range(2)]
         multiply(z2_planes, banks[5:7])
         store("result1", banks[1], 0, 4, P, nc.scalar.copy, nc.sync)
         for half in range(2):
-            store("result2_%d" % half, banks[5 + half], 2 * half, 2, 2 * P, nc.scalar.copy, nc.sync)
+            store("result2_%d" % half, banks[5 + half], 2 * half, 2, 2 * P, (nc.vector.tensor_copy, nc.scalar.copy)[half], nc.sync)
         last = [banks[n] for n in (2, 7, 4, 3)]
         last_planes = [quantise("last%d" % i, z3[i], P) for i in range(2)]
         for i in range(2):

@@ -249,7 +249,11 @@ def tile_picked_kpconv2_none_p_kernel(
                         look_up(l, b, t, gathered[:, 0, t, l, :])
             for i in range(2):
                 for l in range(2):
-                    terms[l, b, i] = sb("term%d_%d_%d" % (l, b, i), [P, H], F32)[:]
+                    name = "term%d_%d_%d" % (l, b, i)
+                    if (b, i) == (1, 1):
+                        terms[l, b, i] = placed(name, [P, H], F32, AT_LAST + 2048 * l)[:]
+                    else:
+                        terms[l, b, i] = sb(name, [P, H], F32)[:]
             for u in range(2):
                 for i in range(2):
                     for l in range(2):
@@ -267,8 +271,9 @@ def tile_picked_kpconv2_none_p_kernel(
             for l in range(2):
                 look_up(l, 2, t, gathered[:, 1, t, l, :])
         for l in range(2):
-            scale(l, 2, 0, placed("term%d_2_0" % l, [P, H], F32, AT_LAST + 2048 * l)[:])
-        add_terms(2, 0, placed("zt2_0", [P, HALF], F32, AT_W3 + 3072)[:], banks[6][:, :HALF])
+            terms[l, 2, 0] = sb("term%d_2_0" % l, [P, H], F32)[:]
+            nc.scalar.activation(terms[l, 2, 0], by_list[2][l][:], COPY, scale=k_col(0, l, 2))
+        add_by_turning(2, 0, banks[0])
         scale(0, 2, 1, sb("term0_2_1", [P, H], F32)[:])
         for t in range(3):
             first_product(t, 0, S, banks[2][:], None)
@@ -277,7 +282,7 @@ def tile_picked_kpconv2_none_p_kernel(
         weave(z0[:, HALF:], banks[4], 1)
         for t in range(PACK):
             look_up(1, 3, t, gathered[:, 2, t, 1, :])
-        combine(2, 1, sb("zt2_1", [P, HALF], F32)[:], banks[6][:, HALF:])
+        combine(2, 1, sb("zt2_1", [P, HALF], F32)[:], banks[6][:, :HALF])
         z1 = weave(placed("z1", [P, H], F32, AT_Z1)[:], banks[5], 2)
         weights.append(quantise("w2", w_grouped[0][:], N, placed("w2_scales", [P, N], U8, AT_LAST)))
         z0_planes = quantise("z0", z0[:].bitcast(BF16), 2 * P, placed("z0_scales", [P, 2 * P], U8, AT_LAST + 2048))
@@ -286,8 +291,14 @@ def tile_picked_kpconv2_none_p_kernel(
         multiply(quantise("z1", z1, 2 * P, placed("z1_scales", [P, 2 * P], U8, AT_W2 + 512)), banks[1:2])
         scale(0, 3, 0, placed("term0_3_0", [P, H], F32, AT_W3 - 1024)[:])
         combine(3, 0, placed("zt3_0", [P, HALF], F32, AT_W2 + 4096)[:], banks[7])
-        z2 = weave(sb("z2", [P, H], F32)[:], banks[6], 2)
-        scale(0, 3, 1, placed("term0_3_1", [P, H], F32, AT_W3 + 3072)[:])
+        z2_words = sb("z2", [P, H], F32)
+        z2 = z2_words[:].bitcast(BF16)
+        nc.scalar.copy(
+            z2[:, :H].rearrange("p (j u e) -> p j u e", u=2, e=2),
+            banks[0][:].rearrange("p (e u j) -> p j u e", u=2, e=2),
+        )
+        weave(z2_words[:, HALF:], banks[6], 1)
+        scale(0, 3, 1, placed("term0_3_1", [P, H], F32, AT_W3 + 2048)[:])
         z2_planes = quantise("z2", z2, 2 * P)
         combine(3, 1, placed("zt3_1", [P, HALF], F32, AT_Z1)[:], banks[0])
         store("result0", banks[3], 0, 4, 0, nc.scalar.copy, nc.sync)

@@ -103,11 +103,10 @@ def tile_picked_kpconv2_none_p_kernel(
                 copy(y[t][:, cols], bank)
 
         first_product(0, 0, HALF, banks[4][:, :HALF], nc.scalar.copy)
-        first_product(1, 0, HALF, banks[0][:, :HALF], None)
+        first_product(1, 0, HALF, banks[6][:, :HALF], nc.scalar.copy)
         first_product(0, HALF, P, banks[5][:, :P], nc.vector.tensor_copy)
         first_product(0, HALF + P, P, banks[7][:, :P], nc.scalar.copy)
-        first_product(1, HALF, HALF, banks[0][:, HALF:], None)
-        nc.scalar.copy(y[1][:], banks[0][:])
+        first_product(1, HALF, HALF, banks[0][:, :HALF], nc.scalar.copy)
         for t in range(2, PACK):
             for h in range(2):
                 first_product(t, h * HALF, HALF, banks[t][:, h * HALF : (h + 1) * HALF], None)
@@ -299,14 +298,17 @@ def tile_picked_kpconv2_none_p_kernel(
         )
         weave(z2_words[:, HALF:], banks[6], 1)
         scale(0, 3, 1, placed("term0_3_1", [P, H], F32, AT_W3 + 2048)[:])
-        z2_planes = quantise("z2", z2, 2 * P)
+        z2_planes = [quantise("z2_%d" % i, z2[:, i * H : (i + 1) * H], P) for i in range(2)]
         combine(3, 1, placed("zt3_1", [P, HALF], F32, AT_Z1)[:], banks[0])
         store("result0", banks[3], 0, 4, 0, nc.scalar.copy, nc.sync)
-        z3 = [weave(sb("z3_%d" % i, [P, HALF], F32)[:], banks[(7, 0)[i]], 1, nc.scalar.copy) for i in range(2)]
-        multiply(z2_planes, banks[5:7])
+        z3 = [weave(sb("z3_%d" % i, [P, HALF], F32)[:], banks[(7, 0)[i]], 1, (nc.scalar.copy, nc.vector.tensor_copy)[i]) for i in range(2)]
+        for i, (codes, scales) in enumerate(z2_planes):
+            for mt in range(4):
+                target = banks[5 + mt // 2][:, mt % 2 * P : (mt % 2 + 1) * P]
+                product(i, mt, codes[:], scales[:], target, i == 0 and mt % 2 == 0, i == 1 and mt % 2 == 1)
         store("result1", banks[1], 0, 4, P, nc.scalar.copy, nc.sync)
         for half in range(2):
-            store("result2_%d" % half, banks[5 + half], 2 * half, 2, 2 * P, (nc.vector.tensor_copy, nc.scalar.copy)[half], nc.sync)
+            store("result2_%d" % half, banks[5 + half], 2 * half, 2, 2 * P, nc.scalar.copy, nc.sync)
         last = [banks[n] for n in (2, 7, 4, 3)]
         last_planes = [quantise("last%d" % i, z3[i], P) for i in range(2)]
         for i in range(2):

@@ -23,7 +23,12 @@ MULT = mybir.AluOpType.mult
 ADD = mybir.AluOpType.add
 
 M_VECTOR = 48
-AT_W3, AT_GATHER, AT_LAST, AT_W2, AT_Z1 = 2048, 8192, 24576, 28672, 36864
+AT_W2RAW, AT_W3RAW, AT_WG = 0, 8192, 16384
+AT_PIECE = 24576
+AT_TERM = 32768
+AT_ZT = 40960
+AT_Z = 57344
+AT_TERM2 = 69632
 
 
 def tile_picked_kpconv2_none_p_kernel(
@@ -36,8 +41,10 @@ def tile_picked_kpconv2_none_p_kernel(
         psum = ctx.enter_context(tc.psum_pool(name="psum", bufs=1))
         banks = [psum.tile([P, 512], F32, name="bank%d" % n) for n in range(8)]
 
-        def sb(name, shape, dtype, tag=None):
-            return keep.tile(shape, dtype, name=name, tag=tag or name, align_bytes=64)
+        def sb(name, shape, dtype, at=None):
+            if at is None:
+                return keep.tile(shape, dtype, name=name, align_bytes=64)
+            return shared.tile(shape, dtype, name=name, offset=at, align_bytes=64)
 
         offs_t = sb("offs_t", [P, S // 16], U16)
         p1_t = sb("p1_t", [P, S // 16], U16)
@@ -45,12 +52,8 @@ def tile_picked_kpconv2_none_p_kernel(
         xw = sb("xw", [P, T], U32)
         xs = sb("xs", [P, T], U8)
         w1_raw = sb("w1_raw", [P, PACK, H], F32)
-        w2_raw = sb("w2_raw", [P, PACK, N], F32)
-
-        def placed(name, shape, dtype, offset):
-            return shared.tile(shape, dtype, name=name, offset=offset, align_bytes=64)
-
-        w3_raw = [sb("w3_raw0", [P, PACK, N // 2], F32), placed("w3_raw1", [P, PACK, N // 2], F32, AT_W3)]
+        w2_raw = sb("w2_raw", [P, PACK, N], F32, AT_W2RAW)
+        w3_raw = [sb("w3_raw%d" % h, [P, PACK, N // 2], F32, AT_W3RAW + 4096 * h) for h in range(2)]
         ident = sb("ident", [P, P], F32)
         k_rows = sb("k_rows", [P, P], F32)
         k_cols = sb("k_cols", [P, 4 * BLOCKS], F32)
@@ -102,20 +105,62 @@ def tile_picked_kpconv2_none_p_kernel(
             if copy is not None:
                 copy(y[t][:, cols], bank)
 
-        first_product(0, 0, HALF, banks[4][:, :HALF], nc.scalar.copy)
-        first_product(1, 0, HALF, banks[6][:, :HALF], nc.scalar.copy)
-        first_product(0, HALF, P, banks[5][:, :P], nc.vector.tensor_copy)
-        first_product(0, HALF + P, P, banks[7][:, :P], nc.scalar.copy)
-        first_product(1, HALF, HALF, banks[0][:, :HALF], nc.scalar.copy)
-        for t in range(2, PACK):
-            for h in range(2):
-                first_product(t, h * HALF, HALF, banks[t][:, h * HALF : (h + 1) * HALF], None)
-            nc.scalar.copy(y[t][:], banks[t][:])
+        lists = (p1_t, p2_t)
 
+        def k_col(i, l, b):
+            n = (2 * i + l) * BLOCKS + b
+            return k_cols[:, n : n + 1]
 
-        nc.tensor.transpose(banks[2][:, :P], k_rows[:], ident[:])
-        nc.scalar.copy(k_cols[:], banks[2][:, : 4 * BLOCKS])
-        w_grouped = [placed("w_grouped%d" % i, [P, N * PACK], BF16, AT_W2 + 4096 * i) for i in range(2)]
+        def look_up(engine, l, b, t, bank, at=None):
+            piece = sb("g%d_%d_%d" % (b, l, t), [P, P], F32, at)
+            window = y[t][:].indirect(lists[l][:, 8 * b : 8 * (b + 1)])
+            if engine is nc.vector:
+                nc.vector.tensor_copy(piece[:], window)
+            else:
+                nc.scalar.activation(piece[:], window, COPY)
+            place = t // 2 + 2 * (t % 2)
+            nc.tensor.transpose(bank[:, place * P : (place + 1) * P], piece[:], ident[:])
+
+        def pairs(ap, order):
+            return ap.rearrange("q (%s) -> q x e" % order, e=2)
+
+        terms = {}
+
+        def term(b, i, bank, at=None):
+            terms[b, i] = sb("term%d_%d" % (b, i), [P, H], F32, at)
+            nc.scalar.activation(pairs(terms[b, i][:], "x e"), pairs(bank[:], "e x"), COPY, scale=k_col(i, 0, b))
+
+        def plain(b, bank, at=None):
+            terms[b] = sb("plain%d" % b, [P, H], F32, at)
+            nc.scalar.copy(pairs(terms[b][:], "x e"), pairs(bank[:], "e x"))
+
+        def term_on_gpsimd(b, i, at=None):
+            terms[b, i] = sb("term%d_%d" % (b, i), [P, H], F32, at)
+            nc.gpsimd.tensor_scalar(terms[b, i][:], terms[b][:], k_col(i, 0, b), 0.0, MULT, ADD)
+
+        def combine(b, i, bank, target, at=None):
+            words = sb("zt%d_%d" % (b, i), [P, HALF], F32, at)
+            nc.vector.scalar_tensor_tensor(
+                out=pairs(words[:].bitcast(BF16), "x e"),
+                in0=pairs(bank[:], "e x"),
+                scalar=k_col(i, 1, b),
+                in1=pairs(terms[b, i][:], "x e"),
+                op0=MULT,
+                op1=ADD,
+            )
+            for u in range(2):
+                nc.tensor.transpose(target[:, u * P : (u + 1) * P], words[:, u * P : (u + 1) * P], ident[:])
+
+        def weave(z, source, copy=nc.scalar.copy):
+            copy(z, source.rearrange("p (i u j) -> p i j u", u=2, j=P))
+
+        def quantise(name, values, width, at=None):
+            codes = sb(name + "_codes", [P, width], U32)
+            scales = sb(name + "_scales", [P, width], U8, at)
+            nc.vector.quantize_mx(out=codes[:].bitcast(FP8X4), scales=scales[:], in_=values)
+            return codes, scales
+
+        w_grouped = [sb("w_grouped%d" % i, [P, N * PACK], BF16, AT_WG + 4096 * i) for i in range(2)]
 
         def round_on_gpsimd(i, first, raw):
             nc.gpsimd.tensor_scalar(
@@ -127,80 +172,7 @@ def tile_picked_kpconv2_none_p_kernel(
                 ADD,
             )
 
-        lists = (p1_t, p2_t)
-        by_pair = [[banks[0], banks[3]], [banks[1], banks[2]]]
-        by_list = {2: [banks[3], banks[1]], 3: [banks[2], banks[4]]}
-
-        def k_col(i, l, b):
-            n = (2 * i + l) * BLOCKS + b
-            return k_cols[:, n : n + 1]
-
-        def look_up(l, b, t, piece):
-            nc.vector.tensor_copy(piece, y[t][:].indirect(lists[l][:, 8 * b : 8 * (b + 1)]))
-            if b < 2:
-                bank, place = by_pair[b][t // 2], 2 * l + t % 2
-            else:
-                bank, place = by_list[b][l], t // 2 + 2 * (t % 2)
-            nc.tensor.transpose(bank[:, place * P : (place + 1) * P], piece, ident[:])
-
-        def pairs(ap, order):
-            return ap.rearrange("q (%s) -> q x e" % order, e=2)
-
-        terms = {}
-
-        def scale_half(l, b, i, u):
-            source = by_pair[b][u][:, l * HALF : (l + 1) * HALF]
-            target = terms[l, b, i][:, u * HALF : (u + 1) * HALF]
-            if (b, i) != (0, 0):
-                source, target = pairs(source, "e x"), pairs(target, "x e")
-            nc.scalar.activation(target, source, COPY, scale=k_col(i, l, b))
-
-        def scale(l, b, i, target):
-            terms[l, b, i] = target
-            nc.scalar.activation(pairs(target, "x e"), pairs(by_list[b][l][:], "e x"), COPY, scale=k_col(i, l, b))
-
-        def turn_back(words, target):
-            for u in range(2):
-                nc.tensor.transpose(target[:, u * P : (u + 1) * P], words[:, u * P : (u + 1) * P], ident[:])
-
-        def add_terms(b, i, room, target):
-            nc.gpsimd.tensor_tensor(room.bitcast(BF16), terms[0, b, i], terms[1, b, i], ADD)
-            turn_back(room, target)
-
-        def add_by_turning(b, i, bank):
-            for n in range(2 * PACK):
-                u, l, e = n // 4, n // 2 % 2, n % 2
-                cols = slice((2 * u + e) * P, (2 * u + e + 1) * P)
-                nc.tensor.matmul(
-                    bank[:, cols], terms[l, b, i][:, cols], ident[:], start=n == 0, stop=n == 2 * PACK - 1, is_transpose=True
-                )
-
-        def combine(b, i, room, target):
-            nc.vector.scalar_tensor_tensor(
-                out=pairs(room.bitcast(BF16), "x e"),
-                in0=pairs(by_list[b][1][:], "e x"),
-                scalar=k_col(i, 1, b),
-                in1=pairs(terms[0, b, i], "x e"),
-                op0=MULT,
-                op1=ADD,
-            )
-            turn_back(room, target)
-
-        def weave(z, bank, sums, copy=nc.scalar.copy):
-            copy(
-                z.rearrange("p (i j u) -> p i j u", i=sums, u=2),
-                bank[:, : sums * 2 * P].rearrange("p (i u j) -> p i j u", i=sums, u=2),
-            )
-            return z.bitcast(BF16)
-
-        def quantise(name, values, width, scales=None):
-            codes = sb(name + "_codes", [P, width], U32)
-            if scales is None:
-                scales = sb(name + "_scales", [P, width], U8)
-            nc.vector.quantize_mx(out=codes[:].bitcast(FP8X4), scales=scales[:], in_=values)
-            return codes, scales
-
-        weights = []
+        weights = {}
 
         def product(i, mt, codes, scales, target, start, stop):
             nc.tensor.matmul_mx(
@@ -213,107 +185,153 @@ def tile_picked_kpconv2_none_p_kernel(
                 stop=stop,
             )
 
-        def multiply(planes, targets):
-            codes, scales = planes
+        def multiply(i, codes, scales, targets):
+            width = codes.shape[1]
             per_bank = 4 // len(targets)
-            for i in range(2):
-                cols = slice(i * P, (i + 1) * P)
-                for mt in range(4):
-                    place = mt % per_bank
-                    target = targets[mt // per_bank][:, place * P : (place + 1) * P]
-                    product(i, mt, codes[:, cols], scales[:, cols], target, i == 0 and place == 0, i == 1 and place == per_bank - 1)
+            for mt in range(4):
+                place = mt % per_bank
+                target = targets[mt // per_bank][:, place * width : (place + 1) * width]
+                product(i, mt, codes, scales, target, i == 0 and place == 0, i == 1 and place == per_bank - 1)
 
         out_rows = out.rearrange("(mt p) j -> p mt j", p=P)
 
-        def store(name, bank, mt0, tiles, col0, copy, queue):
-            result = sb(name, [P, tiles, P], F32)
-            copy(result[:].rearrange("p mt j -> p (mt j)"), bank[:, : tiles * P])
-            queue.dma_start(out_rows[:, mt0 : mt0 + tiles, col0 : col0 + P], result[:])
+        def store(name, bank, mt0, tiles, col0, width, copy, queue, at=None):
+            result = sb(name, [P, tiles, width], F32, at)
+            copy(result[:].rearrange("p mt j -> p (mt j)"), bank[:, : tiles * width])
+            queue.dma_start(out_rows[:, mt0 : mt0 + tiles, col0 : col0 + width], result[:])
 
-        for t in range(PACK):
-            for l in range(2):
-                if (t, l) == (2, 1):
-                    look_up(l, 0, t, placed("g0_anchor", [P, P], F32, AT_GATHER)[:])
-                else:
-                    look_up(l, 0, t, sb("g0_%d_%d" % (t, l), [P, P], F32)[:])
+        V, A = nc.vector, nc.scalar
+        def fetch(engine, l, b, t, target):
+            window = y[t][:].indirect(lists[l][:, 8 * b : 8 * (b + 1)])
+            if engine is nc.vector:
+                nc.vector.tensor_copy(target, window)
+            else:
+                nc.scalar.activation(target, window, COPY)
+
+        def turn(piece, t, bank):
+            place = t // 2 + 2 * (t % 2)
+            nc.tensor.transpose(bank[:, place * P : (place + 1) * P], piece, ident[:])
+
+        def weigh(target, values, row):
+            nc.vector.tensor_tensor(target, values, row.unsqueeze(1).to_broadcast([P, values.shape[1], P]), MULT)
+
+        def add_woven(target, first, second):
+            nc.vector.tensor_tensor(
+                target.rearrange("p (c e t) -> p c t e", e=2, t=PACK),
+                first.rearrange("p t (c e) -> p c t e", e=2),
+                second.rearrange("p t (c e) -> p c t e", e=2),
+                ADD,
+            )
+
+        def planes(name, values):
+            return quantise(name, values, values.shape[1] // PACK)
+
+        def multiply_both(q, targets):
+            for i in range(2):
+                multiply(i, q[0][:, i * P : (i + 1) * P], q[1][:, i * P : (i + 1) * P], targets)
+
+        def weigh_both(l, values, target):
+            count = values.shape[1]
+            nc.vector.tensor_tensor(
+                target,
+                values.unsqueeze(1).to_broadcast([P, 2, count, P]),
+                banks[2][:, l * HALF : (l + 1) * HALF].rearrange("p (i j) -> p i j", i=2).unsqueeze(2).to_broadcast([P, 2, count, P]),
+                MULT,
+            )
+
+        first_product(0, 0, HALF, banks[4][:, :HALF], nc.scalar.copy)
+        first_product(1, 0, HALF, banks[6][:, :HALF], nc.scalar.copy)
+        first_product(0, HALF, P, banks[5][:, :P], nc.vector.tensor_copy)
+        first_product(0, HALF + P, P, banks[7][:, :P], nc.scalar.copy)
+        first_product(1, HALF, HALF, banks[0][:, :HALF], nc.scalar.copy)
+        for t in range(2, PACK):
+            for h in range(2):
+                first_product(t, h * HALF, HALF, banks[t][:, h * HALF : (h + 1) * HALF], None)
+            nc.scalar.copy(y[t][:], banks[t][:])
+        nc.tensor.transpose(banks[2][:, :P], k_rows[:], ident[:])
+        nc.scalar.copy(k_cols[:], banks[2][:, : 4 * BLOCKS])
         round_on_gpsimd(0, 0, w2_raw[:])
         for h in range(2):
-            round_on_gpsimd(1, h * N // 2, w3_raw[h][:])
-        gathered = placed("gathered", [P, 3, PACK, 2, P], F32, AT_GATHER)
-        z0 = sb("z0", [P, H], F32)
-        for b in range(2):
-            if b == 1:
-                for t in range(PACK):
-                    for l in range(2):
-                        look_up(l, b, t, gathered[:, 0, t, l, :])
-            for i in range(2):
-                for l in range(2):
-                    name = "term%d_%d_%d" % (l, b, i)
-                    if (b, i) == (1, 1):
-                        terms[l, b, i] = placed(name, [P, H], F32, AT_LAST + 2048 * l)[:]
-                    else:
-                        terms[l, b, i] = sb(name, [P, H], F32)[:]
-            for u in range(2):
-                for i in range(2):
-                    for l in range(2):
-                        scale_half(l, b, i, u)
-            if b == 0:
-                add_by_turning(0, 0, banks[0])
-                add_terms(0, 1, placed("zt0_1", [P, HALF], F32, AT_W3 + 1024)[:], banks[4])
-        for i in range(2):
-            add_terms(1, i, placed("zt1_%d" % i, [P, HALF], F32, AT_W3 + 2048 * (1 - i))[:], banks[5][:, i * HALF : (i + 1) * HALF])
-        nc.scalar.copy(
-            z0[:, :HALF].bitcast(BF16).rearrange("p (j u e) -> p j u e", u=2, e=2),
-            banks[0][:].rearrange("p (u e j) -> p j u e", u=2, e=2),
-        )
-        for t in range(PACK):
+            round_on_gpsimd(1, h * HALF, w3_raw[h][:])
+        for t in range(2):
             for l in range(2):
-                look_up(l, 2, t, gathered[:, 1, t, l, :])
-        for l in range(2):
-            terms[l, 2, 0] = sb("term%d_2_0" % l, [P, H], F32)[:]
-            nc.scalar.activation(terms[l, 2, 0], by_list[2][l][:], COPY, scale=k_col(0, l, 2))
-        add_by_turning(2, 0, banks[0])
-        scale(0, 2, 1, sb("term0_2_1", [P, H], F32)[:])
+                look_up(V, l, 0, t, banks[4 + l])
+        look_up(V, 0, 0, 2, banks[4], AT_PIECE)
+        look_up(V, 1, 0, 2, banks[5], AT_PIECE + 512)
+        look_up(V, 0, 0, 3, banks[4], AT_PIECE + 1024)
+        look_up(A, 0, 1, 0, banks[6])
+        look_up(V, 1, 0, 3, banks[5], AT_PIECE + 1536)
         for t in range(3):
-            first_product(t, 0, S, banks[2][:], None)
-        for t in range(PACK):
-            look_up(0, 3, t, gathered[:, 2, t, 0, :])
-        weave(z0[:, HALF:], banks[4], 1)
-        for t in range(PACK):
-            look_up(1, 3, t, gathered[:, 2, t, 1, :])
-        combine(2, 1, sb("zt2_1", [P, HALF], F32)[:], banks[6][:, :HALF])
-        z1 = weave(placed("z1", [P, H], F32, AT_Z1)[:], banks[5], 2)
-        weights.append(quantise("w2", w_grouped[0][:], N, placed("w2_scales", [P, N], U8, AT_LAST)))
-        z0_planes = quantise("z0", z0[:].bitcast(BF16), 2 * P, placed("z0_scales", [P, 2 * P], U8, AT_LAST + 2048))
-        weights.append(quantise("w3", w_grouped[1][:], N, placed("w3_scales", [P, N], U8, AT_W2)))
-        multiply(z0_planes, banks[3:4])
-        multiply(quantise("z1", z1, 2 * P, placed("z1_scales", [P, 2 * P], U8, AT_W2 + 512)), banks[1:2])
-        scale(0, 3, 0, placed("term0_3_0", [P, H], F32, AT_W3 - 1024)[:])
-        combine(3, 0, placed("zt3_0", [P, HALF], F32, AT_W2 + 4096)[:], banks[7])
-        z2_words = sb("z2", [P, H], F32)
-        z2 = z2_words[:].bitcast(BF16)
-        nc.scalar.copy(
-            z2[:, :H].rearrange("p (j u e) -> p j u e", u=2, e=2),
-            banks[0][:].rearrange("p (e u j) -> p j u e", u=2, e=2),
-        )
-        weave(z2_words[:, HALF:], banks[6], 1)
-        scale(0, 3, 1, placed("term0_3_1", [P, H], F32, AT_W3 + 2048)[:])
-        z2_planes = [quantise("z2_%d" % i, z2[:, i * H : (i + 1) * H], P) for i in range(2)]
-        combine(3, 1, placed("zt3_1", [P, HALF], F32, AT_Z1)[:], banks[0])
-        store("result0", banks[3], 0, 4, 0, nc.scalar.copy, nc.sync)
-        z3 = [weave(sb("z3_%d" % i, [P, HALF], F32)[:], banks[(7, 0)[i]], 1, (nc.scalar.copy, nc.vector.tensor_copy)[i]) for i in range(2)]
-        for i, (codes, scales) in enumerate(z2_planes):
-            for mt in range(4):
-                target = banks[5 + mt // 2][:, mt % 2 * P : (mt % 2 + 1) * P]
-                product(i, mt, codes[:], scales[:], target, i == 0 and mt % 2 == 0, i == 1 and mt % 2 == 1)
-        store("result1", banks[1], 0, 4, P, nc.scalar.copy, nc.sync)
-        for half in range(2):
-            store("result2_%d" % half, banks[5 + half], 2 * half, 2, 2 * P, nc.scalar.copy, nc.sync)
-        last = [banks[n] for n in (2, 7, 4, 3)]
-        last_planes = [quantise("last%d" % i, z3[i], P) for i in range(2)]
+            look_up(A, 0, 1, t + 1, banks[6])
+            look_up(V, 1, 1, t, banks[7], AT_PIECE + 512 * t)
+        look_up(V, 1, 1, 3, banks[7], AT_PIECE + 1536)
+        for n in range(4):
+            nc.tensor.transpose(banks[2][:, n * P : (n + 1) * P], k_col(n % 2, n // 2, 3).to_broadcast([P, P]), ident[:])
+        for b in range(2):
+            for i in range(2):
+                term(b, i, banks[4 + 2 * b], AT_TERM + 2048 * (2 * b + i))
+        combine(0, 0, banks[5], banks[3][:, :HALF])
+        combine(0, 1, banks[5], banks[3][:, HALF:], AT_ZT)
+        look_up(A, 0, 2, 0, banks[0], AT_TERM)
+        look_up(A, 0, 2, 1, banks[0], AT_TERM + 512)
+        z = [sb("z%d" % b, [P, 2, P, 2], F32, AT_Z + 4096 * b) for b in range(3)]
+        def words(b):
+            return z[b][:].rearrange("p i j u -> p (i j u)").bitcast(BF16)
+        weave(z[0][:], banks[3][:])
+        combine(1, 0, banks[7], banks[1][:, :HALF])
+        combine(1, 1, banks[7], banks[1][:, HALF:], AT_ZT + 2048)
+        look_up(A, 0, 2, 2, banks[0], AT_ZT)
+        look_up(A, 0, 2, 3, banks[0], AT_ZT + 512)
+        weights[0] = quantise("w2", w_grouped[0][:], N, AT_W3RAW + 4096)
+        q0 = quantise("z0", words(0), HALF, AT_W3RAW + 4096 + 512)
+        multiply(0, q0[0][:, :P], q0[1][:, :P], banks[4:5])
+        weave(z[1][:], banks[1][:])
+        look_up(V, 1, 2, 0, banks[5], AT_WG)
+        look_up(V, 1, 2, 1, banks[5], AT_WG + 512)
+        weights[1] = quantise("w3", w_grouped[1][:], N)
+        look_up(A, 1, 2, 2, banks[5], AT_ZT + 2048)
+        look_up(A, 1, 2, 3, banks[5], AT_ZT + 2048 + 512)
+        multiply(1, q0[0][:, P:], q0[1][:, P:], banks[4:5])
+        g3 = {
+            (0, 0): sb("g3_00", [P, 2, P], F32, AT_WG + 1024),
+            (0, 1): sb("g3_01", [P, 2, P], F32, AT_ZT + 2048 - 512),
+            (1, 0): sb("g3_10", [P, 2, P], F32, AT_ZT + 2048 + 512),
+            (1, 1): sb("g3_11", [P, 2, P], F32, AT_ZT + 6144 - 512),
+        }
+        m3 = sb("m3", [P, 2, 2, PACK, P], F32, AT_TERM2 + 2048)
+        for t in range(2):
+            fetch(V, 0, 3, t, g3[0, 0][:, t])
+        q1 = [quantise("z1_0", words(1)[:, :H], P, AT_WG + 2048)]
+        term(2, 0, banks[0], AT_TERM2)
+        term(2, 1, banks[0], AT_TERM2 + 2048)
+        multiply(0, q1[0][0][:], q1[0][1][:], banks[6:7])
+        combine(2, 0, banks[5], banks[3][:, :HALF])
+        combine(2, 1, banks[5], banks[3][:, HALF:], AT_ZT + 6144)
+        for t in range(2):
+            fetch(A, 0, 3, 2 + t, g3[0, 1][:, t])
+        q1.append(quantise("z1_1", words(1)[:, H:], P, AT_TERM2))
+        multiply(1, q1[1][0][:], q1[1][1][:], banks[6:7])
+        for h in range(2):
+            weigh_both(0, g3[0, h][:], m3[:, 0, :, 2 * h : 2 * h + 2])
+        for t in range(2):
+            fetch(A, 1, 3, t, g3[1, 0][:, t])
+        weave(z[2][:], banks[3][:])
+        for t in range(2):
+            fetch(A, 1, 3, 2 + t, g3[1, 1][:, t])
+        weigh_both(1, g3[1, 0][:], m3[:, 1, :, :2])
+        multiply_both(planes("z2", words(2)), banks[5:6])
         for i in range(2):
-            for mt in range(4):
-                product(i, mt, last_planes[i][0][:], last_planes[i][1][:], last[mt][:, :P], i == 0, i == 1)
+            weigh(m3[:, 1, i, 2:], g3[1, 1][:], banks[2][:, HALF + i * P : HALF + (i + 1) * P])
+        store("r0", banks[4], 0, 4, 0, P, nc.scalar.copy, nc.sync, AT_ZT + 6144 + 512)
+        store("r1", banks[6], 0, 4, P, P, nc.scalar.copy, nc.sync, AT_Z + 8192)
+        store("r2", banks[5], 0, 4, HALF, P, nc.scalar.copy, nc.sync)
+        z3 = [sb("z3_%d" % i, [P, H], BF16) for i in range(2)]
+        for i in range(2):
+            add_woven(z3[i][:], m3[:, 0, i], m3[:, 1, i])
+        last = [banks[n] for n in (7, 3, 0, 1)]
+        for i in range(2):
+            q = planes("z3_%d" % i, z3[i][:])
+            multiply(i, q[0][:], q[1][:], last)
         for mt in range(4):
             copy, queue = ((nc.vector.tensor_copy, nc.sync), (nc.scalar.copy, nc.scalar))[mt % 2]
-            store("result_last%d" % mt, last[mt], mt, 1, 3 * P, copy, queue)
+            store("r3_%d" % mt, last[mt], mt, 1, 3 * P, P, copy, queue)

@@ -1,3 +1,4 @@
+import math
 from contextlib import ExitStack
 
 import concourse.mybir as mybir
@@ -23,12 +24,9 @@ MULT = mybir.AluOpType.mult
 ADD = mybir.AluOpType.add
 
 M_VECTOR = 48
-AT_W2RAW, AT_W3RAW, AT_WG = 0, 8192, 16384
-AT_PIECE = 24576
-AT_TERM = 32768
-AT_ZT = 40960
-AT_Z = 57344
-AT_TERM2 = 69632
+SIZE = {F32: 4, BF16: 2, U32: 4, U16: 2, U8: 1}
+ROOM, FRONT, BACK = "room", -1, -2
+MARGIN, TOUCH = 2048, 64
 
 
 def tile_picked_kpconv2_none_p_kernel(
@@ -41,10 +39,19 @@ def tile_picked_kpconv2_none_p_kernel(
         psum = ctx.enter_context(tc.psum_pool(name="psum", bufs=1))
         banks = [psum.tile([P, 512], F32, name="bank%d" % n) for n in range(8)]
 
-        def sb(name, shape, dtype, at=None):
-            if at is None:
+        rooms = {}
+
+        def sb(name, shape, dtype, behind=None):
+            size = SIZE[dtype] * math.prod(shape[1:])
+            if behind is None:
                 return keep.tile(shape, dtype, name=name, align_bytes=64)
-            return shared.tile(shape, dtype, name=name, offset=at, align_bytes=64)
+            if behind == ROOM:
+                start = MARGIN + max([0] + [end for first, end in rooms.values()]) + MARGIN
+            else:
+                first, end = rooms[behind[0]]
+                start = {FRONT: first + TOUCH - size, BACK: end - TOUCH}.get(behind[1], first + 512 * behind[1])
+            rooms[name] = (start, start + size)
+            return shared.tile(shape, dtype, name=name, offset=start, align_bytes=64)
 
         offs_t = sb("offs_t", [P, S // 16], U16)
         p1_t = sb("p1_t", [P, S // 16], U16)
@@ -52,8 +59,8 @@ def tile_picked_kpconv2_none_p_kernel(
         xw = sb("xw", [P, T], U32)
         xs = sb("xs", [P, T], U8)
         w1_raw = sb("w1_raw", [P, PACK, H], F32)
-        w2_raw = sb("w2_raw", [P, PACK, N], F32, AT_W2RAW)
-        w3_raw = [sb("w3_raw%d" % h, [P, PACK, N // 2], F32, AT_W3RAW + 4096 * h) for h in range(2)]
+        w2_raw = sb("w2_raw", [P, PACK, N], F32)
+        w3_raw = [sb("w3_raw%d" % h, [P, PACK, N // 2], F32, ROOM if h else None) for h in range(2)]
         ident = sb("ident", [P, P], F32)
         k_rows = sb("k_rows", [P, P], F32)
         k_cols = sb("k_cols", [P, 4 * BLOCKS], F32)
@@ -160,7 +167,7 @@ def tile_picked_kpconv2_none_p_kernel(
             nc.vector.quantize_mx(out=codes[:].bitcast(FP8X4), scales=scales[:], in_=values)
             return codes, scales
 
-        w_grouped = [sb("w_grouped%d" % i, [P, N * PACK], BF16, AT_WG + 4096 * i) for i in range(2)]
+        w_grouped = [sb("w_grouped%d" % i, [P, N * PACK], BF16, ROOM) for i in range(2)]
 
         def round_on_gpsimd(i, first, raw):
             nc.gpsimd.tensor_scalar(
@@ -201,44 +208,6 @@ def tile_picked_kpconv2_none_p_kernel(
             queue.dma_start(out_rows[:, mt0 : mt0 + tiles, col0 : col0 + width], result[:])
 
         V, A = nc.vector, nc.scalar
-        def fetch(engine, l, b, t, target):
-            window = y[t][:].indirect(lists[l][:, 8 * b : 8 * (b + 1)])
-            if engine is nc.vector:
-                nc.vector.tensor_copy(target, window)
-            else:
-                nc.scalar.activation(target, window, COPY)
-
-        def turn(piece, t, bank):
-            place = t // 2 + 2 * (t % 2)
-            nc.tensor.transpose(bank[:, place * P : (place + 1) * P], piece, ident[:])
-
-        def weigh(target, values, row):
-            nc.vector.tensor_tensor(target, values, row.unsqueeze(1).to_broadcast([P, values.shape[1], P]), MULT)
-
-        def add_woven(target, first, second):
-            nc.vector.tensor_tensor(
-                target.rearrange("p (c e t) -> p c t e", e=2, t=PACK),
-                first.rearrange("p t (c e) -> p c t e", e=2),
-                second.rearrange("p t (c e) -> p c t e", e=2),
-                ADD,
-            )
-
-        def planes(name, values):
-            return quantise(name, values, values.shape[1] // PACK)
-
-        def multiply_both(q, targets):
-            for i in range(2):
-                multiply(i, q[0][:, i * P : (i + 1) * P], q[1][:, i * P : (i + 1) * P], targets)
-
-        def weigh_both(l, values, target):
-            count = values.shape[1]
-            nc.vector.tensor_tensor(
-                target,
-                values.unsqueeze(1).to_broadcast([P, 2, count, P]),
-                banks[2][:, l * HALF : (l + 1) * HALF].rearrange("p (i j) -> p i j", i=2).unsqueeze(2).to_broadcast([P, 2, count, P]),
-                MULT,
-            )
-
         first_product(0, 0, HALF, banks[4][:, :HALF], nc.scalar.copy)
         first_product(1, 0, HALF, banks[6][:, :HALF], nc.scalar.copy)
         first_product(0, HALF, P, banks[5][:, :P], nc.vector.tensor_copy)
@@ -253,85 +222,80 @@ def tile_picked_kpconv2_none_p_kernel(
         round_on_gpsimd(0, 0, w2_raw[:])
         for h in range(2):
             round_on_gpsimd(1, h * HALF, w3_raw[h][:])
+        first = {0: banks[4], 1: banks[6], 2: banks[0], 3: banks[4]}
+        second = {0: banks[5], 1: banks[7], 2: banks[1], 3: banks[6]}
+        back = {(b, i): banks[(2, 3, 2, 3, 0, 2, 3, 0)[2 * b + i]] for b in range(4) for i in range(2)}
+        result = {0: banks[5:6], 1: banks[7:8], 2: banks[1:2], 3: [banks[n] for n in (4, 5, 6, 2)]}
+        z = {}
+        def fetch_turn(engine, b, l, t, at=None):
+            look_up(engine, l, b, t, (first, second)[l][b], at)
+        def sum_up(b, i, at=None):
+            combine(b, i, second[b], back[b, i], at)
+        def weave_one(b, i, at=None, copy=nc.scalar.copy):
+            z[b, i] = sb("z%d_%d" % (b, i), [P, 1, P, 2], F32, at)
+            weave(z[b, i][:], back[b, i][:, :HALF], copy)
+        def finish(b, i, at=None):
+            q = quantise("z%d_%d" % (b, i), z[b, i][:].rearrange("p i j u -> p (i j u)").bitcast(BF16), P, at)
+            multiply(i, q[0][:], q[1][:], result[b])
         for t in range(2):
             for l in range(2):
-                look_up(V, l, 0, t, banks[4 + l])
-        look_up(V, 0, 0, 2, banks[4], AT_PIECE)
-        look_up(V, 1, 0, 2, banks[5], AT_PIECE + 512)
-        look_up(V, 0, 0, 3, banks[4], AT_PIECE + 1024)
-        look_up(A, 0, 1, 0, banks[6])
-        look_up(V, 1, 0, 3, banks[5], AT_PIECE + 1536)
+                fetch_turn(V, 0, l, t)
+        fetch_turn(V, 0, 0, 2, ROOM)
+        fetch_turn(V, 0, 1, 2, ROOM)
+        fetch_turn(V, 0, 0, 3, ROOM)
+        fetch_turn(A, 1, 0, 0)
+        fetch_turn(V, 0, 1, 3, ROOM)
+        ring = ["g0_0_2", "g0_1_2", "g0_0_3", "g0_1_3"]
         for t in range(3):
-            look_up(A, 0, 1, t + 1, banks[6])
-            look_up(V, 1, 1, t, banks[7], AT_PIECE + 512 * t)
-        look_up(V, 1, 1, 3, banks[7], AT_PIECE + 1536)
-        for n in range(4):
-            nc.tensor.transpose(banks[2][:, n * P : (n + 1) * P], k_col(n % 2, n // 2, 3).to_broadcast([P, P]), ident[:])
-        for b in range(2):
-            for i in range(2):
-                term(b, i, banks[4 + 2 * b], AT_TERM + 2048 * (2 * b + i))
-        combine(0, 0, banks[5], banks[3][:, :HALF])
-        combine(0, 1, banks[5], banks[3][:, HALF:], AT_ZT)
-        look_up(A, 0, 2, 0, banks[0], AT_TERM)
-        look_up(A, 0, 2, 1, banks[0], AT_TERM + 512)
-        z = [sb("z%d" % b, [P, 2, P, 2], F32, AT_Z + 4096 * b) for b in range(3)]
-        def words(b):
-            return z[b][:].rearrange("p i j u -> p (i j u)").bitcast(BF16)
-        weave(z[0][:], banks[3][:])
-        combine(1, 0, banks[7], banks[1][:, :HALF])
-        combine(1, 1, banks[7], banks[1][:, HALF:], AT_ZT + 2048)
-        look_up(A, 0, 2, 2, banks[0], AT_ZT)
-        look_up(A, 0, 2, 3, banks[0], AT_ZT + 512)
-        weights[0] = quantise("w2", w_grouped[0][:], N, AT_W3RAW + 4096)
-        q0 = quantise("z0", words(0), HALF, AT_W3RAW + 4096 + 512)
-        multiply(0, q0[0][:, :P], q0[1][:, :P], banks[4:5])
-        weave(z[1][:], banks[1][:])
-        look_up(V, 1, 2, 0, banks[5], AT_WG)
-        look_up(V, 1, 2, 1, banks[5], AT_WG + 512)
+            fetch_turn(A, 1, 0, t + 1, ROOM if t else None)
+            fetch_turn(V, 1, 1, t, (ring[t], 0))
+        fetch_turn(V, 1, 1, 3, (ring[3], 0))
+        for i in range(2):
+            term(0, i, first[0])
+        for t in range(4):
+            fetch_turn(V, 2, 0, t, (ring[t], 0))
+        for i in range(2):
+            term(1, i, first[1])
+        for t in range(4):
+            fetch_turn(V, 2, 1, t, (ring[t], 0))
+            fetch_turn(A, 3, 0, t, (("g1_0_3", FRONT), ("g1_0_3", BACK), ("g1_0_2", FRONT), ("g1_0_2", BACK))[t])
+        sum_up(0, 0, (ring[1], FRONT))
+        fetch_turn(A, 3, 1, 0, (ring[0], FRONT))
+        fetch_turn(A, 3, 1, 1, (ring[0], BACK))
+        sum_up(0, 1, (ring[2], FRONT))
+        fetch_turn(A, 3, 1, 2, (ring[3], BACK))
+        weights[0] = quantise("w2", w_grouped[0][:], N, ("w3_raw1", 0))
+        weave_one(0, 0, ROOM)
+        fetch_turn(A, 3, 1, 3, ("zt0_0", 0))
+        finish(0, 0, ("w3_raw1", 1))
         weights[1] = quantise("w3", w_grouped[1][:], N)
-        look_up(A, 1, 2, 2, banks[5], AT_ZT + 2048)
-        look_up(A, 1, 2, 3, banks[5], AT_ZT + 2048 + 512)
-        multiply(1, q0[0][:, P:], q0[1][:, P:], banks[4:5])
-        g3 = {
-            (0, 0): sb("g3_00", [P, 2, P], F32, AT_WG + 1024),
-            (0, 1): sb("g3_01", [P, 2, P], F32, AT_ZT + 2048 - 512),
-            (1, 0): sb("g3_10", [P, 2, P], F32, AT_ZT + 2048 + 512),
-            (1, 1): sb("g3_11", [P, 2, P], F32, AT_ZT + 6144 - 512),
-        }
-        m3 = sb("m3", [P, 2, 2, PACK, P], F32, AT_TERM2 + 2048)
-        for t in range(2):
-            fetch(V, 0, 3, t, g3[0, 0][:, t])
-        q1 = [quantise("z1_0", words(1)[:, :H], P, AT_WG + 2048)]
-        term(2, 0, banks[0], AT_TERM2)
-        term(2, 1, banks[0], AT_TERM2 + 2048)
-        multiply(0, q1[0][0][:], q1[0][1][:], banks[6:7])
-        combine(2, 0, banks[5], banks[3][:, :HALF])
-        combine(2, 1, banks[5], banks[3][:, HALF:], AT_ZT + 6144)
-        for t in range(2):
-            fetch(A, 0, 3, 2 + t, g3[0, 1][:, t])
-        q1.append(quantise("z1_1", words(1)[:, H:], P, AT_TERM2))
-        multiply(1, q1[1][0][:], q1[1][1][:], banks[6:7])
-        for h in range(2):
-            weigh_both(0, g3[0, h][:], m3[:, 0, :, 2 * h : 2 * h + 2])
-        for t in range(2):
-            fetch(A, 1, 3, t, g3[1, 0][:, t])
-        weave(z[2][:], banks[3][:])
-        for t in range(2):
-            fetch(A, 1, 3, 2 + t, g3[1, 1][:, t])
-        weigh_both(1, g3[1, 0][:], m3[:, 1, :, :2])
-        multiply_both(planes("z2", words(2)), banks[5:6])
-        for i in range(2):
-            weigh(m3[:, 1, i, 2:], g3[1, 1][:], banks[2][:, HALF + i * P : HALF + (i + 1) * P])
-        store("r0", banks[4], 0, 4, 0, P, nc.scalar.copy, nc.sync, AT_ZT + 6144 + 512)
-        store("r1", banks[6], 0, 4, P, P, nc.scalar.copy, nc.sync, AT_Z + 8192)
-        store("r2", banks[5], 0, 4, HALF, P, nc.scalar.copy, nc.sync)
-        z3 = [sb("z3_%d" % i, [P, H], BF16) for i in range(2)]
-        for i in range(2):
-            add_woven(z3[i][:], m3[:, 0, i], m3[:, 1, i])
-        last = [banks[n] for n in (7, 3, 0, 1)]
-        for i in range(2):
-            q = planes("z3_%d" % i, z3[i][:])
-            multiply(i, q[0][:], q[1][:], last)
+        weave_one(0, 1)
+        finish(0, 1, ("w3_raw1", 2))
+        term(2, 0, first[2], ("zt0_1", FRONT))
+        sum_up(1, 0, ("w_grouped0", 1))
+        term(2, 1, first[2], ("w_grouped0", FRONT))
+        sum_up(1, 1, ("w_grouped0", 6))
+        term(3, 0, first[3], ("z0_0", 0))
+        sum_up(2, 0, ("w_grouped1", 1))
+        weave_one(1, 0)
+        sum_up(2, 1, ("w_grouped1", 6))
+        weave_one(1, 1)
+        term(3, 1, first[3], ("zt1_1", BACK))
+        finish(1, 0)
+        finish(1, 1)
+        sum_up(3, 0, ("zt1_1", FRONT))
+        weave_one(2, 0, ROOM)
+        sum_up(3, 1, ("zt2_0", 0))
+        weave_one(2, 1)
+        finish(2, 0)
+        finish(2, 1)
+        store("r0", result[0][0], 0, 4, 0, P, nc.scalar.copy, nc.sync, ("zt2_1", 0))
+        store("r1", result[1][0], 0, 4, P, P, nc.vector.tensor_copy, nc.sync, ("z2_0", 0))
+        weave_one(3, 0)
+        finish(3, 0)
+        weave_one(3, 1)
+        finish(3, 1)
+        store("r2", result[2][0], 0, 4, HALF, P, nc.scalar.copy, nc.sync, ("zt3_1", FRONT))
         for mt in range(4):
             copy, queue = ((nc.vector.tensor_copy, nc.sync), (nc.scalar.copy, nc.scalar))[mt % 2]
-            store("r3_%d" % mt, last[mt], mt, 1, 3 * P, P, copy, queue)
+            store("r3_%d" % mt, result[3][mt], mt, 1, 3 * P, P, copy, queue)

@@ -59,7 +59,7 @@ def tile_picked_kpconv2_none_p_kernel(
         xw = sb("xw", [P, T], U32)
         xs = sb("xs", [P, T], U8)
         w1_raw = sb("w1_raw", [P, PACK, H], F32)
-        w2_raw = sb("w2_raw", [P, PACK, N], F32)
+        w2_raw = sb("w2_raw", [P, PACK, N], F32, ROOM)
         w3_raw = [sb("w3_raw%d" % h, [P, PACK, N // 2], F32, ROOM if h else None) for h in range(2)]
         ident = sb("ident", [P, P], F32)
         k_rows = sb("k_rows", [P, P], F32)
@@ -93,8 +93,8 @@ def tile_picked_kpconv2_none_p_kernel(
         nc.scalar.copy(dst[:, M_VECTOR:], src[:, M_VECTOR:])
         nc.vector.tensor_copy(xs_g[:], xs[:].indirect(offs_t[:]))
         nc.vector.quantize_mx(out=w1_codes[:].bitcast(FP8X4), scales=w1_scales[:], in_=w1_grouped[:])
-        for h in range(2):
-            nc.vector.tensor_copy(xw_g[:, h * HALF : (h + 1) * HALF], xw[:].indirect(offs_t[:, 16 * h : 16 * h + 16]))
+        for col0, width in ((0, HALF), (HALF, P), (HALF + P, P)):
+            nc.vector.tensor_copy(xw_g[:, col0 : col0 + width], xw[:].indirect(offs_t[:, col0 // 16 : (col0 + width) // 16]))
 
         y = [sb("y%d" % t, [P, S], F32) for t in range(PACK)]
 
@@ -118,15 +118,14 @@ def tile_picked_kpconv2_none_p_kernel(
             n = (2 * i + l) * BLOCKS + b
             return k_cols[:, n : n + 1]
 
-        def look_up(engine, l, b, t, bank, at=None):
-            piece = sb("g%d_%d_%d" % (b, l, t), [P, P], F32, at)
+        def look_up(engine, l, b, t, bank, piece):
             window = y[t][:].indirect(lists[l][:, 8 * b : 8 * (b + 1)])
             if engine is nc.vector:
-                nc.vector.tensor_copy(piece[:], window)
+                nc.vector.tensor_copy(piece, window)
             else:
-                nc.scalar.activation(piece[:], window, COPY)
+                nc.scalar.activation(piece, window, COPY)
             place = t // 2 + 2 * (t % 2)
-            nc.tensor.transpose(bank[:, place * P : (place + 1) * P], piece[:], ident[:])
+            nc.tensor.transpose(bank[:, place * P : (place + 1) * P], piece, ident[:])
 
         def pairs(ap, order):
             return ap.rearrange("q (%s) -> q x e" % order, e=2)
@@ -161,8 +160,8 @@ def tile_picked_kpconv2_none_p_kernel(
         def weave(z, source, copy=nc.scalar.copy):
             copy(z, source.rearrange("p (i u j) -> p i j u", u=2, j=P))
 
-        def quantise(name, values, width, at=None):
-            codes = sb(name + "_codes", [P, width], U32)
+        def quantise(name, values, width, at=None, codes_at=None):
+            codes = sb(name + "_codes", [P, width], U32, codes_at)
             scales = sb(name + "_scales", [P, width], U8, at)
             nc.vector.quantize_mx(out=codes[:].bitcast(FP8X4), scales=scales[:], in_=values)
             return codes, scales
@@ -208,27 +207,24 @@ def tile_picked_kpconv2_none_p_kernel(
             queue.dma_start(out_rows[:, mt0 : mt0 + tiles, col0 : col0 + width], result[:])
 
         V, A = nc.vector, nc.scalar
-        first_product(0, 0, HALF, banks[4][:, :HALF], nc.scalar.copy)
-        first_product(1, 0, HALF, banks[6][:, :HALF], nc.scalar.copy)
+        first_product(0, 0, HALF, banks[4][:, :HALF], nc.vector.tensor_copy)
         first_product(0, HALF, P, banks[5][:, :P], nc.vector.tensor_copy)
+        first_product(1, 0, P, banks[6][:, :P], nc.scalar.copy)
         first_product(0, HALF + P, P, banks[7][:, :P], nc.scalar.copy)
-        first_product(1, HALF, HALF, banks[0][:, :HALF], nc.scalar.copy)
+        first_product(1, P, P, banks[0][:, :P], None)
+        first_product(1, HALF, HALF, banks[0][:, P : P + HALF], None)
+        nc.scalar.copy(y[1][:, P:], banks[0][:, : P + HALF])
         for t in range(2, PACK):
-            for h in range(2):
-                first_product(t, h * HALF, HALF, banks[t][:, h * HALF : (h + 1) * HALF], None)
-            nc.scalar.copy(y[t][:], banks[t][:])
-        nc.tensor.transpose(banks[2][:, :P], k_rows[:], ident[:])
-        nc.scalar.copy(k_cols[:], banks[2][:, : 4 * BLOCKS])
-        round_on_gpsimd(0, 0, w2_raw[:])
-        for h in range(2):
-            round_on_gpsimd(1, h * HALF, w3_raw[h][:])
+            first_product(t, 0, S, banks[t][:], nc.scalar.copy)
+        nc.tensor.transpose(banks[6][:, :P], k_rows[:], ident[:])
+        nc.scalar.copy(k_cols[:], banks[6][:, : 4 * BLOCKS])
         first = {0: banks[4], 1: banks[6], 2: banks[0], 3: banks[4]}
         second = {0: banks[5], 1: banks[7], 2: banks[1], 3: banks[6]}
-        back = {(b, i): banks[(2, 3, 2, 3, 0, 2, 3, 0)[2 * b + i]] for b in range(4) for i in range(2)}
-        result = {0: banks[5:6], 1: banks[7:8], 2: banks[1:2], 3: [banks[n] for n in (4, 5, 6, 2)]}
+        back = {(b, i): banks[(2, 3, 5, 7, 2, 3, 0, 1)[2 * b + i]] for b in range(4) for i in range(2)}
+        result = {0: [banks[5], banks[7]], 2: [banks[2], banks[4]], 3: [banks[n] for n in (5, 6, 7, 3)]}
         z = {}
-        def fetch_turn(engine, b, l, t, at=None):
-            look_up(engine, l, b, t, (first, second)[l][b], at)
+        def fetch_turn(engine, b, l, t, piece):
+            look_up(engine, l, b, t, (first, second)[l][b], piece)
         def sum_up(b, i, at=None):
             combine(b, i, second[b], back[b, i], at)
         def weave_one(b, i, at=None, copy=nc.scalar.copy):
@@ -237,65 +233,86 @@ def tile_picked_kpconv2_none_p_kernel(
         def finish(b, i, at=None):
             q = quantise("z%d_%d" % (b, i), z[b, i][:].rearrange("p i j u -> p (i j u)").bitcast(BF16), P, at)
             multiply(i, q[0][:], q[1][:], result[b])
-        for t in range(2):
-            for l in range(2):
-                fetch_turn(V, 0, l, t)
-        fetch_turn(V, 0, 0, 2, ROOM)
-        fetch_turn(V, 0, 1, 2, ROOM)
-        fetch_turn(V, 0, 0, 3, ROOM)
-        fetch_turn(A, 1, 0, 0)
-        fetch_turn(V, 0, 1, 3, ROOM)
-        ring = ["g0_0_2", "g0_1_2", "g0_0_3", "g0_1_3"]
+        def pieces(name, count, at=None):
+            room = sb(name, [P, count * P], F32, at)
+            return [room[:, n * P : (n + 1) * P] for n in range(count)]
+        early = [sb("z01_%d" % i, [P, 2, P, 2], F32, ROOM) for i in range(2)]
+        def weave_early(b, i):
+            weave(early[i][:, b : b + 1], back[b, i][:, :HALF])
+        def finish_early(i, at):
+            q = quantise("z01_%d" % i, early[i][:].rearrange("p b j u -> p (b j u)").bitcast(BF16), HALF, at)
+            multiply(i, q[0][:], q[1][:], result[0])
+        round_on_gpsimd(0, 0, w2_raw[:])
+        round_on_gpsimd(1, 0, w3_raw[0][:])
+        va, vb, sa = pieces("va", 6, ROOM), pieces("vb", 2, ROOM), pieces("sa", 4)
         for t in range(3):
-            fetch_turn(A, 1, 0, t + 1, ROOM if t else None)
-            fetch_turn(V, 1, 1, t, (ring[t], 0))
-        fetch_turn(V, 1, 1, 3, (ring[3], 0))
-        for i in range(2):
-            term(0, i, first[0])
+            for l in range(2):
+                fetch_turn(V, 0, l, t, va[2 * t + l])
+        fetch_turn(A, 1, 1, 0, sa[0])
+        fetch_turn(V, 0, 0, 3, vb[0])
+        fetch_turn(A, 1, 1, 1, sa[1])
+        fetch_turn(V, 0, 1, 3, vb[1])
+        vc = pieces("vc", 4, ("va", 1))
+        for t in range(2):
+            fetch_turn(A, 1, 1, 2 + t, sa[2 + t])
+            fetch_turn(V, 1, 0, t, vc[t])
+        fetch_turn(A, 2, 0, 0, pieces("sx", 1)[0])
+        plain(0, first[0], ROOM)
+        fetch_turn(V, 1, 0, 2, vc[2])
+        fetch_turn(V, 1, 0, 3, vc[3])
+        sb1, vd = pieces("sb1", 3, ("vb", FRONT)), pieces("vd", 4, ("vb", BACK))
+        fetch_turn(A, 2, 0, 1, sb1[0])
+        fetch_turn(V, 2, 1, 0, vd[0])
+        fetch_turn(A, 2, 0, 2, sb1[1])
+        fetch_turn(V, 2, 1, 1, vd[1])
+        fetch_turn(A, 2, 0, 3, sb1[2])
+        fetch_turn(V, 2, 1, 2, vd[2])
+        plain(1, first[1], ROOM)
+        fetch_turn(V, 2, 1, 3, vd[3])
+        term_on_gpsimd(0, 0, ("w2_raw", 0))
+        term_on_gpsimd(0, 1, ("w2_raw", 4))
+        term_on_gpsimd(1, 0, ("w2_raw", 8))
+        term_on_gpsimd(1, 1, ("w2_raw", 12))
+        round_on_gpsimd(1, HALF, w3_raw[1][:])
+        ve, sc = pieces("ve", 2, ("vc", FRONT)), pieces("sc", 6, ("vc", BACK))
+        for t in range(2):
+            fetch_turn(V, 3, 1, t, ve[t])
         for t in range(4):
-            fetch_turn(V, 2, 0, t, (ring[t], 0))
-        for i in range(2):
-            term(1, i, first[1])
-        for t in range(4):
-            fetch_turn(V, 2, 1, t, (ring[t], 0))
-            fetch_turn(A, 3, 0, t, (("g1_0_3", FRONT), ("g1_0_3", BACK), ("g1_0_2", FRONT), ("g1_0_2", BACK))[t])
-        sum_up(0, 0, (ring[1], FRONT))
-        fetch_turn(A, 3, 1, 0, (ring[0], FRONT))
-        fetch_turn(A, 3, 1, 1, (ring[0], BACK))
-        sum_up(0, 1, (ring[2], FRONT))
-        fetch_turn(A, 3, 1, 2, (ring[3], BACK))
-        weights[0] = quantise("w2", w_grouped[0][:], N, ("w3_raw1", 0))
-        weave_one(0, 0, ROOM)
-        fetch_turn(A, 3, 1, 3, ("zt0_0", 0))
-        finish(0, 0, ("w3_raw1", 1))
+            fetch_turn(A, 3, 0, t, sc[t])
+        for t in range(2, 4):
+            fetch_turn(A, 3, 1, t, sc[2 + t])
+        sum_up(0, 0)
+        sum_up(0, 1)
+        term(2, 0, first[2])
+        sum_up(1, 0, ROOM)
+        term(2, 1, first[2], ROOM)
+        sum_up(1, 1, ROOM)
+        weave_early(0, 0)
+        weave_early(0, 1)
+        sum_up(2, 0, ("term1_0", 0))
+        weave_early(1, 0)
+        weights[0] = quantise("w2", w_grouped[0][:], N, ("w3_raw1", 0), ("term1_1", 0))
+        weave_early(1, 1)
+        finish_early(0, ("w3_raw1", 1))
+        term(3, 0, first[3], ("zt1_1", 0))
         weights[1] = quantise("w3", w_grouped[1][:], N)
-        weave_one(0, 1)
-        finish(0, 1, ("w3_raw1", 2))
-        term(2, 0, first[2], ("zt0_1", FRONT))
-        sum_up(1, 0, ("w_grouped0", 1))
-        term(2, 1, first[2], ("w_grouped0", FRONT))
-        sum_up(1, 1, ("w_grouped0", 6))
-        term(3, 0, first[3], ("z0_0", 0))
-        sum_up(2, 0, ("w_grouped1", 1))
-        weave_one(1, 0)
-        sum_up(2, 1, ("w_grouped1", 6))
-        weave_one(1, 1)
-        term(3, 1, first[3], ("zt1_1", BACK))
-        finish(1, 0)
-        finish(1, 1)
-        sum_up(3, 0, ("zt1_1", FRONT))
-        weave_one(2, 0, ROOM)
-        sum_up(3, 1, ("zt2_0", 0))
+        weave_one(2, 0)
+        finish_early(1, ("w3_raw1", 2))
+        term(3, 1, first[3], ("zt2_0", FRONT))
+        sum_up(2, 1, ("w_grouped1", 0))
+        sum_up(3, 0, ("z01_1", 0))
+        store("r01a", result[0][0], 0, 2, 0, HALF, nc.scalar.copy, nc.sync)
+        sum_up(3, 1, ("term2_1", 0))
         weave_one(2, 1)
-        finish(2, 0)
-        finish(2, 1)
-        store("r0", result[0][0], 0, 4, 0, P, nc.scalar.copy, nc.sync, ("zt2_1", 0))
-        store("r1", result[1][0], 0, 4, P, P, nc.vector.tensor_copy, nc.sync, ("z2_0", 0))
+        finish(2, 0, ("term3_0", 0))
+        store("r01b", result[0][1], 2, 2, 0, HALF, nc.vector.tensor_copy, nc.sync)
         weave_one(3, 0)
-        finish(3, 0)
+        finish(2, 1)
         weave_one(3, 1)
+        finish(3, 0)
         finish(3, 1)
-        store("r2", result[2][0], 0, 4, HALF, P, nc.scalar.copy, nc.sync, ("zt3_1", FRONT))
+        store("r2a", result[2][0], 0, 2, HALF, P, nc.scalar.copy, nc.sync)
+        store("r2b", result[2][1], 2, 2, HALF, P, nc.vector.tensor_copy, nc.sync)
         for mt in range(4):
             copy, queue = ((nc.vector.tensor_copy, nc.sync), (nc.scalar.copy, nc.scalar))[mt % 2]
             store("r3_%d" % mt, result[3][mt], mt, 1, 3 * P, P, copy, queue)

@@ -183,8 +183,8 @@ def tile_picked_kpconv2_none_p_kernel(
         def product(i, mt, codes, scales, target, start, stop):
             nc.tensor.matmul_mx(
                 out=target,
-                lhsT=weights[i][0][:, mt * P : (mt + 1) * P].bitcast(FP8X4),
-                lhsT_scale=weights[i][1][:, mt * P : (mt + 1) * P],
+                lhsT=weights[i, mt // 2][0][:, mt % 2 * P : (mt % 2 + 1) * P].bitcast(FP8X4),
+                lhsT_scale=weights[i, mt // 2][1][:, mt % 2 * P : (mt % 2 + 1) * P],
                 rhs=codes.bitcast(FP8X4),
                 rhs_scale=scales,
                 start=start,
@@ -220,8 +220,8 @@ def tile_picked_kpconv2_none_p_kernel(
         nc.scalar.copy(k_cols[:], banks[6][:, : 4 * BLOCKS])
         first = {0: banks[4], 1: banks[6], 2: banks[0], 3: banks[4]}
         second = {0: banks[5], 1: banks[7], 2: banks[1], 3: banks[6]}
-        back = {(b, i): banks[(2, 3, 5, 7, 2, 3, 0, 1)[2 * b + i]] for b in range(4) for i in range(2)}
-        result = {0: [banks[5], banks[7]], 2: [banks[2], banks[4]], 3: [banks[n] for n in (5, 6, 7, 3)]}
+        back = {(b, i): banks[(2, 3, 5, 7, 2, 3, 4, 2)[2 * b + i]] for b in range(4) for i in range(2)}
+        result = {0: [banks[n] for n in (5, 0, 7, 1)], 2: [banks[5], banks[0]], 3: [banks[n] for n in (6, 7, 1, 3)]}
         z = {}
         def fetch_turn(engine, b, l, t, piece):
             look_up(engine, l, b, t, (first, second)[l][b], piece)
@@ -240,8 +240,9 @@ def tile_picked_kpconv2_none_p_kernel(
         def weave_early(b, i):
             weave(early[i][:, b : b + 1], back[b, i][:, :HALF])
         def finish_early(i, at):
-            q = quantise("z01_%d" % i, early[i][:].rearrange("p b j u -> p (b j u)").bitcast(BF16), HALF, at)
-            multiply(i, q[0][:], q[1][:], result[0])
+            return quantise("z01_%d" % i, early[i][:].rearrange("p b j u -> p (b j u)").bitcast(BF16), HALF, at)
+        def pass_early(q, i, mt):
+            product(i, mt, q[0][:], q[1][:], result[0][mt][:, :HALF], i == 0, i == 1)
         round_on_gpsimd(0, 0, w2_raw[:])
         round_on_gpsimd(1, 0, w3_raw[0][:])
         va, vb, sa = pieces("va", 6, ROOM), pieces("vb", 2, ROOM), pieces("sa", 4)
@@ -283,7 +284,7 @@ def tile_picked_kpconv2_none_p_kernel(
             fetch_turn(A, 3, 1, t, sc[2 + t])
         sum_up(0, 0)
         sum_up(0, 1)
-        term(2, 0, first[2])
+        term(2, 0, first[2], ROOM)
         sum_up(1, 0, ROOM)
         term(2, 1, first[2], ROOM)
         sum_up(1, 1, ROOM)
@@ -291,23 +292,39 @@ def tile_picked_kpconv2_none_p_kernel(
         weave_early(0, 1)
         sum_up(2, 0, ("term1_0", 0))
         weave_early(1, 0)
-        weights[0] = quantise("w2", w_grouped[0][:], N, ("w3_raw1", 0), ("term1_1", 0))
+        sum_up(2, 1, ("term1_1", FRONT))
+        def quantise_weight(i, h, at=None, codes_at=None):
+            weights[i, h] = quantise("w%d_%d" % (2 + i, h), w_grouped[i][:, h * 2 * N : (h + 1) * 2 * N], HALF, at, codes_at)
+        quantise_weight(0, 0, ("w3_raw1", 0), ("term2_0", 0))
         weave_early(1, 1)
-        finish_early(0, ("w3_raw1", 1))
-        term(3, 0, first[3], ("zt1_1", 0))
-        weights[1] = quantise("w3", w_grouped[1][:], N)
+        q0 = finish_early(0, ("w3_raw1", 1))
+        for mt in range(2):
+            pass_early(q0, 0, mt)
+        term(3, 0, first[3], ("zt1_1", BACK))
+        quantise_weight(1, 0, ("w3_raw1", 3))
+        q1 = finish_early(1, ("w3_raw1", 2))
+        for mt in range(2):
+            pass_early(q1, 1, mt)
+        quantise_weight(0, 1, ("z01_0", 0))
+        quantise_weight(1, 1, ("z01_0", 2))
+        for i, q in enumerate((q0, q1)):
+            for mt in range(2, 4):
+                pass_early(q, i, mt)
+        term(3, 1, first[3], ("zt1_1", FRONT))
         weave_one(2, 0)
-        finish_early(1, ("w3_raw1", 2))
-        term(3, 1, first[3], ("zt2_0", FRONT))
-        sum_up(2, 1, ("w_grouped1", 0))
-        sum_up(3, 0, ("z01_1", 0))
-        store("r01a", result[0][0], 0, 2, 0, HALF, nc.scalar.copy, nc.sync)
-        sum_up(3, 1, ("term2_1", 0))
         weave_one(2, 1)
-        finish(2, 0, ("term3_0", 0))
-        store("r01b", result[0][1], 2, 2, 0, HALF, nc.vector.tensor_copy, nc.sync)
+        sum_up(3, 0, ("w_grouped0", 0))
+        for mt in range(3):
+            store("r01_%d" % mt, result[0][mt], mt, 1, 0, HALF, nc.scalar.copy, nc.sync)
+        sum_up(3, 1, ("w_grouped1", 0))
+        q2 = [quantise("z2_%d" % i, z[2, i][:].rearrange("p i j u -> p (i j u)").bitcast(BF16), P, ("term3_0", 2 * i)) for i in range(2)]
+        for h in range(2):
+            for i in range(2):
+                for place in range(2):
+                    target = result[2][h][:, place * P : (place + 1) * P]
+                    product(i, 2 * h + place, q2[i][0][:], q2[i][1][:], target, i == 0 and place == 0, i == 1 and place == 1)
+        store("r01_3", result[0][3], 3, 1, 0, HALF, nc.vector.tensor_copy, nc.sync)
         weave_one(3, 0)
-        finish(2, 1)
         weave_one(3, 1)
         finish(3, 0)
         finish(3, 1)

@@ -24,6 +24,7 @@ MULT = mybir.AluOpType.mult
 ADD = mybir.AluOpType.add
 
 M_VECTOR = 48
+W3_EARLY = 192
 SIZE = {F32: 4, BF16: 2, U32: 4, U16: 2, U8: 1}
 ROOM, FRONT, BACK = "room", -1, -2
 MARGIN, TOUCH = 2048, 64
@@ -60,7 +61,8 @@ def tile_picked_kpconv2_none_p_kernel(
         xs = sb("xs", [P, T], U8)
         w1_raw = sb("w1_raw", [P, PACK, H], F32)
         w2_raw = sb("w2_raw", [P, PACK, N], F32, ROOM)
-        w3_raw = [sb("w3_raw%d" % h, [P, PACK, N // 2], F32, ROOM if h else None) for h in range(2)]
+        w3_cols = (slice(0, W3_EARLY), slice(W3_EARLY, N))
+        w3_raw = [sb("w3_raw%d" % h, [P, PACK, c.stop - c.start], F32, ROOM if h else None) for h, c in enumerate(w3_cols)]
         ident = sb("ident", [P, P], F32)
         k_rows = sb("k_rows", [P, P], F32)
         k_cols = sb("k_cols", [P, 4 * BLOCKS], F32)
@@ -80,7 +82,7 @@ def tile_picked_kpconv2_none_p_kernel(
         nc.sync.dma_start(p1_t[:], p1)
         nc.sync.dma_start(w2_raw[:], w2.rearrange(by_rows, j=PACK))
         for h in range(2):
-            nc.sync.dma_start(w3_raw[h][:], w3.rearrange(by_rows, j=PACK)[:, :, h * N // 2 : (h + 1) * N // 2])
+            nc.sync.dma_start(w3_raw[h][:], w3.rearrange(by_rows, j=PACK)[:, :, w3_cols[h]])
 
         xs_g = sb("xs_g", [P, S], U8)
         xw_g = sb("xw_g", [P, S], U32)
@@ -211,17 +213,17 @@ def tile_picked_kpconv2_none_p_kernel(
         first_product(0, HALF, P, banks[5][:, :P], nc.vector.tensor_copy)
         first_product(1, 0, P, banks[6][:, :P], nc.scalar.copy)
         first_product(0, HALF + P, P, banks[7][:, :P], nc.scalar.copy)
-        first_product(1, P, P, banks[0][:, :P], None)
-        first_product(1, HALF, HALF, banks[0][:, P : P + HALF], None)
-        nc.scalar.copy(y[1][:, P:], banks[0][:, : P + HALF])
+        first_product(1, P, P, banks[0][:, :P], nc.scalar.copy)
+        first_product(1, HALF, HALF, banks[1][:, :HALF], nc.scalar.copy)
         for t in range(2, PACK):
-            first_product(t, 0, S, banks[t][:], nc.scalar.copy)
-        nc.tensor.transpose(banks[6][:, :P], k_rows[:], ident[:])
-        nc.scalar.copy(k_cols[:], banks[6][:, : 4 * BLOCKS])
-        first = {0: banks[4], 1: banks[6], 2: banks[0], 3: banks[4]}
-        second = {0: banks[5], 1: banks[7], 2: banks[1], 3: banks[6]}
-        back = {(b, i): banks[(2, 3, 5, 7, 2, 3, 4, 2)[2 * b + i]] for b in range(4) for i in range(2)}
-        result = {0: [banks[n] for n in (5, 0, 7, 1)], 2: [banks[5], banks[0]], 3: [banks[n] for n in (6, 7, 1, 3)]}
+            for h in range(2):
+                first_product(t, h * HALF, HALF, banks[2 * t - 2 + h][:, :HALF], nc.scalar.copy)
+        nc.tensor.transpose(banks[0][:, :P], k_rows[:], ident[:])
+        nc.scalar.copy(k_cols[:], banks[0][:, : 4 * BLOCKS])
+        first = {0: banks[6], 1: banks[4], 2: banks[0], 3: banks[6]}
+        second = {0: banks[7], 1: banks[5], 2: banks[1], 3: banks[4]}
+        back = {(b, i): banks[(2, 3, 7, 5, 2, 3, 6, 2)[2 * b + i]] for b in range(4) for i in range(2)}
+        result = {0: [banks[n] for n in (7, 0, 5, 1)], 2: [banks[7], banks[0]], 3: [banks[n] for n in (4, 5, 1, 3)]}
         z = {}
         def fetch_turn(engine, b, l, t, piece):
             look_up(engine, l, b, t, (first, second)[l][b], piece)
@@ -274,7 +276,7 @@ def tile_picked_kpconv2_none_p_kernel(
         term_on_gpsimd(0, 1, ("w2_raw", 4))
         term_on_gpsimd(1, 0, ("w2_raw", 8))
         term_on_gpsimd(1, 1, ("w2_raw", 12))
-        round_on_gpsimd(1, HALF, w3_raw[1][:])
+        round_on_gpsimd(1, W3_EARLY, w3_raw[1][:])
         ve, sc = pieces("ve", 2, ("vc", FRONT)), pieces("sc", 6, ("vc", BACK))
         for t in range(2):
             fetch_turn(V, 3, 1, t, ve[t])

import math
from contextlib import ExitStack

import concourse.mybir as mybir
from concourse.masks import make_identity

K, T, S, N, H = 512, 2048, 512, 512, 512
P = 128
PACK = 4
BLOCKS = S // P
HALF = S // 2
FLOPS = 2 * K * H * S + 2 * 2 * H * N * S
BYTES = K * T + 16 * T + 3 * 4 * K * H + 4 * 4 * S + 3 * 2 * P * (S // 16) + 4 * N * S

F32 = mybir.dt.float32
BF16 = mybir.dt.bfloat16
I32 = mybir.dt.int32
U32 = mybir.dt.uint32
U16 = mybir.dt.uint16
U8 = mybir.dt.uint8
FP8X4 = mybir.dt.float8_e4m3fn_x4
COPY = mybir.ActivationFunctionType.Copy
MULT = mybir.AluOpType.mult
ADD = mybir.AluOpType.add

M_VECTOR = 48
W3_EARLY = 192
SIZE = {F32: 4, BF16: 2, U32: 4, U16: 2, U8: 1}
ROOM, FRONT, BACK = "room", -1, -2
MARGIN, TOUCH = 2048, 64


def tile_picked_kpconv2_none_p_kernel(
    tc, x_words, x_scales, w1, k11, k12, k21, k22, w2, w3, offs, p1, p2, out
):
    nc = tc.nc
    with ExitStack() as ctx:
        keep = ctx.enter_context(tc.tile_pool(name="keep", bufs=1))
        shared = ctx.enter_context(tc.tile_pool(name="shared", bufs=1))
        psum = ctx.enter_context(tc.psum_pool(name="psum", bufs=1))
        banks = [psum.tile([P, 512], F32, name="bank%d" % n) for n in range(8)]

        rooms = {}

        def sb(name, shape, dtype, behind=None):
            size = SIZE[dtype] * math.prod(shape[1:])
            if behind is None:
                return keep.tile(shape, dtype, name=name, align_bytes=64)
            if behind == ROOM:
                start = MARGIN + max([0] + [end for first, end in rooms.values()]) + MARGIN
            else:
                first, end = rooms[behind[0]]
                start = {FRONT: first + TOUCH - size, BACK: end - TOUCH}.get(behind[1], first + 512 * behind[1])
            rooms[name] = (start, start + size)
            return shared.tile(shape, dtype, name=name, offset=start, align_bytes=64)

        offs_t = sb("offs_t", [P, S // 16], U16)
        p1_t = sb("p1_t", [P, S // 16], U16)
        p2_t = sb("p2_t", [P, S // 16], U16)
        xw = sb("xw", [P, T], U32)
        xs = sb("xs", [P, T], U8)
        w1_raw = sb("w1_raw", [P, PACK, H], F32)
        w2_raw = sb("w2_raw", [P, PACK, N], F32, ROOM)
        w3_cols = (slice(0, W3_EARLY), slice(W3_EARLY, N))
        w3_raw = [sb("w3_raw%d" % h, [P, PACK, c.stop - c.start], F32, ROOM if h else None) for h, c in enumerate(w3_cols)]
        ident = sb("ident", [P, P], F32)
        k_rows = sb("k_rows", [P, P], F32)
        k_cols = sb("k_cols", [P, 4 * BLOCKS], F32)

        nc.gpsimd.memset(k_rows[:], 0.0)
        for n, k in enumerate((k11, k12, k21, k22)):
            nc.gpsimd.dma_start(k_rows[BLOCKS * n : BLOCKS * (n + 1), :], k[0:1, :].rearrange("r (b q) -> (r b) q", b=BLOCKS))
        nc.vector.memset(xs[:].bitcast(I32), 0)
        make_identity(nc, ident[:])
        by_rows = "(p j) c -> p j c"
        nc.sync.dma_start(offs_t[:], offs)
        nc.sync.dma_start(w1_raw[:], w1.rearrange(by_rows, j=PACK))
        nc.sync.dma_start(p2_t[:], p2)
        for r in range(4):
            nc.sync.dma_start(xs[r:P:32, :].bitcast(I32), x_scales[0, r:16:4, :].bitcast(I32))
        nc.sync.dma_start(xw[:].bitcast(I32), x_words[0].rearrange("p n t -> p (n t)").bitcast(I32))
        nc.sync.dma_start(p1_t[:], p1)
        nc.sync.dma_start(w2_raw[:], w2.rearrange(by_rows, j=PACK))
        for h in range(2):
            nc.sync.dma_start(w3_raw[h][:], w3.rearrange(by_rows, j=PACK)[:, :, w3_cols[h]])

        xs_g = sb("xs_g", [P, S], U8)
        xw_g = sb("xw_g", [P, S], U32)
        w1_codes = sb("w1_codes", [P, H], U32)
        w1_scales = sb("w1_scales", [P, H], U8)
        w1_grouped = sb("w1_grouped", [P, H * PACK], BF16)
        dst = w1_grouped[:].rearrange("p (t m j) -> p m j t", t=PACK, j=PACK)
        src = w1_raw[:].rearrange("p j (m t) -> p m j t", t=PACK)
        nc.vector.tensor_copy(dst[:, :M_VECTOR], src[:, :M_VECTOR])
        nc.scalar.copy(dst[:, M_VECTOR:], src[:, M_VECTOR:])
        nc.vector.tensor_copy(xs_g[:], xs[:].indirect(offs_t[:]))
        nc.vector.quantize_mx(out=w1_codes[:].bitcast(FP8X4), scales=w1_scales[:], in_=w1_grouped[:])
        for col0, width in ((0, HALF), (HALF, P), (HALF + P, P)):
            nc.vector.tensor_copy(xw_g[:, col0 : col0 + width], xw[:].indirect(offs_t[:, col0 // 16 : (col0 + width) // 16]))

        y = [sb("y%d" % t, [P, S], F32) for t in range(PACK)]

        def first_product(t, col0, width, bank, copy):
            cols = slice(col0, col0 + width)
            nc.tensor.matmul_mx(
                out=bank,
                lhsT=w1_codes[:, t * P : (t + 1) * P].bitcast(FP8X4),
                lhsT_scale=w1_scales[:, t * P : (t + 1) * P],
                rhs=xw_g[:, cols].bitcast(FP8X4),
                rhs_scale=xs_g[:, cols],
                start=True,
                stop=True,
            )
            if copy is not None:
                copy(y[t][:, cols], bank)

        lists = (p1_t, p2_t)

        def k_col(i, l, b):
            n = (2 * i + l) * BLOCKS + b
            return k_cols[:, n : n + 1]

        def look_up(engine, l, b, t, bank, piece):
            window = y[t][:].indirect(lists[l][:, 8 * b : 8 * (b + 1)])
            if engine is nc.vector:
                nc.vector.tensor_copy(piece, window)
            else:
                nc.scalar.activation(piece, window, COPY)
            place = t // 2 + 2 * (t % 2)
            nc.tensor.transpose(bank[:, place * P : (place + 1) * P], piece, ident[:])

        def pairs(ap, order):
            return ap.rearrange("q (%s) -> q x e" % order, e=2)

        terms = {}

        def term(b, i, bank, at=None):
            terms[b, i] = sb("term%d_%d" % (b, i), [P, H], F32, at)
            nc.scalar.activation(pairs(terms[b, i][:], "x e"), pairs(bank[:], "e x"), COPY, scale=k_col(i, 0, b))

        def plain(b, bank, at=None):
            terms[b] = sb("plain%d" % b, [P, H], F32, at)
            nc.scalar.copy(pairs(terms[b][:], "x e"), pairs(bank[:], "e x"))

        def term_on_gpsimd(b, i, at=None):
            terms[b, i] = sb("term%d_%d" % (b, i), [P, H], F32, at)
            nc.gpsimd.tensor_scalar(terms[b, i][:], terms[b][:], k_col(i, 0, b), 0.0, MULT, ADD)

        def combine(b, i, bank, target, at=None):
            words = sb("zt%d_%d" % (b, i), [P, HALF], F32, at)
            nc.vector.scalar_tensor_tensor(
                out=pairs(words[:].bitcast(BF16), "x e"),
                in0=pairs(bank[:], "e x"),
                scalar=k_col(i, 1, b),
                in1=pairs(terms[b, i][:], "x e"),
                op0=MULT,
                op1=ADD,
            )
            for u in range(2):
                nc.tensor.transpose(target[:, u * P : (u + 1) * P], words[:, u * P : (u + 1) * P], ident[:])

        def weave(z, source, copy=nc.scalar.copy):
            copy(z, source.rearrange("p (i u j) -> p i j u", u=2, j=P))

        def quantise(name, values, width, at=None, codes_at=None):
            codes = sb(name + "_codes", [P, width], U32, codes_at)
            scales = sb(name + "_scales", [P, width], U8, at)
            nc.vector.quantize_mx(out=codes[:].bitcast(FP8X4), scales=scales[:], in_=values)
            return codes, scales

        w_grouped = [sb("w_grouped%d" % i, [P, N * PACK], BF16, ROOM) for i in range(2)]

        def round_on_gpsimd(i, first, raw):
            nc.gpsimd.tensor_scalar(
                w_grouped[i][:, first * PACK : (first + raw.shape[2]) * PACK].rearrange("p (c j) -> p c j", j=PACK),
                raw.rearrange("p j c -> p c j"),
                1.0,
                0.0,
                MULT,
                ADD,
            )

        weights = {}

        def product(i, mt, codes, scales, target, start, stop):
            nc.tensor.matmul_mx(
                out=target,
                lhsT=weights[i, mt // 2][0][:, mt % 2 * P : (mt % 2 + 1) * P].bitcast(FP8X4),
                lhsT_scale=weights[i, mt // 2][1][:, mt % 2 * P : (mt % 2 + 1) * P],
                rhs=codes.bitcast(FP8X4),
                rhs_scale=scales,
                start=start,
                stop=stop,
            )

        def multiply(i, codes, scales, targets):
            width = codes.shape[1]
            per_bank = 4 // len(targets)
            for mt in range(4):
                place = mt % per_bank
                target = targets[mt // per_bank][:, place * width : (place + 1) * width]
                product(i, mt, codes, scales, target, i == 0 and place == 0, i == 1 and place == per_bank - 1)

        out_rows = out.rearrange("(mt p) j -> p mt j", p=P)

        def store(name, bank, mt0, tiles, col0, width, copy, queue, at=None):
            result = sb(name, [P, tiles, width], F32, at)
            copy(result[:].rearrange("p mt j -> p (mt j)"), bank[:, : tiles * width])
            queue.dma_start(out_rows[:, mt0 : mt0 + tiles, col0 : col0 + width], result[:])

        V, A = nc.vector, nc.scalar
        first_product(0, 0, HALF, banks[4][:, :HALF], nc.vector.tensor_copy)
        first_product(0, HALF, P, banks[5][:, :P], nc.vector.tensor_copy)
        first_product(1, 0, P, banks[6][:, :P], nc.scalar.copy)
        first_product(0, HALF + P, P, banks[7][:, :P], nc.scalar.copy)
        first_product(1, P, P, banks[0][:, :P], nc.scalar.copy)
        first_product(1, HALF, HALF, banks[1][:, :HALF], nc.scalar.copy)
        for t in range(2, PACK):
            for h in range(2):
                first_product(t, h * HALF, HALF, banks[2 * t - 2 + h][:, :HALF], nc.scalar.copy)
        nc.tensor.transpose(banks[0][:, :P], k_rows[:], ident[:])
        nc.scalar.copy(k_cols[:], banks[0][:, : 4 * BLOCKS])
        first = {0: banks[6], 1: banks[4], 2: banks[0], 3: banks[6]}
        second = {0: banks[7], 1: banks[5], 2: banks[1], 3: banks[4]}
        back = {(b, i): banks[(2, 3, 7, 5, 2, 3, 6, 2)[2 * b + i]] for b in range(4) for i in range(2)}
        result = {0: [banks[n] for n in (7, 0, 5, 1)], 2: [banks[7], banks[0]], 3: [banks[n] for n in (4, 5, 1, 3)]}
        z = {}
        def fetch_turn(engine, b, l, t, piece):
            look_up(engine, l, b, t, (first, second)[l][b], piece)
        def sum_up(b, i, at=None):
            combine(b, i, second[b], back[b, i], at)
        def weave_one(b, i, at=None, copy=nc.scalar.copy):
            z[b, i] = sb("z%d_%d" % (b, i), [P, 1, P, 2], F32, at)
            weave(z[b, i][:], back[b, i][:, :HALF], copy)
        def finish(b, i, at=None):
            q = quantise("z%d_%d" % (b, i), z[b, i][:].rearrange("p i j u -> p (i j u)").bitcast(BF16), P, at)
            multiply(i, q[0][:], q[1][:], result[b])
        def pieces(name, count, at=None):
            room = sb(name, [P, count * P], F32, at)
            return [room[:, n * P : (n + 1) * P] for n in range(count)]
        early = [sb("z01_%d" % i, [P, 2, P, 2], F32, ROOM) for i in range(2)]
        def weave_early(b, i):
            weave(early[i][:, b : b + 1], back[b, i][:, :HALF])
        def finish_early(i, at):
            return quantise("z01_%d" % i, early[i][:].rearrange("p b j u -> p (b j u)").bitcast(BF16), HALF, at)
        def pass_early(q, i, mt):
            product(i, mt, q[0][:], q[1][:], result[0][mt][:, :HALF], i == 0, i == 1)
        round_on_gpsimd(0, 0, w2_raw[:])
        round_on_gpsimd(1, 0, w3_raw[0][:])
        va, vb, sa = pieces("va", 6, ROOM), pieces("vb", 2, ROOM), pieces("sa", 4)
        for t in range(3):
            for l in range(2):
                fetch_turn(V, 0, l, t, va[2 * t + l])
        fetch_turn(A, 1, 1, 0, sa[0])
        fetch_turn(V, 0, 0, 3, vb[0])
        fetch_turn(A, 1, 1, 1, sa[1])
        fetch_turn(V, 0, 1, 3, vb[1])
        vc = pieces("vc", 4, ("va", 1))
        for t in range(2):
            fetch_turn(A, 1, 1, 2 + t, sa[2 + t])
            fetch_turn(V, 1, 0, t, vc[t])
        fetch_turn(A, 2, 0, 0, pieces("sx", 1)[0])
        plain(0, first[0], ROOM)
        fetch_turn(V, 1, 0, 2, vc[2])
        fetch_turn(V, 1, 0, 3, vc[3])
        sb1, vd = pieces("sb1", 3, ("vb", FRONT)), pieces("vd", 4, ("vb", BACK))
        fetch_turn(A, 2, 0, 1, sb1[0])
        fetch_turn(V, 2, 1, 0, vd[0])
        fetch_turn(A, 2, 0, 2, sb1[1])
        fetch_turn(V, 2, 1, 1, vd[1])
        fetch_turn(A, 2, 0, 3, sb1[2])
        fetch_turn(V, 2, 1, 2, vd[2])
        plain(1, first[1], ROOM)
        fetch_turn(V, 2, 1, 3, vd[3])
        term_on_gpsimd(0, 0, ("w2_raw", 0))
        term_on_gpsimd(0, 1, ("w2_raw", 4))
        term_on_gpsimd(1, 0, ("w2_raw", 8))
        term_on_gpsimd(1, 1, ("w2_raw", 12))
        round_on_gpsimd(1, W3_EARLY, w3_raw[1][:])
        ve, sc = pieces("ve", 2, ("vc", FRONT)), pieces("sc", 6, ("vc", BACK))
        for t in range(2):
            fetch_turn(V, 3, 1, t, ve[t])
        for t in range(4):
            fetch_turn(A, 3, 0, t, sc[t])
        for t in range(2, 4):
            fetch_turn(A, 3, 1, t, sc[2 + t])
        sum_up(0, 0)
        sum_up(0, 1)
        term(2, 0, first[2], ROOM)
        sum_up(1, 0, ROOM)
        term(2, 1, first[2], ROOM)
        sum_up(1, 1, ROOM)
        weave_early(0, 0)
        weave_early(0, 1)
        sum_up(2, 0, ("term1_0", 0))
        weave_early(1, 0)
        sum_up(2, 1, ("term1_1", FRONT))
        def quantise_weight(i, h, at=None, codes_at=None):
            weights[i, h] = quantise("w%d_%d" % (2 + i, h), w_grouped[i][:, h * 2 * N : (h + 1) * 2 * N], HALF, at, codes_at)
        quantise_weight(0, 0, ("w3_raw1", 0), ("term2_0", 0))
        weave_early(1, 1)
        q0 = finish_early(0, ("w3_raw1", 1))
        for mt in range(2):
            pass_early(q0, 0, mt)
        term(3, 0, first[3], ("zt1_1", BACK))
        quantise_weight(1, 0, ("w3_raw1", 3))
        q1 = finish_early(1, ("w3_raw1", 2))
        for mt in range(2):
            pass_early(q1, 1, mt)
        quantise_weight(0, 1, ("z01_0", 0))
        quantise_weight(1, 1, ("z01_0", 2))
        for i, q in enumerate((q0, q1)):
            for mt in range(2, 4):
                pass_early(q, i, mt)
        term(3, 1, first[3], ("zt1_1", FRONT))
        weave_one(2, 0)
        weave_one(2, 1)
        sum_up(3, 0, ("w_grouped0", 0))
        for mt in range(3):
            store("r01_%d" % mt, result[0][mt], mt, 1, 0, HALF, nc.scalar.copy, nc.sync)
        sum_up(3, 1, ("w_grouped1", 0))
        q2 = [quantise("z2_%d" % i, z[2, i][:].rearrange("p i j u -> p (i j u)").bitcast(BF16), P, ("term3_0", 2 * i)) for i in range(2)]
        for h in range(2):
            for i in range(2):
                for place in range(2):
                    target = result[2][h][:, place * P : (place + 1) * P]
                    product(i, 2 * h + place, q2[i][0][:], q2[i][1][:], target, i == 0 and place == 0, i == 1 and place == 1)
        store("r01_3", result[0][3], 3, 1, 0, HALF, nc.vector.tensor_copy, nc.sync)
        weave_one(3, 0)
        weave_one(3, 1)
        finish(3, 0)
        finish(3, 1)
        store("r2a", result[2][0], 0, 2, HALF, P, nc.scalar.copy, nc.sync)
        store("r2b", result[2][1], 2, 2, HALF, P, nc.vector.tensor_copy, nc.sync)
        for mt in range(4):
            copy, queue = ((nc.vector.tensor_copy, nc.sync), (nc.scalar.copy, nc.scalar))[mt % 2]
            store("r3_%d" % mt, result[3][mt], mt, 1, 3 * P, P, copy, queue)
